import numpy as np
import ml_dtypes


def mxq(x, axis, fmt="e4m3"):
    dtype, down = {"e4m3": (ml_dtypes.float8_e4m3fn, 7), "e5m2": (ml_dtypes.float8_e5m2, 14)}[fmt]
    v = np.moveaxis(np.asarray(x, np.float32).astype(ml_dtypes.bfloat16).astype(np.float64), axis, -1)
    blocks = v.reshape(v.shape[:-1] + (-1, 32))
    amax = np.abs(blocks).max(-1, keepdims=True)
    byte = np.maximum(np.where(amax > 0, np.frexp(amax)[1] - 1 + 127, 0) - down, 1)
    scale = np.exp2(byte - 127.0)
    codes = (blocks / scale).astype(np.float32).astype(dtype).astype(np.float64)
    return np.moveaxis((codes * scale).reshape(v.shape), -1, axis)


WIDE = False


def mx_kscale(k):
    if not WIDE:
        return np.ones(k)
    levels = np.array([18, -18])
    if k % 512:
        return np.exp2(np.random.permutation(np.resize(levels, k // 32))).repeat(32)
    a = np.empty((k // 512, 16))
    for p in range(k // 512):
        a[p, :8] = np.random.permutation(np.resize(levels, 8))
        for g in range(8):
            far = levels[np.abs(levels - a[p, g]) >= 10]
            a[p, g + 8] = far[np.random.randint(len(far))]
    return np.exp2(a.ravel()).repeat(32)


def f64(x):
    return np.asarray(x).astype(np.float64)


def striped(idx):
    return np.tile(np.asarray(idx).reshape(-1, 16).T, (8, 1)).astype(np.uint16)


def unstriped(offs):
    return offs[:16].T.reshape(-1).astype(np.int64)

def planes(y):
    n, m = y.shape
    v = y.astype(np.float32).astype(ml_dtypes.bfloat16).astype(np.float64).reshape(n // 32, 32, m)
    top = np.abs(v).max(1)
    byte = np.clip(np.where(top > 0, np.frexp(top)[1] - 1 + 127 - 7, 1), 1, 254)
    codes = (v * np.exp2(127.0 - byte)[:, None, :]).reshape(n, m).astype(np.float32).astype(ml_dtypes.float8_e4m3fn).view(np.uint8)
    words = codes.reshape(n // 512, 128, 4, m).transpose(0, 1, 3, 2)
    return np.ascontiguousarray(words), np.ascontiguousarray(byte.astype(np.uint8).reshape(n // 512, 16, m))


def sig(x):
    return 1.0 / (1.0 + np.exp(-x))


def setup_inputs():
    n = np.random.standard_normal
    uni = np.random.uniform
    idx = np.random.permutation(2048)[:512]
    f_d = mx_kscale(512)
    f_f = mx_kscale(512)
    return {
        "eT": (n((512, 2048)) * f_d[:, None]).astype(np.float32),
        "w1": (n((512, 512)) / np.sqrt(512) / f_d[:, None] * f_f[None, :]).astype(np.float32),
        "w2": (n((512, 512)) / np.sqrt(512) / f_d[:, None] * f_f[None, :]).astype(np.float32),
        "dy": (n((512, 512))).astype(np.float32),
        "c1": (uni(0.75, 1.3, (512, 1)) / f_f[:, None]).astype(np.float32),
        "c2": (uni(0.75, 1.3, (512, 1)) / f_f[:, None]).astype(np.float32),
        "ts": np.tile(uni(0.75, 1.3, 2048), (128, 1)).astype(np.float32),
        "offs": striped(idx),
    }


def reference(eT, w1, w2, dy, c1, c2, ts, offs):
    idx = unstriped(offs)
    eT_i = f64(eT)[:, idx]
    ts_i = f64(ts)[:1][:, idx]
    q_eT_i = mxq(eT_i, 0, "e4m3")
    a = mxq(f64(w1), 0, "e4m3").T @ q_eT_i
    b = mxq(f64(w2), 0, "e4m3").T @ q_eT_i
    s = sig(f64(c2) * ts_i * b)
    da = f64(c1) * ts_i * f64(dy) * s
    db = f64(c1) * f64(c2) * np.square(ts_i) * f64(dy) * a * s * (1.0 - s)
    x1 = mxq(f64(w1), 1, "e4m3") @ mxq(da, 0, "e5m2")
    x2 = mxq(f64(w2), 1, "e4m3") @ mxq(db, 0, "e5m2")
    de = x1 + x2
    out_0 = np.zeros((512, 2048))
    out_0[:, idx] = de
    return (out_0,) + planes(out_0)

@@ -1,0 +1,227 @@
+from contextlib import ExitStack
+
+import concourse.mybir as mybir
+from concourse.masks import make_identity
+
+F32 = mybir.dt.float32
+BF16 = mybir.dt.bfloat16
+I32 = mybir.dt.int32
+U32 = mybir.dt.uint32
+U16 = mybir.dt.uint16
+U8 = mybir.dt.uint8
+E4 = mybir.dt.float8_e4m3fn_x4
+E5 = mybir.dt.float8_e5m2_x4
+ALU = mybir.AluOpType
+ACT = mybir.ActivationFunctionType
+
+P = 128
+L = 4
+N = 512
+T = 2048
+K = 512
+CH = 4
+CW = T // CH
+
+FLOPS = 4 * 2 * 512 * 512 * 512
+
+
+def tile_attend_ggate_E_pl_kernel(tc, eT, w1, w2, dy, c1, c2, ts, offs, out_0, out_1, out_2):
+    nc = tc.nc
+    with ExitStack() as ctx:
+        sb = ctx.enter_context(tc.tile_pool(name="sb", bufs=1))
+        ps = ctx.enter_context(tc.psum_pool(name="ps", bufs=1))
+
+        def bank(i, name):
+            return ps.tile([P, 512], F32, name=name, tag="bank%d" % i)
+
+        def quantise(src, fmt, name):
+            codes = sb.tile([P, N], U32, name=name + "_codes", align_bytes=64)
+            scales = sb.tile([P, N], U8, name=name + "_scales", align_bytes=64)
+            nc.vector.quantize_mx(out=codes[:].bitcast(fmt), scales=scales[:], in_=src)
+            return codes, scales
+
+        ts_row = sb.tile([P, T // P], F32, name="ts_row")
+        nc.sync.dma_start(out=ts_row[:], in_=ts[0:1, :].rearrange("o (p m) -> (o p) m", p=P))
+        offsets = sb.tile([P, N // 16], U16, name="offsets")
+        nc.sync.dma_start(offsets[:], offs)
+        w2_raw = sb.tile([P, L, K], F32, name="w2_raw")
+        nc.sync.dma_start(out=w2_raw[:], in_=w2.rearrange("(p j) f -> p j f", j=L))
+        e_rows = eT.rearrange("(p j) c -> p j c", j=L)
+        e_planes = []
+        for j in range(L):
+            plane = sb.tile([P, T], F32, name="e_plane%d" % j)
+            nc.sync.dma_start(out=plane[:], in_=e_rows[:, j, :])
+            e_planes.append(plane)
+        c2_sb = sb.tile([P, L], F32, name="c2_sb")
+        nc.sync.dma_start(out=c2_sb[:], in_=c2.rearrange("(p t) o -> p (t o)", t=L))
+        c1_sb = sb.tile([P, L], F32, name="c1_sb")
+        nc.sync.dma_start(out=c1_sb[:], in_=c1.rearrange("(p t) o -> p (t o)", t=L))
+        w1_raw = sb.tile([P, L, K], F32, name="w1_raw")
+        nc.sync.dma_start(out=w1_raw[:], in_=w1.rearrange("(p j) f -> p j f", j=L))
+        dy_sb = sb.tile([P, L, N], F32, name="dy_sb")
+        nc.sync.dma_start(out=dy_sb[:], in_=dy.rearrange("(p t) n -> p t n", t=L))
+
+        ident = sb.tile([P, P], F32, name="ident")
+        make_identity(nc, ident[:])
+
+        windows = []
+        for j in range(L):
+            win = sb.tile([P, T], F32, name="window%d" % j)
+            nc.vector.memset(win[:].bitcast(I32), 0)
+            windows.append(win)
+
+        ts_all = sb.tile([P, T], F32, name="ts_all")
+        ts_view = ts_all[:].rearrange("q (p m) -> q p m", p=P)
+        for g in range(4):
+            bk = bank(g, "ts_bank%d" % g)
+            for r in range(4):
+                m = 4 * g + r
+                nc.tensor.transpose(bk[:, r * P:(r + 1) * P], ts_row[:, m:m + 1].to_broadcast([P, P]), ident[:])
+            nc.scalar.copy(out=ts_view[:, :, 4 * g:4 * g + 4], in_=bk[:].rearrange("q (r p) -> q p r", r=4))
+
+        def along_d(raw, name):
+            wd = sb.tile([P, L, P, L], BF16, name=name + "_d", align_bytes=64)
+            nc.scalar.copy(out=wd[:].rearrange("p t m j -> p m j t"),
+                           in_=raw[:].rearrange("p j (m t) -> p m j t", t=L))
+            return wd
+
+        def along_f(wd, name, first_bank):
+            words = wd[:].rearrange("p t m j -> p (t m j)").bitcast(F32).rearrange("p (t m v) -> p t m v", t=L, v=2)
+            wf = sb.tile([P, L, P, L], BF16, name=name + "_f", align_bytes=64)
+            for v in range(2):
+                bk = bank(first_bank + v, name + "_turn%d" % v)
+                for t in range(L):
+                    nc.tensor.transpose(bk[:, t * P:(t + 1) * P], words[:, t, :, v], ident[:])
+                nc.scalar.copy(out=wf[:, 2 * v:2 * v + 2, :, :],
+                               in_=bk[:].bitcast(BF16).rearrange("m (t p e) -> m e p t", t=L, e=2))
+            return wf
+
+        def flat(x):
+            return x[:].rearrange("p a b c -> p (a b c)")
+
+        w2_d = along_d(w2_raw, "w2")
+        w2d_q = quantise(flat(w2_d), E4, "w2d")
+        w2_f = along_f(w2_d, "w2", 4)
+
+        ts_slot = sb.tile([P, N], F32, name="ts_slot")
+        nc.vector.tensor_copy(out=ts_slot[:], in_=ts_all[:].indirect(offsets[:]))
+        c2_neg = sb.tile([P, L], F32, name="c2_neg")
+        nc.vector.tensor_scalar(out=c2_neg[:], in0=c2_sb[:], scalar1=-1.0, scalar2=None, op0=ALU.mult)
+        w2f_q = quantise(flat(w2_f), E4, "w2f")
+
+        e_slot = sb.tile([P, N, L], BF16, name="e_slot", align_bytes=64)
+        for j in range(L):
+            nc.vector.tensor_copy(out=e_slot[:, :, j], in_=e_planes[j][:].indirect(offsets[:]))
+        e_q = quantise(e_slot[:].rearrange("p n j -> p (n j)"), E4, "e")
+
+        def product(out, stat, cols, mov, mov_fmt, start, stop):
+            nc.tensor.matmul_mx(out=out, lhsT=stat[0][:, cols].bitcast(E4), lhsT_scale=stat[1][:, cols],
+                                rhs=mov[0][:].bitcast(mov_fmt), rhs_scale=mov[1][:], start=start, stop=stop)
+
+        def block(i):
+            return slice(i * P, (i + 1) * P)
+
+        w1_d = along_d(w1_raw, "w1")
+
+        s = sb.tile([P, L, N], F32, name="s")
+        for t in range(L):
+            b = bank(t, "b%d" % t)
+            product(b[:], w2d_q, block(t), e_q, E4, True, True)
+            nc.vector.scalar_tensor_tensor(out=s[:, t, :], in0=b[:], scalar=c2_sb[:, t:t + 1], in1=ts_slot[:],
+                                           op0=ALU.mult, op1=ALU.mult)
+            nc.scalar.activation(out=s[:, t, :], in_=s[:, t, :], func=ACT.Sigmoid)
+
+        w1d_q = quantise(flat(w1_d), E4, "w1d")
+        da = sb.tile([P, L, N], F32, name="da")
+        for t in range(L):
+            nc.vector.scalar_tensor_tensor(out=da[:, t, :], in0=dy_sb[:, t, :], scalar=c1_sb[:, t:t + 1], in1=ts_slot[:],
+                                           op0=ALU.mult, op1=ALU.mult)
+        g = sb.tile([P, L, N], F32, name="g")
+        for t in range(L):
+            a = bank(4 + t, "a%d" % t)
+            product(a[:], w1d_q, block(t), e_q, E4, True, True)
+            nc.vector.scalar_tensor_tensor(out=g[:, t, :], in0=a[:], scalar=c2_neg[:, t:t + 1], in1=ts_slot[:],
+                                           op0=ALU.mult, op1=ALU.mult)
+        w1_f = along_f(w1_d, "w1", 0)
+
+        halves = [slice(0, N // 2), slice(N // 2, N)]
+        for h in halves:
+            nc.vector.tensor_tensor(out=da[:, :, h], in0=da[:, :, h], in1=s[:, :, h], op=ALU.mult)
+        for h in halves:
+            nc.vector.scalar_tensor_tensor(out=g[:, :, h], in0=s[:, :, h], scalar=1.0, in1=g[:, :, h],
+                                           op0=ALU.subtract, op1=ALU.mult)
+        da_w = sb.tile([P, N, L], BF16, name="da_w", align_bytes=64)
+        db_w = sb.tile([P, N, L], BF16, name="db_w", align_bytes=64)
+
+        def woven(x, h):
+            return x[:, h, :].rearrange("p (c i) t -> p c t i", i=4)
+
+        def planar(x, h):
+            return x[:, :, h].rearrange("p t (c i) -> p c t i", i=4)
+
+        for h in halves:
+            nc.scalar.copy(out=woven(da_w, h), in_=planar(da, h))
+        w1f_q = quantise(flat(w1_f), E4, "w1f")
+        da_q = quantise(da_w[:].rearrange("p n t -> p (n t)"), E5, "da")
+        for h in halves:
+            nc.vector.tensor_tensor(out=woven(db_w, h), in0=planar(da, h), in1=planar(g, h), op=ALU.mult)
+        db_q = (sb.tile([P, N], U32, name="db_codes", align_bytes=64), sb.tile([P, N], U8, name="db_scales", align_bytes=64))
+        for h in halves:
+            nc.vector.quantize_mx(out=db_q[0][:, h].bitcast(E5), scales=db_q[1][:, h],
+                                  in_=db_w[:, h, :].rearrange("p n t -> p (n t)"))
+
+        order = [2, 0, 1, 3]
+        xs = [bank(2 + j, "x%d" % j) for j in range(L)]
+        for j in order:
+            product(xs[j][:], w1f_q, block(j), da_q, E5, True, False)
+        for j in order:
+            product(xs[j][:], w2f_q, block(j), db_q, E5, False, True)
+
+        pairs = [sb.tile([P, 2, CW, 2], BF16, name="pairs%d" % c) for c in range(CH)]
+        out_rows = out_0.rearrange("(p j) c -> p j c", j=L)
+
+        def place(j):
+            de = sb.tile([P, N], F32, name="de%d" % j, tag="de", bufs=3)
+            nc.scalar.copy(out=de[:], in_=xs[j][:])
+            nc.vector.tensor_copy(out=windows[j][:].indirect(offsets[:]), in_=de[:])
+            nc.sync.dma_start(out=out_rows[:, j, :], in_=windows[j][:])
+
+        def lane(j, chunks):
+            for c in chunks:
+                nc.scalar.copy(out=pairs[c][:, j // 2, :, j % 2], in_=windows[j][:, c * CW:(c + 1) * CW])
+
+        for j in order[:3]:
+            place(j)
+        lane(2, [0, 1])
+        place(3)
+        lane(2, [2, 3])
+        lane(0, range(CH))
+        lane(1, range(CH))
+
+        y_scales = sb.tile([P, T], U8, name="y_scales", align_bytes=64)
+        words_out = out_1[0].rearrange("p c l -> p (c l)").bitcast(I32)
+        on_vector = [0, 1]
+        ys = []
+        for c in range(CH):
+            cols = slice(c * CW, (c + 1) * CW)
+            if c in on_vector:
+                nc.vector.tensor_copy(out=pairs[c][:, 1, :, 1], in_=windows[L - 1][:, cols])
+            else:
+                nc.scalar.copy(out=pairs[c][:, 1, :, 1], in_=windows[L - 1][:, cols])
+
+            y = sb.tile([P, CW * L], BF16, name="y%d" % c, align_bytes=64)
+            ys.append(y)
+            if c not in on_vector:
+                nc.scalar.copy(out=y[:].bitcast(U32).rearrange("p (n u) -> p n u", u=2),
+                               in_=pairs[c][:].rearrange("p u n e -> p (u n e)").bitcast(U32).rearrange("p (u n) -> p n u", u=2))
+        for c in on_vector:
+            nc.vector.tensor_copy(out=ys[c][:].bitcast(I32).rearrange("p (n u) -> p n u", u=2),
+                                  in_=pairs[c][:].rearrange("p u n e -> p (u n e)").bitcast(I32).rearrange("p (u n) -> p n u", u=2))
+        for c in range(CH):
+            cols = slice(c * CW, (c + 1) * CW)
+            codes = sb.tile([P, CW], U32, name="y_codes%d" % c, align_bytes=64)
+            nc.vector.quantize_mx(out=codes[:].bitcast(E4), scales=y_scales[:, cols], in_=ys[c][:])
+            nc.sync.dma_start(out=words_out[:, cols], in_=codes[:].bitcast(I32))
+        for q in range(4):
+            nc.scalar.dma_start(out=out_2[0, 4 * q:4 * q + 4, :].bitcast(I32),
+                                in_=y_scales[32 * q:32 * q + 4, :].bitcast(I32))

@@ -34,11 +34,18 @@ def tile_attend_ggate_E_pl_kernel(tc, eT, w1, w2, dy, c1, c2, ts, offs, out_0, o
         def bank(i, name):
             return ps.tile([P, 512], F32, name=name, tag="bank%d" % i)
 
+        def operand(name):
+            return (sb.tile([P, N], U32, name=name + "_codes", align_bytes=64),
+                    sb.tile([P, N], U8, name=name + "_scales", align_bytes=64))
+
+        def quantise_part(dst, src, fmt, first, last):
+            nc.vector.quantize_mx(out=dst[0][:, first:last].bitcast(fmt), scales=dst[1][:, first:last],
+                                  in_=src[:, L * first:L * last])
+
         def quantise(src, fmt, name):
-            codes = sb.tile([P, N], U32, name=name + "_codes", align_bytes=64)
-            scales = sb.tile([P, N], U8, name=name + "_scales", align_bytes=64)
-            nc.vector.quantize_mx(out=codes[:].bitcast(fmt), scales=scales[:], in_=src)
-            return codes, scales
+            dst = operand(name)
+            quantise_part(dst, src, fmt, 0, N)
+            return dst
 
         ts_row = sb.tile([P, T // P], F32, name="ts_row")
         nc.sync.dma_start(out=ts_row[:], in_=ts[0:1, :].rearrange("o (p m) -> (o p) m", p=P))
@@ -53,13 +60,15 @@ def tile_attend_ggate_E_pl_kernel(tc, eT, w1, w2, dy, c1, c2, ts, offs, out_0, o
             nc.sync.dma_start(out=plane[:], in_=e_rows[:, j, :])
             e_planes.append(plane)
         c2_sb = sb.tile([P, L], F32, name="c2_sb")
-        nc.sync.dma_start(out=c2_sb[:], in_=c2.rearrange("(p t) o -> p (t o)", t=L))
+        nc.scalar.dma_start(out=c2_sb[:], in_=c2.rearrange("(p t) o -> p (t o)", t=L))
         c1_sb = sb.tile([P, L], F32, name="c1_sb")
-        nc.sync.dma_start(out=c1_sb[:], in_=c1.rearrange("(p t) o -> p (t o)", t=L))
+        nc.scalar.dma_start(out=c1_sb[:], in_=c1.rearrange("(p t) o -> p (t o)", t=L))
         w1_raw = sb.tile([P, L, K], F32, name="w1_raw")
         nc.sync.dma_start(out=w1_raw[:], in_=w1.rearrange("(p j) f -> p j f", j=L))
         dy_sb = sb.tile([P, L, N], F32, name="dy_sb")
-        nc.sync.dma_start(out=dy_sb[:], in_=dy.rearrange("(p t) n -> p t n", t=L))
+        dy_rows = dy.rearrange("(p t) n -> p t n", t=L)
+        nc.sync.dma_start(out=dy_sb[:, 0:2, :], in_=dy_rows[:, 0:2, :])
+        nc.sync.dma_start(out=dy_sb[:, 2:4, :], in_=dy_rows[:, 2:4, :])
 
         ident = sb.tile([P, P], F32, name="ident")
         make_identity(nc, ident[:])
@@ -108,6 +117,9 @@ def tile_attend_ggate_E_pl_kernel(tc, eT, w1, w2, dy, c1, c2, ts, offs, out_0, o
         c2_neg = sb.tile([P, L], F32, name="c2_neg")
         nc.vector.tensor_scalar(out=c2_neg[:], in0=c2_sb[:], scalar1=-1.0, scalar2=None, op0=ALU.mult)
         w2f_q = quantise(flat(w2_f), E4, "w2f")
+        da = sb.tile([P, L, N], F32, name="da")
+        for t in range(L):
+            nc.scalar.activation(out=da[:, t, :], in_=ts_slot[:], func=ACT.Copy, scale=c1_sb[:, t:t + 1])
 
         e_slot = sb.tile([P, N, L], BF16, name="e_slot", align_bytes=64)
         for j in range(L):
@@ -131,11 +143,11 @@ def tile_attend_ggate_E_pl_kernel(tc, eT, w1, w2, dy, c1, c2, ts, offs, out_0, o
                                            op0=ALU.mult, op1=ALU.mult)
             nc.scalar.activation(out=s[:, t, :], in_=s[:, t, :], func=ACT.Sigmoid)
 
-        w1d_q = quantise(flat(w1_d), E4, "w1d")
-        da = sb.tile([P, L, N], F32, name="da")
+        w1d_q = operand("w1d")
+        quantise_part(w1d_q, flat(w1_d), E4, 0, N // 2)
+        quantise_part(w1d_q, flat(w1_d), E4, N // 2, N)
         for t in range(L):
-            nc.vector.scalar_tensor_tensor(out=da[:, t, :], in0=dy_sb[:, t, :], scalar=c1_sb[:, t:t + 1], in1=ts_slot[:],
-                                           op0=ALU.mult, op1=ALU.mult)
+            nc.gpsimd.tensor_tensor(out=da[:, t, :], in0=da[:, t, :], in1=dy_sb[:, t, :], op=ALU.mult)
         g = sb.tile([P, L, N], F32, name="g")
         for t in range(L):
             a = bank(4 + t, "a%d" % t)
@@ -145,11 +157,6 @@ def tile_attend_ggate_E_pl_kernel(tc, eT, w1, w2, dy, c1, c2, ts, offs, out_0, o
         w1_f = along_f(w1_d, "w1", 0)
 
         halves = [slice(0, N // 2), slice(N // 2, N)]
-        for h in halves:
-            nc.vector.tensor_tensor(out=da[:, :, h], in0=da[:, :, h], in1=s[:, :, h], op=ALU.mult)
-        for h in halves:
-            nc.vector.scalar_tensor_tensor(out=g[:, :, h], in0=s[:, :, h], scalar=1.0, in1=g[:, :, h],
-                                           op0=ALU.subtract, op1=ALU.mult)
         da_w = sb.tile([P, N, L], BF16, name="da_w", align_bytes=64)
         db_w = sb.tile([P, N, L], BF16, name="db_w", align_bytes=64)
 
@@ -159,22 +166,30 @@ def tile_attend_ggate_E_pl_kernel(tc, eT, w1, w2, dy, c1, c2, ts, offs, out_0, o
         def planar(x, h):
             return x[:, :, h].rearrange("p t (c i) -> p c t i", i=4)
 
+        def gate_slope(h):
+            nc.vector.scalar_tensor_tensor(out=g[:, :, h], in0=s[:, :, h], scalar=1.0, in1=g[:, :, h],
+                                           op0=ALU.subtract, op1=ALU.mult)
+
+        gate_slope(halves[0])
         for h in halves:
+            nc.vector.tensor_tensor(out=da[:, :, h], in0=da[:, :, h], in1=s[:, :, h], op=ALU.mult)
             nc.scalar.copy(out=woven(da_w, h), in_=planar(da, h))
-        w1f_q = quantise(flat(w1_f), E4, "w1f")
+        gate_slope(halves[1])
+        w1f_q = operand("w1f")
+        quantise_part(w1f_q, flat(w1_f), E4, 2 * P, 3 * P)
+        nc.vector.tensor_tensor(out=woven(db_w, halves[0]), in0=planar(da, halves[0]), in1=planar(g, halves[0]), op=ALU.mult)
         da_q = quantise(da_w[:].rearrange("p n t -> p (n t)"), E5, "da")
-        for h in halves:
-            nc.vector.tensor_tensor(out=woven(db_w, h), in0=planar(da, h), in1=planar(g, h), op=ALU.mult)
-        db_q = (sb.tile([P, N], U32, name="db_codes", align_bytes=64), sb.tile([P, N], U8, name="db_scales", align_bytes=64))
-        for h in halves:
-            nc.vector.quantize_mx(out=db_q[0][:, h].bitcast(E5), scales=db_q[1][:, h],
-                                  in_=db_w[:, h, :].rearrange("p n t -> p (n t)"))
+        nc.vector.tensor_tensor(out=woven(db_w, halves[1]), in0=planar(da, halves[1]), in1=planar(g, halves[1]), op=ALU.mult)
+        db_q = operand("db")
+        quantise_part(db_q, db_w[:].rearrange("p n t -> p (n t)"), E5, 0, N // 2)
+        quantise_part(db_q, db_w[:].rearrange("p n t -> p (n t)"), E5, N // 2, N)
+        quantise_part(w1f_q, flat(w1_f), E4, 0, 2 * P)
+        quantise_part(w1f_q, flat(w1_f), E4, 3 * P, 4 * P)
 
         order = [2, 0, 1, 3]
         xs = [bank(2 + j, "x%d" % j) for j in range(L)]
         for j in order:
             product(xs[j][:], w1f_q, block(j), da_q, E5, True, False)
-        for j in order:
             product(xs[j][:], w2f_q, block(j), db_q, E5, False, True)
 
         pairs = [sb.tile([P, 2, CW, 2], BF16, name="pairs%d" % c) for c in range(CH)]

@@ -90,8 +90,9 @@ def tile_attend_ggate_E_pl_kernel(tc, eT, w1, w2, dy, c1, c2, ts, offs, out_0, o
 
         def along_d(raw, name):
             wd = sb.tile([P, L, P, L], BF16, name=name + "_d", align_bytes=64)
-            nc.scalar.copy(out=wd[:].rearrange("p t m j -> p m j t"),
-                           in_=raw[:].rearrange("p j (m t) -> p m j t", t=L))
+            for t in range(0, L, 2):
+                nc.scalar.copy(out=wd[:].rearrange("p t m j -> p m j t")[:, :, :, t:t + 2],
+                               in_=raw[:].rearrange("p j (m t) -> p m j t", t=L)[:, :, :, t:t + 2])
             return wd
 
         def along_f(wd, name, first_bank):
@@ -161,10 +162,10 @@ def tile_attend_ggate_E_pl_kernel(tc, eT, w1, w2, dy, c1, c2, ts, offs, out_0, o
         db_w = sb.tile([P, N, L], BF16, name="db_w", align_bytes=64)
 
         def woven(x, h):
-            return x[:, h, :].rearrange("p (c i) t -> p c t i", i=4)
+            return x[:, h, :].rearrange("p (c i) t -> p c t i", i=2)
 
         def planar(x, h):
-            return x[:, :, h].rearrange("p t (c i) -> p c t i", i=4)
+            return x[:, :, h].rearrange("p t (c i) -> p c t i", i=2)
 
         def gate_slope(h):
             nc.vector.scalar_tensor_tensor(out=g[:, :, h], in0=s[:, :, h], scalar=1.0, in1=g[:, :, h],
@@ -227,11 +228,11 @@ def tile_attend_ggate_E_pl_kernel(tc, eT, w1, w2, dy, c1, c2, ts, offs, out_0, o
             y = sb.tile([P, CW * L], BF16, name="y%d" % c, align_bytes=64)
             ys.append(y)
             if c not in on_vector:
-                nc.scalar.copy(out=y[:].bitcast(U32).rearrange("p (n u) -> p n u", u=2),
-                               in_=pairs[c][:].rearrange("p u n e -> p (u n e)").bitcast(U32).rearrange("p (u n) -> p n u", u=2))
+                nc.scalar.copy(out=y[:].bitcast(U32).rearrange("p (n i u) -> p n u i", u=2, i=2),
+                               in_=pairs[c][:].rearrange("p u n e -> p (u n e)").bitcast(U32).rearrange("p (u n i) -> p n u i", u=2, i=2))
         for c in on_vector:
-            nc.vector.tensor_copy(out=ys[c][:].bitcast(I32).rearrange("p (n u) -> p n u", u=2),
-                                  in_=pairs[c][:].rearrange("p u n e -> p (u n e)").bitcast(I32).rearrange("p (u n) -> p n u", u=2))
+            nc.vector.tensor_copy(out=ys[c][:].bitcast(I32).rearrange("p (n i u) -> p n u i", u=2, i=2),
+                                  in_=pairs[c][:].rearrange("p u n e -> p (u n e)").bitcast(I32).rearrange("p (u n i) -> p n u i", u=2, i=2))
         for c in range(CH):
             cols = slice(c * CW, (c + 1) * CW)
             codes = sb.tile([P, CW], U32, name="y_codes%d" % c, align_bytes=64)

@@ -35,7 +35,7 @@ def tile_attend_ggate_E_pl_kernel(tc, eT, w1, w2, dy, c1, c2, ts, offs, out_0, o
             return ps.tile([P, 512], F32, name=name, tag="bank%d" % i)
 
         def operand(name):
-            return (sb.tile([P, N], U32, name=name + "_codes", align_bytes=64),
+            return (sb.tile([P, N], U32, name=name + "_codes", tag=name + "_codes", align_bytes=64),
                     sb.tile([P, N], U8, name=name + "_scales", align_bytes=64))
 
         def quantise_part(dst, src, fmt, first, last):
@@ -63,9 +63,9 @@ def tile_attend_ggate_E_pl_kernel(tc, eT, w1, w2, dy, c1, c2, ts, offs, out_0, o
         nc.scalar.dma_start(out=c2_sb[:], in_=c2.rearrange("(p t) o -> p (t o)", t=L))
         c1_sb = sb.tile([P, L], F32, name="c1_sb")
         nc.scalar.dma_start(out=c1_sb[:], in_=c1.rearrange("(p t) o -> p (t o)", t=L))
-        w1_raw = sb.tile([P, L, K], F32, name="w1_raw")
+        w1_raw = sb.tile([P, L, K], F32, name="w1_raw", tag="w1_then_s")
         nc.sync.dma_start(out=w1_raw[:], in_=w1.rearrange("(p j) f -> p j f", j=L))
-        dy_sb = sb.tile([P, L, N], F32, name="dy_sb")
+        dy_sb = sb.tile([P, L, N], F32, name="dy_sb", tag="dy_then_da")
         dy_rows = dy.rearrange("(p t) n -> p t n", t=L)
         nc.sync.dma_start(out=dy_sb[:, 0:2, :], in_=dy_rows[:, 0:2, :])
         nc.sync.dma_start(out=dy_sb[:, 2:4, :], in_=dy_rows[:, 2:4, :])
@@ -73,11 +73,15 @@ def tile_attend_ggate_E_pl_kernel(tc, eT, w1, w2, dy, c1, c2, ts, offs, out_0, o
         ident = sb.tile([P, P], F32, name="ident")
         make_identity(nc, ident[:])
 
-        windows = []
-        for j in range(L):
-            win = sb.tile([P, T], F32, name="window%d" % j)
-            nc.vector.memset(win[:].bitcast(I32), 0)
-            windows.append(win)
+        windows = {}
+
+        def clear(j, engine, tag):
+            windows[j] = sb.tile([P, T], F32, name="window%d" % j, tag=tag)
+            engine.memset(windows[j][:].bitcast(I32), 0)
+
+        clear(2, nc.vector, "window2")
+        clear(0, nc.vector, "window0")
+        clear(1, nc.gpsimd, "window1")
 
         ts_all = sb.tile([P, T], F32, name="ts_all")
         ts_view = ts_all[:].rearrange("q (p m) -> q p m", p=P)
@@ -95,32 +99,32 @@ def tile_attend_ggate_E_pl_kernel(tc, eT, w1, w2, dy, c1, c2, ts, offs, out_0, o
                                in_=raw[:].rearrange("p j (m t) -> p m j t", t=L)[:, :, :, t:t + 2])
             return wd
 
-        def along_f(wd, name, first_bank):
+        def along_f(wf, wd, v, bk):
             words = wd[:].rearrange("p t m j -> p (t m j)").bitcast(F32).rearrange("p (t m v) -> p t m v", t=L, v=2)
-            wf = sb.tile([P, L, P, L], BF16, name=name + "_f", align_bytes=64)
-            for v in range(2):
-                bk = bank(first_bank + v, name + "_turn%d" % v)
-                for t in range(L):
-                    nc.tensor.transpose(bk[:, t * P:(t + 1) * P], words[:, t, :, v], ident[:])
-                nc.scalar.copy(out=wf[:, 2 * v:2 * v + 2, :, :],
-                               in_=bk[:].bitcast(BF16).rearrange("m (t p e) -> m e p t", t=L, e=2))
-            return wf
+            for t in range(L):
+                nc.tensor.transpose(bk[:, t * P:(t + 1) * P], words[:, t, :, v], ident[:])
+            nc.scalar.copy(out=wf[:, 2 * v:2 * v + 2, :, :],
+                           in_=bk[:].bitcast(BF16).rearrange("m (t p e) -> m e p t", t=L, e=2))
+
+        w1_f = sb.tile([P, L, P, L], BF16, name="w1_f", align_bytes=64)
+        w2_f = sb.tile([P, L, P, L], BF16, name="w2_f", align_bytes=64)
 
         def flat(x):
             return x[:].rearrange("p a b c -> p (a b c)")
 
         w2_d = along_d(w2_raw, "w2")
         w2d_q = quantise(flat(w2_d), E4, "w2d")
-        w2_f = along_f(w2_d, "w2", 4)
+        for v in range(2):
+            along_f(w2_f, w2_d, v, bank(4 + v, "w2_turn%d" % v))
 
         ts_slot = sb.tile([P, N], F32, name="ts_slot")
         nc.vector.tensor_copy(out=ts_slot[:], in_=ts_all[:].indirect(offsets[:]))
         c2_neg = sb.tile([P, L], F32, name="c2_neg")
         nc.vector.tensor_scalar(out=c2_neg[:], in0=c2_sb[:], scalar1=-1.0, scalar2=None, op0=ALU.mult)
         w2f_q = quantise(flat(w2_f), E4, "w2f")
-        da = sb.tile([P, L, N], F32, name="da")
+        dyc = sb.tile([P, L, N], F32, name="dyc", tag="dyc_then_slope")
         for t in range(L):
-            nc.scalar.activation(out=da[:, t, :], in_=ts_slot[:], func=ACT.Copy, scale=c1_sb[:, t:t + 1])
+            nc.scalar.activation(out=dyc[:, t, :], in_=ts_slot[:], func=ACT.Copy, scale=c1_sb[:, t:t + 1])
 
         e_slot = sb.tile([P, N, L], BF16, name="e_slot", align_bytes=64)
         for j in range(L):
@@ -136,56 +140,50 @@ def tile_attend_ggate_E_pl_kernel(tc, eT, w1, w2, dy, c1, c2, ts, offs, out_0, o
 
         w1_d = along_d(w1_raw, "w1")
 
-        s = sb.tile([P, L, N], F32, name="s")
+        u = sb.tile([P, L, N], F32, name="u")
+        s = sb.tile([P, L, N], F32, name="s", tag="w1_then_s")
         for t in range(L):
             b = bank(t, "b%d" % t)
             product(b[:], w2d_q, block(t), e_q, E4, True, True)
-            nc.vector.scalar_tensor_tensor(out=s[:, t, :], in0=b[:], scalar=c2_sb[:, t:t + 1], in1=ts_slot[:],
+            nc.vector.scalar_tensor_tensor(out=u[:, t, :], in0=b[:], scalar=c2_sb[:, t:t + 1], in1=ts_slot[:],
                                            op0=ALU.mult, op1=ALU.mult)
-            nc.scalar.activation(out=s[:, t, :], in_=s[:, t, :], func=ACT.Sigmoid)
+            nc.scalar.activation(out=s[:, t, :], in_=u[:, t, :], func=ACT.Sigmoid)
 
         w1d_q = operand("w1d")
         quantise_part(w1d_q, flat(w1_d), E4, 0, N // 2)
         quantise_part(w1d_q, flat(w1_d), E4, N // 2, N)
         for t in range(L):
-            nc.gpsimd.tensor_tensor(out=da[:, t, :], in0=da[:, t, :], in1=dy_sb[:, t, :], op=ALU.mult)
+            nc.gpsimd.tensor_tensor(out=dyc[:, t, :], in0=dyc[:, t, :], in1=dy_sb[:, t, :], op=ALU.mult)
         g = sb.tile([P, L, N], F32, name="g")
         for t in range(L):
             a = bank(4 + t, "a%d" % t)
             product(a[:], w1d_q, block(t), e_q, E4, True, True)
             nc.vector.scalar_tensor_tensor(out=g[:, t, :], in0=a[:], scalar=c2_neg[:, t:t + 1], in1=ts_slot[:],
                                            op0=ALU.mult, op1=ALU.mult)
-        w1_f = along_f(w1_d, "w1", 0)
+        along_f(w1_f, w1_d, 1, bank(0, "w1_turn1"))
 
-        halves = [slice(0, N // 2), slice(N // 2, N)]
         da_w = sb.tile([P, N, L], BF16, name="da_w", align_bytes=64)
         db_w = sb.tile([P, N, L], BF16, name="db_w", align_bytes=64)
 
-        def woven(x, h):
-            return x[:, h, :].rearrange("p (c i) t -> p c t i", i=2)
+        def woven(x):
+            return x[:].rearrange("p (c i) t -> p c t i", i=2)
 
-        def planar(x, h):
-            return x[:, :, h].rearrange("p t (c i) -> p c t i", i=2)
+        def planar(x):
+            return x[:].rearrange("p t (c i) -> p c t i", i=2)
 
-        def gate_slope(h):
-            nc.vector.scalar_tensor_tensor(out=g[:, :, h], in0=s[:, :, h], scalar=1.0, in1=g[:, :, h],
-                                           op0=ALU.subtract, op1=ALU.mult)
-
-        gate_slope(halves[0])
-        for h in halves:
-            nc.vector.tensor_tensor(out=da[:, :, h], in0=da[:, :, h], in1=s[:, :, h], op=ALU.mult)
-            nc.scalar.copy(out=woven(da_w, h), in_=planar(da, h))
-        gate_slope(halves[1])
+        da = sb.tile([P, L, N], F32, name="da", tag="dy_then_da")
+        nc.gpsimd.tensor_tensor(out=da[:, 0, :], in0=dyc[:, 0, :], in1=s[:, 0, :], op=ALU.mult)
+        nc.vector.tensor_tensor(out=da[:, 1:, :], in0=dyc[:, 1:, :], in1=s[:, 1:, :], op=ALU.mult)
+        nc.scalar.copy(out=woven(da_w), in_=planar(da))
+        slope = sb.tile([P, L, N], F32, name="slope", tag="dyc_then_slope")
+        nc.vector.scalar_tensor_tensor(out=slope[:], in0=s[:], scalar=1.0, in1=g[:], op0=ALU.subtract, op1=ALU.mult)
         w1f_q = operand("w1f")
-        quantise_part(w1f_q, flat(w1_f), E4, 2 * P, 3 * P)
-        nc.vector.tensor_tensor(out=woven(db_w, halves[0]), in0=planar(da, halves[0]), in1=planar(g, halves[0]), op=ALU.mult)
+        quantise_part(w1f_q, flat(w1_f), E4, 2 * P, 4 * P)
+        along_f(w1_f, w1_d, 0, bank(1, "w1_turn0"))
         da_q = quantise(da_w[:].rearrange("p n t -> p (n t)"), E5, "da")
-        nc.vector.tensor_tensor(out=woven(db_w, halves[1]), in0=planar(da, halves[1]), in1=planar(g, halves[1]), op=ALU.mult)
-        db_q = operand("db")
-        quantise_part(db_q, db_w[:].rearrange("p n t -> p (n t)"), E5, 0, N // 2)
-        quantise_part(db_q, db_w[:].rearrange("p n t -> p (n t)"), E5, N // 2, N)
+        nc.vector.tensor_tensor(out=woven(db_w), in0=planar(da), in1=planar(slope), op=ALU.mult)
+        db_q = quantise(db_w[:].rearrange("p n t -> p (n t)"), E5, "db")
         quantise_part(w1f_q, flat(w1_f), E4, 0, 2 * P)
-        quantise_part(w1f_q, flat(w1_f), E4, 3 * P, 4 * P)
 
         order = [2, 0, 1, 3]
         xs = [bank(2 + j, "x%d" % j) for j in range(L)]
@@ -193,11 +191,12 @@ def tile_attend_ggate_E_pl_kernel(tc, eT, w1, w2, dy, c1, c2, ts, offs, out_0, o
             product(xs[j][:], w1f_q, block(j), da_q, E5, True, False)
             product(xs[j][:], w2f_q, block(j), db_q, E5, False, True)
 
-        pairs = [sb.tile([P, 2, CW, 2], BF16, name="pairs%d" % c) for c in range(CH)]
+        pairs = [sb.tile([P, 2, CW, 2], BF16, name="pairs%d" % c, tag=name + "_codes", align_bytes=64)
+                 for c, name in enumerate(["db", "w2f", "da", "w1f"])]
         out_rows = out_0.rearrange("(p j) c -> p j c", j=L)
 
-        def place(j):
-            de = sb.tile([P, N], F32, name="de%d" % j, tag="de", bufs=3)
+        def place(j, tag):
+            de = sb.tile([P, N], F32, name="de%d" % j, tag=tag)
             nc.scalar.copy(out=de[:], in_=xs[j][:])
             nc.vector.tensor_copy(out=windows[j][:].indirect(offsets[:]), in_=de[:])
             nc.sync.dma_start(out=out_rows[:, j, :], in_=windows[j][:])
@@ -206,13 +205,18 @@ def tile_attend_ggate_E_pl_kernel(tc, eT, w1, w2, dy, c1, c2, ts, offs, out_0, o
             for c in chunks:
                 nc.scalar.copy(out=pairs[c][:, j // 2, :, j % 2], in_=windows[j][:, c * CW:(c + 1) * CW])
 
-        for j in order[:3]:
-            place(j)
+        place(2, "de2_then_de3")
+        place(0, "de0_then_window3")
+        place(1, "de1")
         lane(2, [0, 1])
-        place(3)
+        clear(3, nc.gpsimd, "de0_then_window3")
+        place(3, "de2_then_de3")
         lane(2, [2, 3])
-        lane(0, range(CH))
-        lane(1, range(CH))
+        for j in range(2):
+            lane(j, [0, 1])
+            for c in [2, 3]:
+                nc.gpsimd.tensor_scalar(out=pairs[c][:, 0, :, j], in0=windows[j][:, c * CW:(c + 1) * CW],
+                                        scalar1=1.0, scalar2=0.0, op0=ALU.mult, op1=ALU.add)
 
         y_scales = sb.tile([P, T], U8, name="y_scales", align_bytes=64)
         words_out = out_1[0].rearrange("p c l -> p (c l)").bitcast(I32)
@@ -228,11 +232,11 @@ def tile_attend_ggate_E_pl_kernel(tc, eT, w1, w2, dy, c1, c2, ts, offs, out_0, o
             y = sb.tile([P, CW * L], BF16, name="y%d" % c, align_bytes=64)
             ys.append(y)
             if c not in on_vector:
-                nc.scalar.copy(out=y[:].bitcast(U32).rearrange("p (n i u) -> p n u i", u=2, i=2),
-                               in_=pairs[c][:].rearrange("p u n e -> p (u n e)").bitcast(U32).rearrange("p (u n i) -> p n u i", u=2, i=2))
+                nc.scalar.copy(out=y[:].bitcast(U32).rearrange("p (n u) -> p n u", u=2),
+                               in_=pairs[c][:].rearrange("p u n e -> p (u n e)").bitcast(U32).rearrange("p (u n) -> p n u", u=2))
         for c in on_vector:
-            nc.vector.tensor_copy(out=ys[c][:].bitcast(I32).rearrange("p (n i u) -> p n u i", u=2, i=2),
-                                  in_=pairs[c][:].rearrange("p u n e -> p (u n e)").bitcast(I32).rearrange("p (u n i) -> p n u i", u=2, i=2))
+            nc.vector.tensor_copy(out=ys[c][:].bitcast(I32).rearrange("p (n u) -> p n u", u=2),
+                                  in_=pairs[c][:].rearrange("p u n e -> p (u n e)").bitcast(I32).rearrange("p (u n) -> p n u", u=2))
         for c in range(CH):
             cols = slice(c * CW, (c + 1) * CW)
             codes = sb.tile([P, CW], U32, name="y_codes%d" % c, align_bytes=64)

@@ -79,9 +79,10 @@ def tile_attend_ggate_E_pl_kernel(tc, eT, w1, w2, dy, c1, c2, ts, offs, out_0, o
             windows[j] = sb.tile([P, T], F32, name="window%d" % j, tag=tag)
             engine.memset(windows[j][:].bitcast(I32), 0)
 
-        clear(2, nc.vector, "window2")
         clear(0, nc.vector, "window0")
+        clear(2, nc.vector, "window2")
         clear(1, nc.gpsimd, "window1")
+        clear(3, nc.gpsimd, "window3")
 
         ts_all = sb.tile([P, T], F32, name="ts_all")
         ts_view = ts_all[:].rearrange("q (p m) -> q p m", p=P)
@@ -185,63 +186,63 @@ def tile_attend_ggate_E_pl_kernel(tc, eT, w1, w2, dy, c1, c2, ts, offs, out_0, o
         db_q = quantise(db_w[:].rearrange("p n t -> p (n t)"), E5, "db")
         quantise_part(w1f_q, flat(w1_f), E4, 0, 2 * P)
 
-        order = [2, 0, 1, 3]
         xs = [bank(2 + j, "x%d" % j) for j in range(L)]
-        for j in order:
+        for j in range(L):
             product(xs[j][:], w1f_q, block(j), da_q, E5, True, False)
             product(xs[j][:], w2f_q, block(j), db_q, E5, False, True)
 
-        pairs = [sb.tile([P, 2, CW, 2], BF16, name="pairs%d" % c, tag=name + "_codes", align_bytes=64)
-                 for c, name in enumerate(["db", "w2f", "da", "w1f"])]
+        pairs = [sb.tile([P, 2, CW, 2], BF16, name="pairs%d" % c, align_bytes=64) for c in range(CH)]
         out_rows = out_0.rearrange("(p j) c -> p j c", j=L)
+        des = [sb.tile([P, N], F32, name="de%d" % j) for j in range(L)]
+        half = N // 2
 
-        def place(j, tag):
-            de = sb.tile([P, N], F32, name="de%d" % j, tag=tag)
-            nc.scalar.copy(out=de[:], in_=xs[j][:])
-            nc.vector.tensor_copy(out=windows[j][:].indirect(offsets[:]), in_=de[:])
+        def scatter_vector(j):
+            nc.vector.tensor_copy(out=windows[j][:].indirect(offsets[:]), in_=des[j][:])
             nc.sync.dma_start(out=out_rows[:, j, :], in_=windows[j][:])
 
-        def lane(j, chunks):
-            for c in chunks:
-                nc.scalar.copy(out=pairs[c][:, j // 2, :, j % 2], in_=windows[j][:, c * CW:(c + 1) * CW])
+        def scatter_scalar(j):
+            for h in range(2):
+                nc.scalar.activation(out=windows[j][:].indirect(offsets[:, h * half // 16:(h + 1) * half // 16]),
+                                     in_=des[j][:, h * half:(h + 1) * half], func=ACT.Copy)
+            nc.sync.dma_start(out=out_rows[:, j, :], in_=windows[j][:])
 
-        place(2, "de2_then_de3")
-        place(0, "de0_then_window3")
-        place(1, "de1")
-        lane(2, [0, 1])
-        clear(3, nc.gpsimd, "de0_then_window3")
-        place(3, "de2_then_de3")
-        lane(2, [2, 3])
+        nc.vector.tensor_copy(out=des[0][:], in_=xs[0][:])
+        nc.scalar.copy(out=des[1][:], in_=xs[1][:])
+        nc.scalar.copy(out=des[2][:], in_=xs[2][:])
+        scatter_vector(0)
+        scatter_scalar(1)
+        nc.scalar.copy(out=des[3][:], in_=xs[3][:])
+        scatter_vector(2)
+        scatter_scalar(3)
+        on_vector = [0, 1]
         for j in range(2):
-            lane(j, [0, 1])
-            for c in [2, 3]:
-                nc.gpsimd.tensor_scalar(out=pairs[c][:, 0, :, j], in0=windows[j][:, c * CW:(c + 1) * CW],
-                                        scalar1=1.0, scalar2=0.0, op0=ALU.mult, op1=ALU.add)
+            for c in range(CH):
+                if c not in on_vector:
+                    nc.gpsimd.tensor_scalar(out=pairs[c][:, 0, :, j], in0=windows[j][:, c * CW:(c + 1) * CW],
+                                            scalar1=1.0, scalar2=0.0, op0=ALU.mult, op1=ALU.add)
+        words_out = out_1[0].rearrange("p c l -> p (c l)").bitcast(I32)
+        ys = [sb.tile([P, CW * L], BF16, name="y%d" % c, align_bytes=64) for c in range(CH)]
+
+        def pair_words(c, dtype):
+            return pairs[c][:].rearrange("p u n e -> p (u n e)").bitcast(dtype).rearrange("p (u n) -> p n u", u=2)
+
+        for j in range(L):
+            for c in on_vector:
+                nc.vector.tensor_copy(out=pairs[c][:, j // 2, :, j % 2], in_=windows[j][:, c * CW:(c + 1) * CW])
+        for c in range(CH):
+            if c in on_vector:
+                nc.vector.tensor_copy(out=ys[c][:].bitcast(I32).rearrange("p (n u) -> p n u", u=2), in_=pair_words(c, I32))
+            else:
+                for j in range(2, L):
+                    nc.scalar.copy(out=pairs[c][:, 1, :, j % 2], in_=windows[j][:, c * CW:(c + 1) * CW])
+                nc.scalar.copy(out=ys[c][:].bitcast(U32).rearrange("p (n u) -> p n u", u=2), in_=pair_words(c, U32))
 
         y_scales = sb.tile([P, T], U8, name="y_scales", align_bytes=64)
-        words_out = out_1[0].rearrange("p c l -> p (c l)").bitcast(I32)
-        on_vector = [0, 1]
-        ys = []
-        for c in range(CH):
-            cols = slice(c * CW, (c + 1) * CW)
-            if c in on_vector:
-                nc.vector.tensor_copy(out=pairs[c][:, 1, :, 1], in_=windows[L - 1][:, cols])
-            else:
-                nc.scalar.copy(out=pairs[c][:, 1, :, 1], in_=windows[L - 1][:, cols])
-
-            y = sb.tile([P, CW * L], BF16, name="y%d" % c, align_bytes=64)
-            ys.append(y)
-            if c not in on_vector:
-                nc.scalar.copy(out=y[:].bitcast(U32).rearrange("p (n u) -> p n u", u=2),
-                               in_=pairs[c][:].rearrange("p u n e -> p (u n e)").bitcast(U32).rearrange("p (u n) -> p n u", u=2))
-        for c in on_vector:
-            nc.vector.tensor_copy(out=ys[c][:].bitcast(I32).rearrange("p (n u) -> p n u", u=2),
-                                  in_=pairs[c][:].rearrange("p u n e -> p (u n e)").bitcast(I32).rearrange("p (u n) -> p n u", u=2))
         for c in range(CH):
             cols = slice(c * CW, (c + 1) * CW)
             codes = sb.tile([P, CW], U32, name="y_codes%d" % c, align_bytes=64)
             nc.vector.quantize_mx(out=codes[:].bitcast(E4), scales=y_scales[:, cols], in_=ys[c][:])
             nc.sync.dma_start(out=words_out[:, cols], in_=codes[:].bitcast(I32))
-        for q in range(4):
-            nc.scalar.dma_start(out=out_2[0, 4 * q:4 * q + 4, :].bitcast(I32),
-                                in_=y_scales[32 * q:32 * q + 4, :].bitcast(I32))
+        for q, queue in enumerate([nc.scalar, nc.scalar, nc.sync, nc.sync]):
+            queue.dma_start(out=out_2[0, 4 * q:4 * q + 4, :].bitcast(I32),
+                            in_=y_scales[32 * q:32 * q + 4, :].bitcast(I32))

@@ -17,6 +17,7 @@ ACT = mybir.ActivationFunctionType
 P = 128
 L = 4
 N = 512
+H = N // 2
 T = 2048
 K = 512
 CH = 4
@@ -34,18 +35,21 @@ def tile_attend_ggate_E_pl_kernel(tc, eT, w1, w2, dy, c1, c2, ts, offs, out_0, o
         def bank(i, name):
             return ps.tile([P, 512], F32, name=name, tag="bank%d" % i)
 
-        def operand(name):
-            return (sb.tile([P, N], U32, name=name + "_codes", tag=name + "_codes", align_bytes=64),
-                    sb.tile([P, N], U8, name=name + "_scales", align_bytes=64))
+        def quantise(src, fmt, name, width):
+            codes = sb.tile([P, width], U32, name=name + "_codes", align_bytes=64)
+            scales = sb.tile([P, width], U8, name=name + "_scales", align_bytes=64)
+            nc.vector.quantize_mx(out=codes[:].bitcast(fmt), scales=scales[:], in_=src)
+            return codes, scales
 
-        def quantise_part(dst, src, fmt, first, last):
-            nc.vector.quantize_mx(out=dst[0][:, first:last].bitcast(fmt), scales=dst[1][:, first:last],
-                                  in_=src[:, L * first:L * last])
+        def product(out, stat, stat_cols, mov, mov_cols, mov_fmt, start, stop):
+            nc.tensor.matmul_mx(out=out, lhsT=stat[0][:, stat_cols].bitcast(E4), lhsT_scale=stat[1][:, stat_cols],
+                                rhs=mov[0][:, mov_cols].bitcast(mov_fmt), rhs_scale=mov[1][:, mov_cols], start=start, stop=stop)
 
-        def quantise(src, fmt, name):
-            dst = operand(name)
-            quantise_part(dst, src, fmt, 0, N)
-            return dst
+        def block(i):
+            return slice(i * P, (i + 1) * P)
+
+        def half(h):
+            return slice(h * H, (h + 1) * H)
 
         ts_row = sb.tile([P, T // P], F32, name="ts_row")
         nc.sync.dma_start(out=ts_row[:], in_=ts[0:1, :].rearrange("o (p m) -> (o p) m", p=P))
@@ -53,36 +57,33 @@ def tile_attend_ggate_E_pl_kernel(tc, eT, w1, w2, dy, c1, c2, ts, offs, out_0, o
         nc.sync.dma_start(offsets[:], offs)
         w2_raw = sb.tile([P, L, K], F32, name="w2_raw")
         nc.sync.dma_start(out=w2_raw[:], in_=w2.rearrange("(p j) f -> p j f", j=L))
-        e_rows = eT.rearrange("(p j) c -> p j c", j=L)
-        e_planes = []
-        for j in range(L):
-            plane = sb.tile([P, T], F32, name="e_plane%d" % j)
-            nc.sync.dma_start(out=plane[:], in_=e_rows[:, j, :])
-            e_planes.append(plane)
+        w1_raw = sb.tile([P, L, K], F32, name="w1_raw")
+        nc.sync.dma_start(out=w1_raw[:], in_=w1.rearrange("(p j) f -> p j f", j=L))
+        dy_sb = sb.tile([P, L, N], F32, name="dy_sb")
+        nc.sync.dma_start(out=dy_sb[:], in_=dy.rearrange("(p t) n -> p t n", t=L))
         c2_sb = sb.tile([P, L], F32, name="c2_sb")
         nc.scalar.dma_start(out=c2_sb[:], in_=c2.rearrange("(p t) o -> p (t o)", t=L))
         c1_sb = sb.tile([P, L], F32, name="c1_sb")
         nc.scalar.dma_start(out=c1_sb[:], in_=c1.rearrange("(p t) o -> p (t o)", t=L))
-        w1_raw = sb.tile([P, L, K], F32, name="w1_raw", tag="w1_then_s")
-        nc.sync.dma_start(out=w1_raw[:], in_=w1.rearrange("(p j) f -> p j f", j=L))
-        dy_sb = sb.tile([P, L, N], F32, name="dy_sb", tag="dy_then_da")
-        dy_rows = dy.rearrange("(p t) n -> p t n", t=L)
-        nc.sync.dma_start(out=dy_sb[:, 0:2, :], in_=dy_rows[:, 0:2, :])
-        nc.sync.dma_start(out=dy_sb[:, 2:4, :], in_=dy_rows[:, 2:4, :])
+        e_rows = eT.rearrange("(p j) c -> p j c", j=L)
+        e_planes = []
+        for j in range(L):
+            plane = sb.tile([P, T], F32, name="e_plane%d" % j, tag="plane_then_y%d" % j, align_bytes=64)
+            nc.sync.dma_start(out=plane[:], in_=e_rows[:, j, :])
+            e_planes.append(plane)
+
+        def offsets_of(h):
+            return offsets[:, h * H // 16:(h + 1) * H // 16]
 
         ident = sb.tile([P, P], F32, name="ident")
         make_identity(nc, ident[:])
 
-        windows = {}
+        warm = sb.tile([P, 1], F32, name="warm")
+        nc.scalar.activation(out=warm[:], in_=ident[:, 0:1], func=ACT.Sigmoid)
 
-        def clear(j, engine, tag):
-            windows[j] = sb.tile([P, T], F32, name="window%d" % j, tag=tag)
+        windows = [sb.tile([P, T], F32, name="window%d" % j) for j in range(L)]
+        for j, engine in enumerate([nc.vector, nc.gpsimd, nc.vector, nc.gpsimd]):
             engine.memset(windows[j][:].bitcast(I32), 0)
-
-        clear(0, nc.vector, "window0")
-        clear(2, nc.vector, "window2")
-        clear(1, nc.gpsimd, "window1")
-        clear(3, nc.gpsimd, "window3")
 
         ts_all = sb.tile([P, T], F32, name="ts_all")
         ts_view = ts_all[:].rearrange("q (p m) -> q p m", p=P)
@@ -92,157 +93,207 @@ def tile_attend_ggate_E_pl_kernel(tc, eT, w1, w2, dy, c1, c2, ts, offs, out_0, o
                 m = 4 * g + r
                 nc.tensor.transpose(bk[:, r * P:(r + 1) * P], ts_row[:, m:m + 1].to_broadcast([P, P]), ident[:])
             nc.scalar.copy(out=ts_view[:, :, 4 * g:4 * g + 4], in_=bk[:].rearrange("q (r p) -> q p r", r=4))
-
-        def along_d(raw, name):
-            wd = sb.tile([P, L, P, L], BF16, name=name + "_d", align_bytes=64)
-            for t in range(0, L, 2):
-                nc.scalar.copy(out=wd[:].rearrange("p t m j -> p m j t")[:, :, :, t:t + 2],
-                               in_=raw[:].rearrange("p j (m t) -> p m j t", t=L)[:, :, :, t:t + 2])
-            return wd
-
-        def along_f(wf, wd, v, bk):
-            words = wd[:].rearrange("p t m j -> p (t m j)").bitcast(F32).rearrange("p (t m v) -> p t m v", t=L, v=2)
-            for t in range(L):
-                nc.tensor.transpose(bk[:, t * P:(t + 1) * P], words[:, t, :, v], ident[:])
-            nc.scalar.copy(out=wf[:, 2 * v:2 * v + 2, :, :],
-                           in_=bk[:].bitcast(BF16).rearrange("m (t p e) -> m e p t", t=L, e=2))
-
-        w1_f = sb.tile([P, L, P, L], BF16, name="w1_f", align_bytes=64)
-        w2_f = sb.tile([P, L, P, L], BF16, name="w2_f", align_bytes=64)
+        ts_slot = sb.tile([P, N], F32, name="ts_slot")
+        nc.scalar.activation(out=ts_slot[:], in_=ts_all[:].indirect(offsets[:]), func=ACT.Copy)
+        ts_turn = bank(0, "ts_turn")
+        for i in range(4):
+            nc.tensor.transpose(ts_turn[:, block(i)], ts_slot[:, block(i)], ident[:])
+        ts_col = sb.tile([P, 4], F32, name="ts_col")
+        nc.scalar.copy(out=ts_col[:], in_=ts_turn[:].rearrange("p (i q) -> p i q", i=4)[:, :, 0])
 
         def flat(x):
             return x[:].rearrange("p a b c -> p (a b c)")
 
-        w2_d = along_d(w2_raw, "w2")
-        w2d_q = quantise(flat(w2_d), E4, "w2d")
-        for v in range(2):
-            along_f(w2_f, w2_d, v, bank(4 + v, "w2_turn%d" % v))
+        def weights(raw, name, first_bank):
+            wd = sb.tile([P, L, P, L], BF16, name=name + "_d", align_bytes=64)
+            nc.vector.tensor_copy(out=wd[:].rearrange("p t m j -> p m j t"),
+                                  in_=raw[:].rearrange("p j (m t) -> p m j t", t=L))
+            wd_q = quantise(flat(wd), E4, name + "d", K)
+            wf = sb.tile([P, L, P, L], BF16, name=name + "_f", align_bytes=64)
+            words = flat(wd).bitcast(F32).rearrange("p (t m v) -> p t m v", t=L, v=2)
+            for v in range(2):
+                bk = bank(first_bank + v, "%s_turn%d" % (name, v))
+                for t in range(L):
+                    nc.tensor.transpose(bk[:, block(t)], words[:, t, :, v], ident[:])
+                nc.scalar.copy(out=wf[:, 2 * v:2 * v + 2, :, :],
+                               in_=bk[:].bitcast(BF16).rearrange("m (t p e) -> m e p t", t=L, e=2))
+            return wd_q, wf
 
-        ts_slot = sb.tile([P, N], F32, name="ts_slot")
-        nc.vector.tensor_copy(out=ts_slot[:], in_=ts_all[:].indirect(offsets[:]))
+        w2d_q, w2_f = weights(w2_raw, "w2", 4)
+        w1d_q, w1_f = weights(w1_raw, "w1", 6)
+
         c2_neg = sb.tile([P, L], F32, name="c2_neg")
         nc.vector.tensor_scalar(out=c2_neg[:], in0=c2_sb[:], scalar1=-1.0, scalar2=None, op0=ALU.mult)
-        w2f_q = quantise(flat(w2_f), E4, "w2f")
-        dyc = sb.tile([P, L, N], F32, name="dyc", tag="dyc_then_slope")
+        for_da = sb.tile([P, L, N], F32, name="for_da")
+        for_db = sb.tile([P, L, N], F32, name="for_db")
         for t in range(L):
-            nc.scalar.activation(out=dyc[:, t, :], in_=ts_slot[:], func=ACT.Copy, scale=c1_sb[:, t:t + 1])
-
-        e_slot = sb.tile([P, N, L], BF16, name="e_slot", align_bytes=64)
-        for j in range(L):
-            nc.vector.tensor_copy(out=e_slot[:, :, j], in_=e_planes[j][:].indirect(offsets[:]))
-        e_q = quantise(e_slot[:].rearrange("p n j -> p (n j)"), E4, "e")
-
-        def product(out, stat, cols, mov, mov_fmt, start, stop):
-            nc.tensor.matmul_mx(out=out, lhsT=stat[0][:, cols].bitcast(E4), lhsT_scale=stat[1][:, cols],
-                                rhs=mov[0][:].bitcast(mov_fmt), rhs_scale=mov[1][:], start=start, stop=stop)
-
-        def block(i):
-            return slice(i * P, (i + 1) * P)
-
-        w1_d = along_d(w1_raw, "w1")
-
-        u = sb.tile([P, L, N], F32, name="u")
-        s = sb.tile([P, L, N], F32, name="s", tag="w1_then_s")
+            nc.vector.scalar_tensor_tensor(out=for_da[:, t, :], in0=dy_sb[:, t, :], scalar=c1_sb[:, t:t + 1],
+                                           in1=ts_slot[:], op0=ALU.mult, op1=ALU.mult)
+        w2f_q = quantise(flat(w2_f), E4, "w2f", K)
         for t in range(L):
-            b = bank(t, "b%d" % t)
-            product(b[:], w2d_q, block(t), e_q, E4, True, True)
-            nc.vector.scalar_tensor_tensor(out=u[:, t, :], in0=b[:], scalar=c2_sb[:, t:t + 1], in1=ts_slot[:],
-                                           op0=ALU.mult, op1=ALU.mult)
-            nc.scalar.activation(out=s[:, t, :], in_=u[:, t, :], func=ACT.Sigmoid)
+            nc.vector.scalar_tensor_tensor(out=for_db[:, t, :], in0=for_da[:, t, :], scalar=c2_neg[:, t:t + 1],
+                                           in1=ts_slot[:], op0=ALU.mult, op1=ALU.mult)
+        w1f_q = quantise(flat(w1_f), E4, "w1f", K)
 
-        w1d_q = operand("w1d")
-        quantise_part(w1d_q, flat(w1_d), E4, 0, N // 2)
-        quantise_part(w1d_q, flat(w1_d), E4, N // 2, N)
-        for t in range(L):
-            nc.gpsimd.tensor_tensor(out=dyc[:, t, :], in0=dyc[:, t, :], in1=dy_sb[:, t, :], op=ALU.mult)
-        g = sb.tile([P, L, N], F32, name="g")
-        for t in range(L):
-            a = bank(4 + t, "a%d" % t)
-            product(a[:], w1d_q, block(t), e_q, E4, True, True)
-            nc.vector.scalar_tensor_tensor(out=g[:, t, :], in0=a[:], scalar=c2_neg[:, t:t + 1], in1=ts_slot[:],
-                                           op0=ALU.mult, op1=ALU.mult)
-        along_f(w1_f, w1_d, 1, bank(0, "w1_turn1"))
-
-        da_w = sb.tile([P, N, L], BF16, name="da_w", align_bytes=64)
-        db_w = sb.tile([P, N, L], BF16, name="db_w", align_bytes=64)
+        e_low = sb.tile([P, 2, N], BF16, name="e_low")
+        e_slot = [sb.tile([P, H, L], BF16, name="e_slot%d" % h, align_bytes=64) for h in range(2)]
+        for j in range(2):
+            nc.scalar.activation(out=e_low[:, j, :], in_=e_planes[j][:].indirect(offsets[:]), func=ACT.Copy)
+        for h in range(2):
+            nc.scalar.copy(out=e_slot[h][:, :, 0:2], in_=e_low[:, :, half(h)].rearrange("p j n -> p n j"))
+        for h in range(2):
+            nc.vector.tensor_copy(out=e_slot[h][:, :, 2], in_=e_planes[2][:].indirect(offsets_of(h)))
+        e_q = []
+        for h in range(2):
+            nc.vector.tensor_copy(out=e_slot[h][:, :, 3], in_=e_planes[3][:].indirect(offsets_of(h)))
+            e_q.append(quantise(e_slot[h][:].rearrange("p n j -> p (n j)"), E4, "e%d" % h, H))
 
         def woven(x):
-            return x[:].rearrange("p (c i) t -> p c t i", i=2)
+            return x.rearrange("p (c i) t -> p c t i", i=2)
 
         def planar(x):
-            return x[:].rearrange("p t (c i) -> p c t i", i=2)
+            return x.rearrange("p t (c i) -> p c t i", i=2)
 
-        da = sb.tile([P, L, N], F32, name="da", tag="dy_then_da")
-        nc.gpsimd.tensor_tensor(out=da[:, 0, :], in0=dyc[:, 0, :], in1=s[:, 0, :], op=ALU.mult)
-        nc.vector.tensor_tensor(out=da[:, 1:, :], in0=dyc[:, 1:, :], in1=s[:, 1:, :], op=ALU.mult)
-        nc.scalar.copy(out=woven(da_w), in_=planar(da))
-        slope = sb.tile([P, L, N], F32, name="slope", tag="dyc_then_slope")
-        nc.vector.scalar_tensor_tensor(out=slope[:], in0=s[:], scalar=1.0, in1=g[:], op0=ALU.subtract, op1=ALU.mult)
-        w1f_q = operand("w1f")
-        quantise_part(w1f_q, flat(w1_f), E4, 2 * P, 4 * P)
-        along_f(w1_f, w1_d, 0, bank(1, "w1_turn0"))
-        da_q = quantise(da_w[:].rearrange("p n t -> p (n t)"), E5, "da")
-        nc.vector.tensor_tensor(out=woven(db_w), in0=planar(da), in1=planar(slope), op=ALU.mult)
-        db_q = quantise(db_w[:].rearrange("p n t -> p (n t)"), E5, "db")
-        quantise_part(w1f_q, flat(w1_f), E4, 0, 2 * P)
+        b_ts = [sb.tile([P, K], F32, name="b_ts%d" % i) for i in range(4)]
+        s = [sb.tile([P, L, H], F32, name="s%d" % h) for h in range(2)]
+        sq = [sb.tile([P, H, L], F32, name="sq%d" % h) for h in range(2)]
+        ga = [sb.tile([P, H, L], F32, name="ga%d" % h) for h in range(2)]
 
-        xs = [bank(2 + j, "x%d" % j) for j in range(L)]
-        for j in range(L):
-            product(xs[j][:], w1f_q, block(j), da_q, E5, True, False)
-            product(xs[j][:], w2f_q, block(j), db_q, E5, False, True)
+        def turned_b(i):
+            bk = bank(i, "b_turned%d" % i)
+            product(bk[:], e_q[i // 2], block(i % 2), w2d_q, slice(0, K), E4, True, True)
+            nc.scalar.activation(out=b_ts[i][:], in_=bk[:], func=ACT.Copy, scale=ts_col[:, i:i + 1])
 
-        pairs = [sb.tile([P, 2, CW, 2], BF16, name="pairs%d" % c, align_bytes=64) for c in range(CH)]
+        def times_a(i, bank_nr):
+            bk = bank(bank_nr, "a%d" % i)
+            for t in range(L):
+                product(bk[:, block(t)], w1d_q, block(t), e_q[i // 2], block(i % 2), E4, True, True)
+            nc.vector.tensor_tensor(out=woven(ga[i // 2][:, block(i % 2), :]),
+                                    in0=planar(bk[:].rearrange("p (t n) -> p t n", t=L)),
+                                    in1=planar(for_db[:, :, block(i)]), op=ALU.mult)
+
+        def gate(h, first_bank):
+            for u in range(2):
+                bk = bank(first_bank + u, "b_back%d_%d" % (h, u))
+                for i in range(2):
+                    for t in range(2):
+                        nc.tensor.transpose(bk[:, t * H + i * P:t * H + (i + 1) * P],
+                                            b_ts[2 * h + i][:, block(2 * u + t)], ident[:])
+                for t in range(2):
+                    nc.scalar.activation(out=s[h][:, 2 * u + t, :], in_=bk[:, half(t)], func=ACT.Sigmoid,
+                                         scale=c2_sb[:, 2 * u + t:2 * u + t + 1])
+
+        def square(h):
+            nc.scalar.activation(out=woven(sq[h][:]), in_=planar(s[h][:]), func=ACT.Square, bias=-0.5)
+
+        def gradient_a(h):
+            da_w = sb.tile([P, H, L], BF16, name="da_w%d" % h, align_bytes=64)
+            nc.vector.tensor_tensor(out=woven(da_w[:]), in0=planar(for_da[:, :, half(h)]), in1=planar(s[h][:]), op=ALU.mult)
+            return quantise(da_w[:].rearrange("p n t -> p (n t)"), E5, "da%d" % h, H)
+
+        def gradient_b(h):
+            db_w = sb.tile([P, H, L], BF16, name="db_w%d" % h, align_bytes=64)
+            nc.vector.scalar_tensor_tensor(out=db_w[:], in0=sq[h][:], scalar=0.25, in1=ga[h][:],
+                                           op0=ALU.subtract, op1=ALU.mult)
+            return quantise(db_w[:].rearrange("p n t -> p (n t)"), E5, "db%d" % h, H)
+
+        turned_b(0)
+        turned_b(1)
+        times_a(0, 4)
+        times_a(1, 5)
+        turned_b(2)
+        gate(0, 6)
+        turned_b(3)
+        square(0)
+        times_a(2, 4)
+        times_a(3, 5)
+        gate(1, 0)
+        square(1)
+
         out_rows = out_0.rearrange("(p j) c -> p j c", j=L)
-        des = [sb.tile([P, N], F32, name="de%d" % j) for j in range(L)]
-        half = N // 2
 
-        def scatter_vector(j):
-            nc.vector.tensor_copy(out=windows[j][:].indirect(offsets[:]), in_=des[j][:])
+        def result(out, j, grads):
+            product(out, w1f_q, block(j), grads[0], slice(0, H), E5, True, False)
+            product(out, w2f_q, block(j), grads[1], slice(0, H), E5, False, True)
+
+        grads = (gradient_a(0), gradient_b(0))
+        de_first = [sb.tile([P, 2, H], F32, name="de_first%d" % u) for u in range(2)]
+        for u in range(2):
+            bk = bank(2 + u, "x_first%d" % u)
+            for t in range(2):
+                result(bk[:, half(t)], 2 * u + t, grads)
+            nc.scalar.copy(out=de_first[u][:], in_=bk[:].rearrange("p (t n) -> p t n", t=2))
+
+        def scatter_scalar(j, h, src):
+            nc.scalar.activation(out=windows[j][:].indirect(offsets_of(h)), in_=src, func=ACT.Copy)
+
+        def scatter_vector(j, h, src):
+            nc.vector.tensor_copy(out=windows[j][:].indirect(offsets_of(h)), in_=src)
+
+        def store(j):
             nc.sync.dma_start(out=out_rows[:, j, :], in_=windows[j][:])
 
-        def scatter_scalar(j):
-            for h in range(2):
-                nc.scalar.activation(out=windows[j][:].indirect(offsets[:, h * half // 16:(h + 1) * half // 16]),
-                                     in_=des[j][:, h * half:(h + 1) * half], func=ACT.Copy)
-            nc.sync.dma_start(out=out_rows[:, j, :], in_=windows[j][:])
+        da_q = gradient_a(1)
+        xs = [bank(4 + j, "x_second%d" % j) for j in range(L)]
+        for j in range(L):
+            product(xs[j][:, 0:H], w1f_q, block(j), da_q, slice(0, H), E5, True, False)
+        db_q = gradient_b(1)
+        for j in range(L):
+            product(xs[j][:, 0:H], w2f_q, block(j), db_q, slice(0, H), E5, False, True)
+        scatter_scalar(0, 0, de_first[0][:, 0, :])
+        de_second = [sb.tile([P, H], F32, name="de_second%d" % j) for j in range(L)]
+        nc.vector.tensor_copy(out=de_second[0][:], in_=xs[0][:, 0:H])
+        scatter_vector(0, 1, de_second[0][:])
+        store(0)
+        scatter_scalar(1, 0, de_first[0][:, 1, :])
+        nc.scalar.copy(out=de_second[1][:], in_=xs[1][:, 0:H])
+        scatter_scalar(1, 1, de_second[1][:])
+        store(1)
+        nc.vector.tensor_copy(out=de_second[2][:], in_=xs[2][:, 0:H])
+        scatter_vector(2, 1, de_second[2][:])
+        scatter_vector(2, 0, de_first[1][:, 0, :])
+        store(2)
+        nc.scalar.copy(out=de_second[3][:], in_=xs[3][:, 0:H])
+        scatter_scalar(3, 0, de_first[1][:, 1, :])
+        scatter_scalar(3, 1, de_second[3][:])
+        store(3)
 
-        nc.vector.tensor_copy(out=des[0][:], in_=xs[0][:])
-        nc.scalar.copy(out=des[1][:], in_=xs[1][:])
-        nc.scalar.copy(out=des[2][:], in_=xs[2][:])
-        scatter_vector(0)
-        scatter_scalar(1)
-        nc.scalar.copy(out=des[3][:], in_=xs[3][:])
-        scatter_vector(2)
-        scatter_scalar(3)
-        on_vector = [0, 1]
+        pieces = [(0, 512, "vector"), (512, 512, "vector"), (1024, 256, "vector"), (1280, 256, "scalar"), (1536, 512, "scalar")]
+        pairs = [sb.tile([P, 2, width, 2], BF16, name="pairs%d" % c, align_bytes=64)
+                 for c, (first, width, engine) in enumerate(pieces)]
+        on_gpsimd = [2, 3, 4]
         for j in range(2):
-            for c in range(CH):
-                if c not in on_vector:
-                    nc.gpsimd.tensor_scalar(out=pairs[c][:, 0, :, j], in0=windows[j][:, c * CW:(c + 1) * CW],
-                                            scalar1=1.0, scalar2=0.0, op0=ALU.mult, op1=ALU.add)
+            for c in on_gpsimd:
+                first, width, engine = pieces[c]
+                nc.gpsimd.tensor_scalar(out=pairs[c][:, 0, :, j], in0=windows[j][:, first:first + width],
+                                        scalar1=1.0, scalar2=0.0, op0=ALU.mult, op1=ALU.add)
         words_out = out_1[0].rearrange("p c l -> p (c l)").bitcast(I32)
-        ys = [sb.tile([P, CW * L], BF16, name="y%d" % c, align_bytes=64) for c in range(CH)]
+        ys = [sb.tile([P, CW * L], BF16, name="y%d" % c, tag="plane_then_y%d" % c, align_bytes=64) for c in range(CH)]
 
-        def pair_words(c, dtype):
-            return pairs[c][:].rearrange("p u n e -> p (u n e)").bitcast(dtype).rearrange("p (u n) -> p n u", u=2)
+        def weave(copy, c, dtype):
+            first, width, engine = pieces[c]
+            y_words = ys[first // CW][:].bitcast(dtype).rearrange("p (n u) -> p n u", u=2)
+            copy(out=y_words[:, first % CW:first % CW + width, :],
+                 in_=pairs[c][:].rearrange("p u n e -> p (u n e)").bitcast(dtype).rearrange("p (u n) -> p n u", u=2))
 
         for j in range(L):
-            for c in on_vector:
-                nc.vector.tensor_copy(out=pairs[c][:, j // 2, :, j % 2], in_=windows[j][:, c * CW:(c + 1) * CW])
-        for c in range(CH):
-            if c in on_vector:
-                nc.vector.tensor_copy(out=ys[c][:].bitcast(I32).rearrange("p (n u) -> p n u", u=2), in_=pair_words(c, I32))
+            for c, (first, width, engine) in enumerate(pieces):
+                if engine == "vector" and (j >= 2 or c not in on_gpsimd):
+                    nc.vector.tensor_copy(out=pairs[c][:, j // 2, :, j % 2], in_=windows[j][:, first:first + width])
+        for c, (first, width, engine) in enumerate(pieces):
+            if engine == "vector":
+                weave(nc.vector.tensor_copy, c, I32)
             else:
                 for j in range(2, L):
-                    nc.scalar.copy(out=pairs[c][:, 1, :, j % 2], in_=windows[j][:, c * CW:(c + 1) * CW])
-                nc.scalar.copy(out=ys[c][:].bitcast(U32).rearrange("p (n u) -> p n u", u=2), in_=pair_words(c, U32))
+                    nc.scalar.copy(out=pairs[c][:, 1, :, j % 2], in_=windows[j][:, first:first + width])
+                weave(nc.scalar.copy, c, U32)
 
-        y_scales = sb.tile([P, T], U8, name="y_scales", align_bytes=64)
+        y_scales = sb.tile([P, CW], U8, name="y_scales", align_bytes=64)
         for c in range(CH):
             cols = slice(c * CW, (c + 1) * CW)
             codes = sb.tile([P, CW], U32, name="y_codes%d" % c, align_bytes=64)
-            nc.vector.quantize_mx(out=codes[:].bitcast(E4), scales=y_scales[:, cols], in_=ys[c][:])
+            nc.vector.quantize_mx(out=codes[:].bitcast(E4), scales=y_scales[4 * c:P, :], in_=ys[c][:])
             nc.sync.dma_start(out=words_out[:, cols], in_=codes[:].bitcast(I32))
-        for q, queue in enumerate([nc.scalar, nc.scalar, nc.sync, nc.sync]):
-            queue.dma_start(out=out_2[0, 4 * q:4 * q + 4, :].bitcast(I32),
-                            in_=y_scales[32 * q:32 * q + 4, :].bitcast(I32))
+        for q, queue in enumerate([nc.sync, nc.sync, nc.sync, nc.sync]):
+            queue.dma_start(out=out_2[0, 4 * q:4 * q + 4, :].bitcast(I32).rearrange("r (c x) -> c r x", c=CH),
+                            in_=y_scales[32 * q:32 * q + 16, :].bitcast(I32))

@@ -82,7 +82,7 @@ def tile_attend_ggate_E_pl_kernel(tc, eT, w1, w2, dy, c1, c2, ts, offs, out_0, o
         nc.scalar.activation(out=warm[:], in_=ident[:, 0:1], func=ACT.Sigmoid)
 
         windows = [sb.tile([P, T], F32, name="window%d" % j) for j in range(L)]
-        for j, engine in enumerate([nc.vector, nc.gpsimd, nc.vector, nc.gpsimd]):
+        for j, engine in enumerate([nc.vector, nc.vector, nc.vector, nc.vector]):
             engine.memset(windows[j][:].bitcast(I32), 0)
 
         ts_all = sb.tile([P, T], F32, name="ts_all")

@@ -51,15 +51,20 @@ def tile_attend_ggate_E_pl_kernel(tc, eT, w1, w2, dy, c1, c2, ts, offs, out_0, o
         def half(h):
             return slice(h * H, (h + 1) * H)
 
-        ts_row = sb.tile([P, T // P], F32, name="ts_row")
-        nc.sync.dma_start(out=ts_row[:], in_=ts[0:1, :].rearrange("o (p m) -> (o p) m", p=P))
+        warm_in = sb.tile([P, 1], F32, name="warm_in")
+        nc.vector.memset(warm_in[:], 0.0)
+        warm = sb.tile([P, 1], F32, name="warm")
+        nc.scalar.activation(out=warm[:], in_=warm_in[:], func=ACT.Sigmoid)
         offsets = sb.tile([P, N // 16], U16, name="offsets")
         nc.sync.dma_start(offsets[:], offs)
         w2_raw = sb.tile([P, L, K], F32, name="w2_raw")
         nc.sync.dma_start(out=w2_raw[:], in_=w2.rearrange("(p j) f -> p j f", j=L))
+        ts_all = sb.tile([P, T], F32, name="ts_all")
+        nc.vector.memset(ts_all[:].bitcast(I32), 0)
+        nc.sync.dma_start(out=ts_all[0:1, :], in_=ts[0:1, :])
         w1_raw = sb.tile([P, L, K], F32, name="w1_raw")
         nc.sync.dma_start(out=w1_raw[:], in_=w1.rearrange("(p j) f -> p j f", j=L))
-        dy_sb = sb.tile([P, L, N], F32, name="dy_sb")
+        dy_sb = sb.tile([P, L, N], F32, name="dy_sb", tag="dy_then_window", align_bytes=64)
         nc.sync.dma_start(out=dy_sb[:], in_=dy.rearrange("(p t) n -> p t n", t=L))
         c2_sb = sb.tile([P, L], F32, name="c2_sb")
         nc.scalar.dma_start(out=c2_sb[:], in_=c2.rearrange("(p t) o -> p (t o)", t=L))
@@ -78,34 +83,32 @@ def tile_attend_ggate_E_pl_kernel(tc, eT, w1, w2, dy, c1, c2, ts, offs, out_0, o
         ident = sb.tile([P, P], F32, name="ident")
         make_identity(nc, ident[:])
 
-        warm = sb.tile([P, 1], F32, name="warm")
-        nc.scalar.activation(out=warm[:], in_=ident[:, 0:1], func=ACT.Sigmoid)
 
-        windows = [sb.tile([P, T], F32, name="window%d" % j) for j in range(L)]
-        for j, engine in enumerate([nc.vector, nc.vector, nc.vector, nc.vector]):
-            engine.memset(windows[j][:].bitcast(I32), 0)
+        windows = {}
 
-        ts_all = sb.tile([P, T], F32, name="ts_all")
-        ts_view = ts_all[:].rearrange("q (p m) -> q p m", p=P)
-        for g in range(4):
-            bk = bank(g, "ts_bank%d" % g)
-            for r in range(4):
-                m = 4 * g + r
-                nc.tensor.transpose(bk[:, r * P:(r + 1) * P], ts_row[:, m:m + 1].to_broadcast([P, P]), ident[:])
-            nc.scalar.copy(out=ts_view[:, :, 4 * g:4 * g + 4], in_=bk[:].rearrange("q (r p) -> q p r", r=4))
-        ts_slot = sb.tile([P, N], F32, name="ts_slot")
-        nc.scalar.activation(out=ts_slot[:], in_=ts_all[:].indirect(offsets[:]), func=ACT.Copy)
+        def clear(j, tag):
+            windows[j] = sb.tile([P, T], F32, name="window%d" % j, tag=tag, align_bytes=64)
+            nc.gpsimd.memset(windows[j][:].bitcast(I32), 0)
+
+        clear(0, "window0")
+        clear(1, "window1")
+
+        ts_picked = sb.tile([P, N], F32, name="ts_picked")
+        nc.scalar.activation(out=ts_picked[:], in_=ts_all[:].indirect(offsets[:]), func=ACT.Copy)
         ts_turn = bank(0, "ts_turn")
         for i in range(4):
-            nc.tensor.transpose(ts_turn[:, block(i)], ts_slot[:, block(i)], ident[:])
+            nc.tensor.transpose(ts_turn[:, block(i)], ts_picked[:, block(i)], ident[:])
         ts_col = sb.tile([P, 4], F32, name="ts_col")
         nc.scalar.copy(out=ts_col[:], in_=ts_turn[:].rearrange("p (i q) -> p i q", i=4)[:, :, 0])
+        ts_slot = bank(1, "ts_slot")
+        for i in range(4):
+            nc.tensor.transpose(ts_slot[:, block(i)], ts_col[:, i:i + 1].to_broadcast([P, P]), ident[:])
 
         def flat(x):
             return x[:].rearrange("p a b c -> p (a b c)")
 
         def weights(raw, name, first_bank):
-            wd = sb.tile([P, L, P, L], BF16, name=name + "_d", align_bytes=64)
+            wd = sb.tile([P, L, P, L], BF16, name=name + "_d", tag=name + "_d", align_bytes=64)
             nc.vector.tensor_copy(out=wd[:].rearrange("p t m j -> p m j t"),
                                   in_=raw[:].rearrange("p j (m t) -> p m j t", t=L))
             wd_q = quantise(flat(wd), E4, name + "d", K)
@@ -129,10 +132,12 @@ def tile_attend_ggate_E_pl_kernel(tc, eT, w1, w2, dy, c1, c2, ts, offs, out_0, o
         for t in range(L):
             nc.vector.scalar_tensor_tensor(out=for_da[:, t, :], in0=dy_sb[:, t, :], scalar=c1_sb[:, t:t + 1],
                                            in1=ts_slot[:], op0=ALU.mult, op1=ALU.mult)
-        w2f_q = quantise(flat(w2_f), E4, "w2f", K)
         for t in range(L):
             nc.vector.scalar_tensor_tensor(out=for_db[:, t, :], in0=for_da[:, t, :], scalar=c2_neg[:, t:t + 1],
                                            in1=ts_slot[:], op0=ALU.mult, op1=ALU.mult)
+        clear(2, "w1_d")
+        clear(3, "dy_then_window")
+        w2f_q = quantise(flat(w2_f), E4, "w2f", K)
         w1f_q = quantise(flat(w1_f), E4, "w1f", K)
 
         e_low = sb.tile([P, 2, N], BF16, name="e_low")
@@ -172,16 +177,15 @@ def tile_attend_ggate_E_pl_kernel(tc, eT, w1, w2, dy, c1, c2, ts, offs, out_0, o
                                     in0=planar(bk[:].rearrange("p (t n) -> p t n", t=L)),
                                     in1=planar(for_db[:, :, block(i)]), op=ALU.mult)
 
-        def gate(h, first_bank):
-            for u in range(2):
-                bk = bank(first_bank + u, "b_back%d_%d" % (h, u))
-                for i in range(2):
-                    for t in range(2):
-                        nc.tensor.transpose(bk[:, t * H + i * P:t * H + (i + 1) * P],
-                                            b_ts[2 * h + i][:, block(2 * u + t)], ident[:])
+        def gate(h, u, bank_nr):
+            bk = bank(bank_nr, "b_back%d_%d" % (h, u))
+            for i in range(2):
                 for t in range(2):
-                    nc.scalar.activation(out=s[h][:, 2 * u + t, :], in_=bk[:, half(t)], func=ACT.Sigmoid,
-                                         scale=c2_sb[:, 2 * u + t:2 * u + t + 1])
+                    nc.tensor.transpose(bk[:, t * H + i * P:t * H + (i + 1) * P],
+                                        b_ts[2 * h + i][:, block(2 * u + t)], ident[:])
+            for t in range(2):
+                nc.scalar.activation(out=s[h][:, 2 * u + t, :], in_=bk[:, half(t)], func=ACT.Sigmoid,
+                                     scale=c2_sb[:, 2 * u + t:2 * u + t + 1])
 
         def square(h):
             nc.scalar.activation(out=woven(sq[h][:]), in_=planar(s[h][:]), func=ACT.Square, bias=-0.5)
@@ -202,12 +206,14 @@ def tile_attend_ggate_E_pl_kernel(tc, eT, w1, w2, dy, c1, c2, ts, offs, out_0, o
         times_a(0, 4)
         times_a(1, 5)
         turned_b(2)
-        gate(0, 6)
+        gate(0, 0, 6)
+        gate(0, 1, 7)
         turned_b(3)
         square(0)
         times_a(2, 4)
         times_a(3, 5)
-        gate(1, 0)
+        gate(1, 0, 0)
+        gate(1, 1, 1)
         square(1)
 
         out_rows = out_0.rearrange("(p j) c -> p j c", j=L)

@@ -173,9 +173,9 @@ def tile_attend_ggate_E_pl_kernel(tc, eT, w1, w2, dy, c1, c2, ts, offs, out_0, o
             bk = bank(bank_nr, "a%d" % i)
             for t in range(L):
                 product(bk[:, block(t)], w1d_q, block(t), e_q[i // 2], block(i % 2), E4, True, True)
-            nc.vector.tensor_tensor(out=woven(ga[i // 2][:, block(i % 2), :]),
-                                    in0=planar(bk[:].rearrange("p (t n) -> p t n", t=L)),
-                                    in1=planar(for_db[:, :, block(i)]), op=ALU.mult)
+            nc.vector.tensor_tensor(out=ga[i // 2][:, block(i % 2), :],
+                                    in0=bk[:].rearrange("p (t n) -> p n t", t=L),
+                                    in1=for_db[:, :, block(i)].rearrange("p t n -> p n t"), op=ALU.mult)
 
         def gate(h, u, bank_nr):
             bk = bank(bank_nr, "b_back%d_%d" % (h, u))
@@ -188,7 +188,7 @@ def tile_attend_ggate_E_pl_kernel(tc, eT, w1, w2, dy, c1, c2, ts, offs, out_0, o
                                      scale=c2_sb[:, 2 * u + t:2 * u + t + 1])
 
         def square(h):
-            nc.scalar.activation(out=woven(sq[h][:]), in_=planar(s[h][:]), func=ACT.Square, bias=-0.5)
+            nc.scalar.activation(out=sq[h][:], in_=s[h][:].rearrange("p t n -> p n t"), func=ACT.Square, bias=-0.5)
 
         def gradient_a(h):
             da_w = sb.tile([P, H, L], BF16, name="da_w%d" % h, align_bytes=64)

@@ -161,7 +161,7 @@ def tile_attend_ggate_E_pl_kernel(tc, eT, w1, w2, dy, c1, c2, ts, offs, out_0, o
 
         b_ts = [sb.tile([P, K], F32, name="b_ts%d" % i) for i in range(4)]
         s = [sb.tile([P, L, H], F32, name="s%d" % h) for h in range(2)]
-        sq = [sb.tile([P, H, L], F32, name="sq%d" % h) for h in range(2)]
+        sq = [sb.tile([P, H, L], F32, name="sq%d" % h, tag="sq%d" % h) for h in range(2)]
         ga = [sb.tile([P, H, L], F32, name="ga%d" % h) for h in range(2)]
 
         def turned_b(i):
@@ -223,12 +223,13 @@ def tile_attend_ggate_E_pl_kernel(tc, eT, w1, w2, dy, c1, c2, ts, offs, out_0, o
             product(out, w2f_q, block(j), grads[1], slice(0, H), E5, False, True)
 
         grads = (gradient_a(0), gradient_b(0))
-        de_first = [sb.tile([P, 2, H], F32, name="de_first%d" % u) for u in range(2)]
-        for u in range(2):
-            bk = bank(2 + u, "x_first%d" % u)
+        x_first = {}
+        for u in (1, 0):
+            x_first[u] = bank(2 + u, "x_first%d" % u)
             for t in range(2):
-                result(bk[:, half(t)], 2 * u + t, grads)
-            nc.scalar.copy(out=de_first[u][:], in_=bk[:].rearrange("p (t n) -> p t n", t=2))
+                result(x_first[u][:, half(t)], 2 * u + t, grads)
+        first_early = sb.tile([P, 2, H], F32, name="first_early")
+        nc.scalar.copy(out=first_early[:], in_=x_first[1][:].rearrange("p (t n) -> p t n", t=2))
 
         def scatter_scalar(j, h, src):
             nc.scalar.activation(out=windows[j][:].indirect(offsets_of(h)), in_=src, func=ACT.Copy)
@@ -246,28 +247,28 @@ def tile_attend_ggate_E_pl_kernel(tc, eT, w1, w2, dy, c1, c2, ts, offs, out_0, o
         db_q = gradient_b(1)
         for j in range(L):
             product(xs[j][:, 0:H], w2f_q, block(j), db_q, slice(0, H), E5, False, True)
-        scatter_scalar(0, 0, de_first[0][:, 0, :])
+        first_late = sb.tile([P, 2, H], F32, name="first_late", tag="sq1")
+        nc.vector.tensor_copy(out=first_late[:], in_=x_first[0][:].rearrange("p (t n) -> p t n", t=2))
         de_second = [sb.tile([P, H], F32, name="de_second%d" % j) for j in range(L)]
-        nc.vector.tensor_copy(out=de_second[0][:], in_=xs[0][:, 0:H])
+        scatter_scalar(2, 0, first_early[:, 0, :])
+        for j in range(L):
+            nc.scalar.copy(out=de_second[j][:], in_=xs[j][:, 0:H])
+        scatter_vector(0, 0, first_late[:, 0, :])
         scatter_vector(0, 1, de_second[0][:])
         store(0)
-        scatter_scalar(1, 0, de_first[0][:, 1, :])
-        nc.scalar.copy(out=de_second[1][:], in_=xs[1][:, 0:H])
-        scatter_scalar(1, 1, de_second[1][:])
+        scatter_scalar(3, 0, first_early[:, 1, :])
+        scatter_vector(1, 1, de_second[1][:])
+        scatter_vector(1, 0, first_late[:, 1, :])
         store(1)
-        nc.vector.tensor_copy(out=de_second[2][:], in_=xs[2][:, 0:H])
-        scatter_vector(2, 1, de_second[2][:])
-        scatter_vector(2, 0, de_first[1][:, 0, :])
-        store(2)
-        nc.scalar.copy(out=de_second[3][:], in_=xs[3][:, 0:H])
-        scatter_scalar(3, 0, de_first[1][:, 1, :])
         scatter_scalar(3, 1, de_second[3][:])
+        scatter_vector(2, 1, de_second[2][:])
+        store(2)
         store(3)
 
-        pieces = [(0, 512, "vector"), (512, 512, "vector"), (1024, 256, "vector"), (1280, 256, "scalar"), (1536, 512, "scalar")]
+        pieces = [(0, 512, "vector"), (512, 512, "vector"), (1024, 512, "scalar"), (1536, 512, "scalar")]
         pairs = [sb.tile([P, 2, width, 2], BF16, name="pairs%d" % c, align_bytes=64)
                  for c, (first, width, engine) in enumerate(pieces)]
-        on_gpsimd = [2, 3, 4]
+        on_gpsimd = [2, 3]
         for j in range(2):
             for c in on_gpsimd:
                 first, width, engine = pieces[c]

@@ -141,17 +141,13 @@ def tile_attend_ggate_E_pl_kernel(tc, eT, w1, w2, dy, c1, c2, ts, offs, out_0, o
         w1f_q = quantise(flat(w1_f), E4, "w1f", K)
 
         e_low = sb.tile([P, 2, N], BF16, name="e_low")
-        e_slot = [sb.tile([P, H, L], BF16, name="e_slot%d" % h, align_bytes=64) for h in range(2)]
+        e_slot = sb.tile([P, N, L], BF16, name="e_slot", align_bytes=64)
         for j in range(2):
             nc.scalar.activation(out=e_low[:, j, :], in_=e_planes[j][:].indirect(offsets[:]), func=ACT.Copy)
-        for h in range(2):
-            nc.scalar.copy(out=e_slot[h][:, :, 0:2], in_=e_low[:, :, half(h)].rearrange("p j n -> p n j"))
-        for h in range(2):
-            nc.vector.tensor_copy(out=e_slot[h][:, :, 2], in_=e_planes[2][:].indirect(offsets_of(h)))
-        e_q = []
-        for h in range(2):
-            nc.vector.tensor_copy(out=e_slot[h][:, :, 3], in_=e_planes[3][:].indirect(offsets_of(h)))
-            e_q.append(quantise(e_slot[h][:].rearrange("p n j -> p (n j)"), E4, "e%d" % h, H))
+        nc.scalar.copy(out=e_slot[:, :, 0:2], in_=e_low[:].rearrange("p j n -> p n j"))
+        for j in range(2, L):
+            nc.vector.tensor_copy(out=e_slot[:, :, j], in_=e_planes[j][:].indirect(offsets[:]))
+        e_q = [quantise(e_slot[:, half(h), :].rearrange("p n j -> p (n j)"), E4, "e%d" % h, H) for h in range(2)]
 
         def woven(x):
             return x.rearrange("p (c i) t -> p c t i", i=2)
@@ -223,19 +219,18 @@ def tile_attend_ggate_E_pl_kernel(tc, eT, w1, w2, dy, c1, c2, ts, offs, out_0, o
             product(out, w2f_q, block(j), grads[1], slice(0, H), E5, False, True)
 
         grads = (gradient_a(0), gradient_b(0))
-        x_first = {}
-        for u in (1, 0):
-            x_first[u] = bank(2 + u, "x_first%d" % u)
+        de = [sb.tile([P, 2, N], F32, name="de%d" % u) for u in range(2)]
+        for u in range(2):
+            bk = bank(2 + u, "x_first%d" % u)
             for t in range(2):
-                result(x_first[u][:, half(t)], 2 * u + t, grads)
-        first_early = sb.tile([P, 2, H], F32, name="first_early")
-        nc.scalar.copy(out=first_early[:], in_=x_first[1][:].rearrange("p (t n) -> p t n", t=2))
+                result(bk[:, half(t)], 2 * t + u, grads)
+            nc.scalar.copy(out=de[u][:, :, half(0)], in_=bk[:].rearrange("p (t n) -> p t n", t=2))
 
-        def scatter_scalar(j, h, src):
-            nc.scalar.activation(out=windows[j][:].indirect(offsets_of(h)), in_=src, func=ACT.Copy)
+        def scatter_scalar(j, h):
+            nc.scalar.activation(out=windows[j][:].indirect(offsets_of(h)), in_=de[j % 2][:, j // 2, half(h)], func=ACT.Copy)
 
-        def scatter_vector(j, h, src):
-            nc.vector.tensor_copy(out=windows[j][:].indirect(offsets_of(h)), in_=src)
+        def scatter_vector(j):
+            nc.vector.tensor_copy(out=windows[j][:].indirect(offsets[:]), in_=de[j % 2][:, j // 2, :])
 
         def store(j):
             nc.sync.dma_start(out=out_rows[:, j, :], in_=windows[j][:])
@@ -247,28 +242,25 @@ def tile_attend_ggate_E_pl_kernel(tc, eT, w1, w2, dy, c1, c2, ts, offs, out_0, o
         db_q = gradient_b(1)
         for j in range(L):
             product(xs[j][:, 0:H], w2f_q, block(j), db_q, slice(0, H), E5, False, True)
-        first_late = sb.tile([P, 2, H], F32, name="first_late", tag="sq1")
-        nc.vector.tensor_copy(out=first_late[:], in_=x_first[0][:].rearrange("p (t n) -> p t n", t=2))
-        de_second = [sb.tile([P, H], F32, name="de_second%d" % j) for j in range(L)]
-        scatter_scalar(2, 0, first_early[:, 0, :])
-        for j in range(L):
-            nc.scalar.copy(out=de_second[j][:], in_=xs[j][:, 0:H])
-        scatter_vector(0, 0, first_late[:, 0, :])
-        scatter_vector(0, 1, de_second[0][:])
+        scatter_scalar(0, 0)
+        nc.scalar.copy(out=de[0][:, 0, half(1)], in_=xs[0][:, 0:H])
+        scatter_scalar(0, 1)
         store(0)
-        scatter_scalar(3, 0, first_early[:, 1, :])
-        scatter_vector(1, 1, de_second[1][:])
-        scatter_vector(1, 0, first_late[:, 1, :])
+        for j in (1, 3):
+            nc.vector.tensor_copy(out=de[1][:, j // 2, half(1)], in_=xs[j][:, 0:H])
+        scatter_vector(1)
         store(1)
-        scatter_scalar(3, 1, de_second[3][:])
-        scatter_vector(2, 1, de_second[2][:])
+        nc.scalar.copy(out=de[0][:, 1, half(1)], in_=xs[2][:, 0:H])
+        scatter_scalar(2, 1)
+        scatter_scalar(2, 0)
         store(2)
+        scatter_vector(3)
         store(3)
 
         pieces = [(0, 512, "vector"), (512, 512, "vector"), (1024, 512, "scalar"), (1536, 512, "scalar")]
         pairs = [sb.tile([P, 2, width, 2], BF16, name="pairs%d" % c, align_bytes=64)
                  for c, (first, width, engine) in enumerate(pieces)]
-        on_gpsimd = [2, 3]
+        on_gpsimd = [2, 3, 1]
         for j in range(2):
             for c in on_gpsimd:
                 first, width, engine = pieces[c]

@@ -30,6 +30,7 @@ def tile_attend_ggate_E_pl_kernel(tc, eT, w1, w2, dy, c1, c2, ts, offs, out_0, o
     nc = tc.nc
     with ExitStack() as ctx:
         sb = ctx.enter_context(tc.tile_pool(name="sb", bufs=1))
+        after_ts = ctx.enter_context(tc.tile_pool(name="after_ts", bufs=1))
         ps = ctx.enter_context(tc.psum_pool(name="ps", bufs=1))
 
         def bank(i, name):
@@ -51,21 +52,16 @@ def tile_attend_ggate_E_pl_kernel(tc, eT, w1, w2, dy, c1, c2, ts, offs, out_0, o
         def half(h):
             return slice(h * H, (h + 1) * H)
 
-        warm_in = sb.tile([P, 1], F32, name="warm_in")
-        nc.vector.memset(warm_in[:], 0.0)
-        warm = sb.tile([P, 1], F32, name="warm")
-        nc.scalar.activation(out=warm[:], in_=warm_in[:], func=ACT.Sigmoid)
+        ts_row = sb.tile([P, T // P], F32, name="ts_row")
+        nc.sync.dma_start(out=ts_row[:], in_=ts[0:1, :].rearrange("o (p m) -> (o p) m", p=P))
         offsets = sb.tile([P, N // 16], U16, name="offsets")
         nc.sync.dma_start(offsets[:], offs)
         w2_raw = sb.tile([P, L, K], F32, name="w2_raw")
         nc.sync.dma_start(out=w2_raw[:], in_=w2.rearrange("(p j) f -> p j f", j=L))
-        ts_all = sb.tile([P, T], F32, name="ts_all")
-        nc.vector.memset(ts_all[:].bitcast(I32), 0)
-        nc.sync.dma_start(out=ts_all[0:1, :], in_=ts[0:1, :])
-        w1_raw = sb.tile([P, L, K], F32, name="w1_raw")
-        nc.sync.dma_start(out=w1_raw[:], in_=w1.rearrange("(p j) f -> p j f", j=L))
         dy_sb = sb.tile([P, L, N], F32, name="dy_sb", tag="dy_then_window", align_bytes=64)
         nc.sync.dma_start(out=dy_sb[:], in_=dy.rearrange("(p t) n -> p t n", t=L))
+        w1_raw = sb.tile([P, L, K], F32, name="w1_raw")
+        nc.sync.dma_start(out=w1_raw[:], in_=w1.rearrange("(p j) f -> p j f", j=L))
         c2_sb = sb.tile([P, L], F32, name="c2_sb")
         nc.scalar.dma_start(out=c2_sb[:], in_=c2.rearrange("(p t) o -> p (t o)", t=L))
         c1_sb = sb.tile([P, L], F32, name="c1_sb")
@@ -93,26 +89,25 @@ def tile_attend_ggate_E_pl_kernel(tc, eT, w1, w2, dy, c1, c2, ts, offs, out_0, o
         clear(0, "window0")
         clear(1, "window1")
 
-        ts_picked = sb.tile([P, N], F32, name="ts_picked")
-        nc.scalar.activation(out=ts_picked[:], in_=ts_all[:].indirect(offsets[:]), func=ACT.Copy)
-        ts_turn = bank(0, "ts_turn")
-        for i in range(4):
-            nc.tensor.transpose(ts_turn[:, block(i)], ts_picked[:, block(i)], ident[:])
-        ts_col = sb.tile([P, 4], F32, name="ts_col")
-        nc.scalar.copy(out=ts_col[:], in_=ts_turn[:].rearrange("p (i q) -> p i q", i=4)[:, :, 0])
-        ts_slot = bank(1, "ts_slot")
-        for i in range(4):
-            nc.tensor.transpose(ts_slot[:, block(i)], ts_col[:, i:i + 1].to_broadcast([P, P]), ident[:])
+        ts_all = after_ts.tile([P, T], F32, name="ts_all", offset=0, align_bytes=64)
+        ts_view = ts_all[:].rearrange("q (p m) -> q p m", p=P)
+        for g in range(4):
+            bk = bank(g, "ts_bank%d" % g)
+            for r in range(4):
+                m = 4 * g + r
+                nc.tensor.transpose(bk[:, r * P:(r + 1) * P], ts_row[:, m:m + 1].to_broadcast([P, P]), ident[:])
+            nc.scalar.copy(out=ts_view[:, :, 4 * g:4 * g + 4], in_=bk[:].rearrange("q (r p) -> q p r", r=4))
+        ts_slot = sb.tile([P, N], F32, name="ts_slot")
+        nc.scalar.activation(out=ts_slot[:], in_=ts_all[:].indirect(offsets[:]), func=ACT.Copy)
 
         def flat(x):
             return x[:].rearrange("p a b c -> p (a b c)")
 
-        def weights(raw, name, first_bank):
-            wd = sb.tile([P, L, P, L], BF16, name=name + "_d", tag=name + "_d", align_bytes=64)
-            nc.vector.tensor_copy(out=wd[:].rearrange("p t m j -> p m j t"),
-                                  in_=raw[:].rearrange("p j (m t) -> p m j t", t=L))
+        def weights(raw, name, wd, wf, first_bank, copy, step):
+            for t in range(0, L, step):
+                copy(out=wd[:].rearrange("p t m j -> p m j t")[:, :, :, t:t + step],
+                     in_=raw[:].rearrange("p j (m t) -> p m j t", t=L)[:, :, :, t:t + step])
             wd_q = quantise(flat(wd), E4, name + "d", K)
-            wf = sb.tile([P, L, P, L], BF16, name=name + "_f", align_bytes=64)
             words = flat(wd).bitcast(F32).rearrange("p (t m v) -> p t m v", t=L, v=2)
             for v in range(2):
                 bk = bank(first_bank + v, "%s_turn%d" % (name, v))
@@ -120,12 +115,14 @@ def tile_attend_ggate_E_pl_kernel(tc, eT, w1, w2, dy, c1, c2, ts, offs, out_0, o
                     nc.tensor.transpose(bk[:, block(t)], words[:, t, :, v], ident[:])
                 nc.scalar.copy(out=wf[:, 2 * v:2 * v + 2, :, :],
                                in_=bk[:].bitcast(BF16).rearrange("m (t p e) -> m e p t", t=L, e=2))
-            return wd_q, wf
+            return wd_q
 
-        w2d_q, w2_f = weights(w2_raw, "w2", 4)
-        w1d_q, w1_f = weights(w1_raw, "w1", 6)
-
-        c2_neg = sb.tile([P, L], F32, name="c2_neg")
+        w2_d = sb.tile([P, L, P, L], BF16, name="w2_d", tag="w2_d", align_bytes=64)
+        w2_f = after_ts.tile([P, L, P, L], BF16, name="w2_f", offset=0, align_bytes=64)
+        w1_d = after_ts.tile([P, L, P, L], BF16, name="w1_d", offset=4096, align_bytes=64)
+        w1_f = sb.tile([P, L, P, L], BF16, name="w1_f", align_bytes=64)
+        w2d_q = weights(w2_raw, "w2", w2_d, w2_f, 4, nc.vector.tensor_copy, 4)
+        c2_neg = sb.tile([P, L], F32, name="c2_neg", tag="c2_then_e", align_bytes=64)
         nc.vector.tensor_scalar(out=c2_neg[:], in0=c2_sb[:], scalar1=-1.0, scalar2=None, op0=ALU.mult)
         for_da = sb.tile([P, L, N], F32, name="for_da")
         for_db = sb.tile([P, L, N], F32, name="for_db")
@@ -135,19 +132,21 @@ def tile_attend_ggate_E_pl_kernel(tc, eT, w1, w2, dy, c1, c2, ts, offs, out_0, o
         for t in range(L):
             nc.vector.scalar_tensor_tensor(out=for_db[:, t, :], in0=for_da[:, t, :], scalar=c2_neg[:, t:t + 1],
                                            in1=ts_slot[:], op0=ALU.mult, op1=ALU.mult)
-        clear(2, "w1_d")
+
+        w1d_q = weights(w1_raw, "w1", w1_d, w1_f, 6, nc.scalar.copy, 2)
+
+        clear(2, "w2_d")
         clear(3, "dy_then_window")
+
+        e_slot = sb.tile([P, N, L], BF16, name="e_slot", tag="c2_then_e", align_bytes=64)
+        for j in range(L - 1):
+            nc.vector.tensor_copy(out=e_slot[:, :, j], in_=e_planes[j][:].indirect(offsets[:]))
         w2f_q = quantise(flat(w2_f), E4, "w2f", K)
         w1f_q = quantise(flat(w1_f), E4, "w1f", K)
-
-        e_low = sb.tile([P, 2, N], BF16, name="e_low")
-        e_slot = sb.tile([P, N, L], BF16, name="e_slot", align_bytes=64)
-        for j in range(2):
-            nc.scalar.activation(out=e_low[:, j, :], in_=e_planes[j][:].indirect(offsets[:]), func=ACT.Copy)
-        nc.scalar.copy(out=e_slot[:, :, 0:2], in_=e_low[:].rearrange("p j n -> p n j"))
-        for j in range(2, L):
-            nc.vector.tensor_copy(out=e_slot[:, :, j], in_=e_planes[j][:].indirect(offsets[:]))
-        e_q = [quantise(e_slot[:, half(h), :].rearrange("p n j -> p (n j)"), E4, "e%d" % h, H) for h in range(2)]
+        e_q = []
+        for h in range(2):
+            nc.vector.tensor_copy(out=e_slot[:, half(h), L - 1], in_=e_planes[L - 1][:].indirect(offsets_of(h)))
+            e_q.append(quantise(e_slot[:, half(h), :].rearrange("p n j -> p (n j)"), E4, "e%d" % h, H))
 
         def woven(x):
             return x.rearrange("p (c i) t -> p c t i", i=2)
@@ -155,15 +154,22 @@ def tile_attend_ggate_E_pl_kernel(tc, eT, w1, w2, dy, c1, c2, ts, offs, out_0, o
         def planar(x):
             return x.rearrange("p t (c i) -> p c t i", i=2)
 
-        b_ts = [sb.tile([P, K], F32, name="b_ts%d" % i) for i in range(4)]
+        u = [sb.tile([P, L, H], F32, name="u%d" % h) for h in range(2)]
         s = [sb.tile([P, L, H], F32, name="s%d" % h) for h in range(2)]
         sq = [sb.tile([P, H, L], F32, name="sq%d" % h, tag="sq%d" % h) for h in range(2)]
         ga = [sb.tile([P, H, L], F32, name="ga%d" % h) for h in range(2)]
 
-        def turned_b(i):
-            bk = bank(i, "b_turned%d" % i)
-            product(bk[:], e_q[i // 2], block(i % 2), w2d_q, slice(0, K), E4, True, True)
-            nc.scalar.activation(out=b_ts[i][:], in_=bk[:], func=ACT.Copy, scale=ts_col[:, i:i + 1])
+        def gate(h):
+            for v in range(2):
+                bk = bank(2 * h + v, "b%d_%d" % (h, v))
+                for t in range(2):
+                    product(bk[:, half(t)], w2d_q, block(2 * v + t), e_q[h], slice(0, H), E4, True, True)
+                for t in range(2):
+                    nc.vector.scalar_tensor_tensor(out=u[h][:, 2 * v + t, :], in0=bk[:, half(t)],
+                                                   scalar=c2_sb[:, 2 * v + t:2 * v + t + 1], in1=ts_slot[:, half(h)],
+                                                   op0=ALU.mult, op1=ALU.mult)
+            nc.scalar.activation(out=s[h][:], in_=u[h][:], func=ACT.Sigmoid)
+            nc.scalar.activation(out=sq[h][:], in_=s[h][:].rearrange("p t n -> p n t"), func=ACT.Square, bias=-0.5)
 
         def times_a(i, bank_nr):
             bk = bank(bank_nr, "a%d" % i)
@@ -172,19 +178,6 @@ def tile_attend_ggate_E_pl_kernel(tc, eT, w1, w2, dy, c1, c2, ts, offs, out_0, o
             nc.vector.tensor_tensor(out=ga[i // 2][:, block(i % 2), :],
                                     in0=bk[:].rearrange("p (t n) -> p n t", t=L),
                                     in1=for_db[:, :, block(i)].rearrange("p t n -> p n t"), op=ALU.mult)
-
-        def gate(h, u, bank_nr):
-            bk = bank(bank_nr, "b_back%d_%d" % (h, u))
-            for i in range(2):
-                for t in range(2):
-                    nc.tensor.transpose(bk[:, t * H + i * P:t * H + (i + 1) * P],
-                                        b_ts[2 * h + i][:, block(2 * u + t)], ident[:])
-            for t in range(2):
-                nc.scalar.activation(out=s[h][:, 2 * u + t, :], in_=bk[:, half(t)], func=ACT.Sigmoid,
-                                     scale=c2_sb[:, 2 * u + t:2 * u + t + 1])
-
-        def square(h):
-            nc.scalar.activation(out=sq[h][:], in_=s[h][:].rearrange("p t n -> p n t"), func=ACT.Square, bias=-0.5)
 
         def gradient_a(h):
             da_w = sb.tile([P, H, L], BF16, name="da_w%d" % h, align_bytes=64)
@@ -197,20 +190,10 @@ def tile_attend_ggate_E_pl_kernel(tc, eT, w1, w2, dy, c1, c2, ts, offs, out_0, o
                                            op0=ALU.subtract, op1=ALU.mult)
             return quantise(db_w[:].rearrange("p n t -> p (n t)"), E5, "db%d" % h, H)
 
-        turned_b(0)
-        turned_b(1)
+        gate(0)
+        gate(1)
         times_a(0, 4)
         times_a(1, 5)
-        turned_b(2)
-        gate(0, 0, 6)
-        gate(0, 1, 7)
-        turned_b(3)
-        square(0)
-        times_a(2, 4)
-        times_a(3, 5)
-        gate(1, 0, 0)
-        gate(1, 1, 1)
-        square(1)
 
         out_rows = out_0.rearrange("(p j) c -> p j c", j=L)
 
@@ -219,18 +202,20 @@ def tile_attend_ggate_E_pl_kernel(tc, eT, w1, w2, dy, c1, c2, ts, offs, out_0, o
             product(out, w2f_q, block(j), grads[1], slice(0, H), E5, False, True)
 
         grads = (gradient_a(0), gradient_b(0))
-        de = [sb.tile([P, 2, N], F32, name="de%d" % u) for u in range(2)]
+        times_a(2, 4)
+        times_a(3, 5)
+        de_first = [sb.tile([P, 2, H], F32, name="de_first%d" % u) for u in range(2)]
         for u in range(2):
             bk = bank(2 + u, "x_first%d" % u)
             for t in range(2):
-                result(bk[:, half(t)], 2 * t + u, grads)
-            nc.scalar.copy(out=de[u][:, :, half(0)], in_=bk[:].rearrange("p (t n) -> p t n", t=2))
+                result(bk[:, half(t)], 2 * u + t, grads)
+            nc.scalar.copy(out=de_first[u][:], in_=bk[:].rearrange("p (t n) -> p t n", t=2))
 
-        def scatter_scalar(j, h):
-            nc.scalar.activation(out=windows[j][:].indirect(offsets_of(h)), in_=de[j % 2][:, j // 2, half(h)], func=ACT.Copy)
+        def scatter_scalar(j, h, src):
+            nc.scalar.activation(out=windows[j][:].indirect(offsets_of(h)), in_=src, func=ACT.Copy)
 
-        def scatter_vector(j):
-            nc.vector.tensor_copy(out=windows[j][:].indirect(offsets[:]), in_=de[j % 2][:, j // 2, :])
+        def scatter_vector(j, h, src):
+            nc.vector.tensor_copy(out=windows[j][:].indirect(offsets_of(h)), in_=src)
 
         def store(j):
             nc.sync.dma_start(out=out_rows[:, j, :], in_=windows[j][:])
@@ -242,50 +227,38 @@ def tile_attend_ggate_E_pl_kernel(tc, eT, w1, w2, dy, c1, c2, ts, offs, out_0, o
         db_q = gradient_b(1)
         for j in range(L):
             product(xs[j][:, 0:H], w2f_q, block(j), db_q, slice(0, H), E5, False, True)
-        scatter_scalar(0, 0)
-        nc.scalar.copy(out=de[0][:, 0, half(1)], in_=xs[0][:, 0:H])
-        scatter_scalar(0, 1)
+        scatter_scalar(0, 0, de_first[0][:, 0, :])
+        scatter_scalar(1, 0, de_first[0][:, 1, :])
+        de_second = [sb.tile([P, H], F32, name="de_second%d" % j) for j in range(L)]
+        nc.vector.tensor_copy(out=de_second[0][:], in_=xs[0][:, 0:H])
+        scatter_vector(0, 1, de_second[0][:])
         store(0)
-        for j in (1, 3):
-            nc.vector.tensor_copy(out=de[1][:, j // 2, half(1)], in_=xs[j][:, 0:H])
-        scatter_vector(1)
+        nc.scalar.copy(out=de_second[1][:], in_=xs[1][:, 0:H])
+        scatter_scalar(1, 1, de_second[1][:])
         store(1)
-        nc.scalar.copy(out=de[0][:, 1, half(1)], in_=xs[2][:, 0:H])
-        scatter_scalar(2, 1)
-        scatter_scalar(2, 0)
+        nc.vector.tensor_copy(out=de_second[2][:], in_=xs[2][:, 0:H])
+        scatter_vector(2, 1, de_second[2][:])
+        scatter_vector(2, 0, de_first[1][:, 0, :])
         store(2)
-        scatter_vector(3)
+        nc.scalar.copy(out=de_second[3][:], in_=xs[3][:, 0:H])
+        scatter_scalar(3, 0, de_first[1][:, 1, :])
+        scatter_scalar(3, 1, de_second[3][:])
         store(3)
 
-        pieces = [(0, 512, "vector"), (512, 512, "vector"), (1024, 512, "scalar"), (1536, 512, "scalar")]
-        pairs = [sb.tile([P, 2, width, 2], BF16, name="pairs%d" % c, align_bytes=64)
-                 for c, (first, width, engine) in enumerate(pieces)]
-        on_gpsimd = [2, 3, 1]
-        for j in range(2):
-            for c in on_gpsimd:
-                first, width, engine = pieces[c]
-                nc.gpsimd.tensor_scalar(out=pairs[c][:, 0, :, j], in0=windows[j][:, first:first + width],
-                                        scalar1=1.0, scalar2=0.0, op0=ALU.mult, op1=ALU.add)
+        split = 11 * T // 16
         words_out = out_1[0].rearrange("p c l -> p (c l)").bitcast(I32)
         ys = [sb.tile([P, CW * L], BF16, name="y%d" % c, tag="plane_then_y%d" % c, align_bytes=64) for c in range(CH)]
-
-        def weave(copy, c, dtype):
-            first, width, engine = pieces[c]
-            y_words = ys[first // CW][:].bitcast(dtype).rearrange("p (n u) -> p n u", u=2)
-            copy(out=y_words[:, first % CW:first % CW + width, :],
-                 in_=pairs[c][:].rearrange("p u n e -> p (u n e)").bitcast(dtype).rearrange("p (u n) -> p n u", u=2))
-
-        for j in range(L):
-            for c, (first, width, engine) in enumerate(pieces):
-                if engine == "vector" and (j >= 2 or c not in on_gpsimd):
-                    nc.vector.tensor_copy(out=pairs[c][:, j // 2, :, j % 2], in_=windows[j][:, first:first + width])
-        for c, (first, width, engine) in enumerate(pieces):
-            if engine == "vector":
-                weave(nc.vector.tensor_copy, c, I32)
-            else:
-                for j in range(2, L):
-                    nc.scalar.copy(out=pairs[c][:, 1, :, j % 2], in_=windows[j][:, first:first + width])
-                weave(nc.scalar.copy, c, U32)
+        for name, copy, dtype, first, last in (("vector", nc.vector.tensor_copy, I32, 0, split),
+                                               ("scalar", nc.scalar.copy, U32, split, T)):
+            pairs = sb.tile([P, 2, last - first, 2], BF16, name="pairs_" + name, align_bytes=64)
+            for j in range(L):
+                copy(out=pairs[:, j // 2, :, j % 2], in_=windows[j][:, first:last])
+            pair_words = pairs[:].rearrange("p u n e -> p (u n e)").bitcast(dtype).rearrange("p (u n) -> p n u", u=2)
+            for c in range(CH):
+                lo, hi = max(first, c * CW), min(last, (c + 1) * CW)
+                if lo < hi:
+                    y_words = ys[c][:].bitcast(dtype).rearrange("p (n u) -> p n u", u=2)
+                    copy(out=y_words[:, lo - c * CW:hi - c * CW, :], in_=pair_words[:, lo - first:hi - first, :])
 
         y_scales = sb.tile([P, CW], U8, name="y_scales", align_bytes=64)
         for c in range(CH):

@@ -103,11 +103,13 @@ def tile_attend_ggate_E_pl_kernel(tc, eT, w1, w2, dy, c1, c2, ts, offs, out_0, o
         def flat(x):
             return x[:].rearrange("p a b c -> p (a b c)")
 
-        def weights(raw, name, wd, wf, first_bank, copy, step):
+        def along_d(raw, name, wd, copy, step):
             for t in range(0, L, step):
                 copy(out=wd[:].rearrange("p t m j -> p m j t")[:, :, :, t:t + step],
                      in_=raw[:].rearrange("p j (m t) -> p m j t", t=L)[:, :, :, t:t + step])
-            wd_q = quantise(flat(wd), E4, name + "d", K)
+            return quantise(flat(wd), E4, name + "d", K)
+
+        def along_f(wd, name, wf, first_bank):
             words = flat(wd).bitcast(F32).rearrange("p (t m v) -> p t m v", t=L, v=2)
             for v in range(2):
                 bk = bank(first_bank + v, "%s_turn%d" % (name, v))
@@ -115,34 +117,38 @@ def tile_attend_ggate_E_pl_kernel(tc, eT, w1, w2, dy, c1, c2, ts, offs, out_0, o
                     nc.tensor.transpose(bk[:, block(t)], words[:, t, :, v], ident[:])
                 nc.scalar.copy(out=wf[:, 2 * v:2 * v + 2, :, :],
                                in_=bk[:].bitcast(BF16).rearrange("m (t p e) -> m e p t", t=L, e=2))
-            return wd_q
 
         w2_d = sb.tile([P, L, P, L], BF16, name="w2_d", tag="w2_d", align_bytes=64)
         w2_f = after_ts.tile([P, L, P, L], BF16, name="w2_f", offset=0, align_bytes=64)
         w1_d = after_ts.tile([P, L, P, L], BF16, name="w1_d", offset=4096, align_bytes=64)
-        w1_f = sb.tile([P, L, P, L], BF16, name="w1_f", align_bytes=64)
-        w2d_q = weights(w2_raw, "w2", w2_d, w2_f, 4, nc.vector.tensor_copy, 4)
-        c2_neg = sb.tile([P, L], F32, name="c2_neg", tag="c2_then_e", align_bytes=64)
-        nc.vector.tensor_scalar(out=c2_neg[:], in0=c2_sb[:], scalar1=-1.0, scalar2=None, op0=ALU.mult)
+        w2d_q = along_d(w2_raw, "w2", w2_d, nc.vector.tensor_copy, 4)
+        along_f(w2_d, "w2", w2_f, 4)
+        c2_neg = [sb.tile([P, 2], F32, name="c2_neg%d" % v, tag="c2_then_e%d" % v, align_bytes=64) for v in range(2)]
+        for v in range(2):
+            nc.vector.tensor_scalar(out=c2_neg[v][:], in0=c2_sb[:, 2 * v:2 * v + 2], scalar1=-1.0, scalar2=None, op0=ALU.mult)
         for_da = sb.tile([P, L, N], F32, name="for_da")
         for_db = sb.tile([P, L, N], F32, name="for_db")
         for t in range(L):
             nc.vector.scalar_tensor_tensor(out=for_da[:, t, :], in0=dy_sb[:, t, :], scalar=c1_sb[:, t:t + 1],
                                            in1=ts_slot[:], op0=ALU.mult, op1=ALU.mult)
         for t in range(L):
-            nc.vector.scalar_tensor_tensor(out=for_db[:, t, :], in0=for_da[:, t, :], scalar=c2_neg[:, t:t + 1],
+            nc.vector.scalar_tensor_tensor(out=for_db[:, t, :], in0=for_da[:, t, :], scalar=c2_neg[t // 2][:, t % 2:t % 2 + 1],
                                            in1=ts_slot[:], op0=ALU.mult, op1=ALU.mult)
 
-        w1d_q = weights(w1_raw, "w1", w1_d, w1_f, 6, nc.scalar.copy, 2)
+        w1d_q = along_d(w1_raw, "w1", w1_d, nc.scalar.copy, 2)
 
         clear(2, "w2_d")
         clear(3, "dy_then_window")
 
-        e_slot = sb.tile([P, N, L], BF16, name="e_slot", tag="c2_then_e", align_bytes=64)
-        for j in range(L - 1):
-            nc.vector.tensor_copy(out=e_slot[:, :, j], in_=e_planes[j][:].indirect(offsets[:]))
+        e_slot = sb.tile([P, N, L], BF16, name="e_slot", tag="c2_then_e0", align_bytes=64)
+        e_low = sb.tile([P, 2, N], BF16, name="e_low", tag="c2_then_e1", align_bytes=64)
+        for j in range(2):
+            nc.vector.tensor_copy(out=e_low[:, j, :], in_=e_planes[j][:].indirect(offsets[:]))
+        nc.scalar.copy(out=e_slot[:, :, 0:2], in_=e_low[:].rearrange("p j n -> p n j"))
         w2f_q = quantise(flat(w2_f), E4, "w2f", K)
-        w1f_q = quantise(flat(w1_f), E4, "w1f", K)
+        nc.vector.tensor_copy(out=e_slot[:, :, 2], in_=e_planes[2][:].indirect(offsets[:]))
+        w1_f = sb.tile([P, L, P, L], BF16, name="w1_f", tag="c2_then_e1", align_bytes=64)
+        along_f(w1_d, "w1", w1_f, 6)
         e_q = []
         for h in range(2):
             nc.vector.tensor_copy(out=e_slot[:, half(h), L - 1], in_=e_planes[L - 1][:].indirect(offsets_of(h)))
@@ -169,15 +175,15 @@ def tile_attend_ggate_E_pl_kernel(tc, eT, w1, w2, dy, c1, c2, ts, offs, out_0, o
                                                    scalar=c2_sb[:, 2 * v + t:2 * v + t + 1], in1=ts_slot[:, half(h)],
                                                    op0=ALU.mult, op1=ALU.mult)
             nc.scalar.activation(out=s[h][:], in_=u[h][:], func=ACT.Sigmoid)
-            nc.scalar.activation(out=sq[h][:], in_=s[h][:].rearrange("p t n -> p n t"), func=ACT.Square, bias=-0.5)
+            nc.scalar.activation(out=woven(sq[h][:]), in_=planar(s[h][:]), func=ACT.Square, bias=-0.5)
 
         def times_a(i, bank_nr):
             bk = bank(bank_nr, "a%d" % i)
             for t in range(L):
                 product(bk[:, block(t)], w1d_q, block(t), e_q[i // 2], block(i % 2), E4, True, True)
-            nc.vector.tensor_tensor(out=ga[i // 2][:, block(i % 2), :],
-                                    in0=bk[:].rearrange("p (t n) -> p n t", t=L),
-                                    in1=for_db[:, :, block(i)].rearrange("p t n -> p n t"), op=ALU.mult)
+            nc.vector.tensor_tensor(out=woven(ga[i // 2][:, block(i % 2), :]),
+                                    in0=planar(bk[:].rearrange("p (t n) -> p t n", t=L)),
+                                    in1=planar(for_db[:, :, block(i)]), op=ALU.mult)
 
         def gradient_a(h):
             da_w = sb.tile([P, H, L], BF16, name="da_w%d" % h, align_bytes=64)
@@ -195,6 +201,8 @@ def tile_attend_ggate_E_pl_kernel(tc, eT, w1, w2, dy, c1, c2, ts, offs, out_0, o
         times_a(0, 4)
         times_a(1, 5)
 
+        w1f_q = quantise(flat(w1_f), E4, "w1f", K)
+
         out_rows = out_0.rearrange("(p j) c -> p j c", j=L)
 
         def result(out, j, grads):
@@ -204,12 +212,11 @@ def tile_attend_ggate_E_pl_kernel(tc, eT, w1, w2, dy, c1, c2, ts, offs, out_0, o
         grads = (gradient_a(0), gradient_b(0))
         times_a(2, 4)
         times_a(3, 5)
-        de_first = [sb.tile([P, 2, H], F32, name="de_first%d" % u) for u in range(2)]
-        for u in range(2):
-            bk = bank(2 + u, "x_first%d" % u)
-            for t in range(2):
-                result(bk[:, half(t)], 2 * u + t, grads)
-            nc.scalar.copy(out=de_first[u][:], in_=bk[:].rearrange("p (t n) -> p t n", t=2))
+        x_first = [bank(2 + v, "x_first%d" % v) for v in range(2)]
+        for j in range(L):
+            result(x_first[j // 2][:, half(j % 2)], j, grads)
+        first_low = sb.tile([P, 2, H], F32, name="first_low")
+        nc.scalar.copy(out=first_low[:], in_=x_first[0][:].rearrange("p (t n) -> p t n", t=2))
 
         def scatter_scalar(j, h, src):
             nc.scalar.activation(out=windows[j][:].indirect(offsets_of(h)), in_=src, func=ACT.Copy)
@@ -227,8 +234,10 @@ def tile_attend_ggate_E_pl_kernel(tc, eT, w1, w2, dy, c1, c2, ts, offs, out_0, o
         db_q = gradient_b(1)
         for j in range(L):
             product(xs[j][:, 0:H], w2f_q, block(j), db_q, slice(0, H), E5, False, True)
-        scatter_scalar(0, 0, de_first[0][:, 0, :])
-        scatter_scalar(1, 0, de_first[0][:, 1, :])
+        first_high = sb.tile([P, 2, H], F32, name="first_high", tag="sq1")
+        nc.vector.tensor_copy(out=first_high[:], in_=x_first[1][:].rearrange("p (t n) -> p t n", t=2))
+        scatter_scalar(0, 0, first_low[:, 0, :])
+        scatter_scalar(1, 0, first_low[:, 1, :])
         de_second = [sb.tile([P, H], F32, name="de_second%d" % j) for j in range(L)]
         nc.vector.tensor_copy(out=de_second[0][:], in_=xs[0][:, 0:H])
         scatter_vector(0, 1, de_second[0][:])
@@ -238,10 +247,10 @@ def tile_attend_ggate_E_pl_kernel(tc, eT, w1, w2, dy, c1, c2, ts, offs, out_0, o
         store(1)
         nc.vector.tensor_copy(out=de_second[2][:], in_=xs[2][:, 0:H])
         scatter_vector(2, 1, de_second[2][:])
-        scatter_vector(2, 0, de_first[1][:, 0, :])
+        scatter_vector(2, 0, first_high[:, 0, :])
         store(2)
         nc.scalar.copy(out=de_second[3][:], in_=xs[3][:, 0:H])
-        scatter_scalar(3, 0, de_first[1][:, 1, :])
+        scatter_scalar(3, 0, first_high[:, 1, :])
         scatter_scalar(3, 1, de_second[3][:])
         store(3)
 

@@ -137,21 +137,25 @@ def tile_attend_ggate_E_pl_kernel(tc, eT, w1, w2, dy, c1, c2, ts, offs, out_0, o
 
         w1d_q = along_d(w1_raw, "w1", w1_d, nc.scalar.copy, 2)
 
+        w1_f = sb.tile([P, L, P, L], BF16, name="w1_f", align_bytes=64)
+        along_f(w1_d, "w1", w1_f, 6)
         clear(2, "w2_d")
         clear(3, "dy_then_window")
 
-        e_slot = sb.tile([P, N, L], BF16, name="e_slot", tag="c2_then_e0", align_bytes=64)
+        e_slot = after_ts.tile([P, N, L], BF16, name="e_slot", offset=4096, align_bytes=64)
         e_low = sb.tile([P, 2, N], BF16, name="e_low", tag="c2_then_e1", align_bytes=64)
         for j in range(2):
             nc.vector.tensor_copy(out=e_low[:, j, :], in_=e_planes[j][:].indirect(offsets[:]))
         nc.scalar.copy(out=e_slot[:, :, 0:2], in_=e_low[:].rearrange("p j n -> p n j"))
         w2f_q = quantise(flat(w2_f), E4, "w2f", K)
-        nc.vector.tensor_copy(out=e_slot[:, :, 2], in_=e_planes[2][:].indirect(offsets[:]))
-        w1_f = sb.tile([P, L, P, L], BF16, name="w1_f", tag="c2_then_e1", align_bytes=64)
-        along_f(w1_d, "w1", w1_f, 6)
+        e_high = sb.tile([P, 2, N], BF16, name="e_high", tag="c2_then_e0", align_bytes=64)
+        nc.vector.tensor_copy(out=e_high[:, 0, :], in_=e_planes[2][:].indirect(offsets[:]))
+        w1f_q = quantise(flat(w1_f), E4, "w1f", K)
         e_q = []
         for h in range(2):
-            nc.vector.tensor_copy(out=e_slot[:, half(h), L - 1], in_=e_planes[L - 1][:].indirect(offsets_of(h)))
+            nc.vector.tensor_copy(out=e_high[:, 1, half(h)], in_=e_planes[L - 1][:].indirect(offsets_of(h)))
+            nc.scalar.copy(out=e_slot[:, half(h), 2:4], in_=e_high[:, :, half(h)].rearrange("p j n -> p n j"))
+        for h in range(2):
             e_q.append(quantise(e_slot[:, half(h), :].rearrange("p n j -> p (n j)"), E4, "e%d" % h, H))
 
         def woven(x):
@@ -200,8 +204,6 @@ def tile_attend_ggate_E_pl_kernel(tc, eT, w1, w2, dy, c1, c2, ts, offs, out_0, o
         gate(1)
         times_a(0, 4)
         times_a(1, 5)
-
-        w1f_q = quantise(flat(w1_f), E4, "w1f", K)
 
         out_rows = out_0.rearrange("(p j) c -> p j c", j=L)
 
@@ -254,7 +256,8 @@ def tile_attend_ggate_E_pl_kernel(tc, eT, w1, w2, dy, c1, c2, ts, offs, out_0, o
         scatter_scalar(3, 1, de_second[3][:])
         store(3)
 
-        split = 11 * T // 16
+        split = 21 * T // 32
+        pieces = [(c * CW, (c + 1) * CW) for c in range(CH - 1)] + [(T - CW, T - CW // 2), (T - CW // 2, T)]
         words_out = out_1[0].rearrange("p c l -> p (c l)").bitcast(I32)
         ys = [sb.tile([P, CW * L], BF16, name="y%d" % c, tag="plane_then_y%d" % c, align_bytes=64) for c in range(CH)]
         for name, copy, dtype, first, last in (("vector", nc.vector.tensor_copy, I32, 0, split),
@@ -263,18 +266,19 @@ def tile_attend_ggate_E_pl_kernel(tc, eT, w1, w2, dy, c1, c2, ts, offs, out_0, o
             for j in range(L):
                 copy(out=pairs[:, j // 2, :, j % 2], in_=windows[j][:, first:last])
             pair_words = pairs[:].rearrange("p u n e -> p (u n e)").bitcast(dtype).rearrange("p (u n) -> p n u", u=2)
-            for c in range(CH):
-                lo, hi = max(first, c * CW), min(last, (c + 1) * CW)
+            for lo, hi in pieces:
+                lo, hi, c = max(first, lo), min(last, hi), lo // CW
                 if lo < hi:
                     y_words = ys[c][:].bitcast(dtype).rearrange("p (n u) -> p n u", u=2)
                     copy(out=y_words[:, lo - c * CW:hi - c * CW, :], in_=pair_words[:, lo - first:hi - first, :])
 
         y_scales = sb.tile([P, CW], U8, name="y_scales", align_bytes=64)
-        for c in range(CH):
-            cols = slice(c * CW, (c + 1) * CW)
-            codes = sb.tile([P, CW], U32, name="y_codes%d" % c, align_bytes=64)
-            nc.vector.quantize_mx(out=codes[:].bitcast(E4), scales=y_scales[4 * c:P, :], in_=ys[c][:])
-            nc.sync.dma_start(out=words_out[:, cols], in_=codes[:].bitcast(I32))
-        for q, queue in enumerate([nc.sync, nc.sync, nc.sync, nc.sync]):
-            queue.dma_start(out=out_2[0, 4 * q:4 * q + 4, :].bitcast(I32).rearrange("r (c x) -> c r x", c=CH),
-                            in_=y_scales[32 * q:32 * q + 16, :].bitcast(I32))
+        for lo, hi in pieces:
+            c = lo // CW
+            codes = sb.tile([P, hi - lo], U32, name="y_codes%d" % lo, align_bytes=64)
+            nc.vector.quantize_mx(out=codes[:].bitcast(E4), scales=y_scales[4 * c:P, lo - c * CW:hi - c * CW],
+                                  in_=ys[c][:, L * (lo - c * CW):L * (hi - c * CW)])
+            nc.sync.dma_start(out=words_out[:, lo:hi], in_=codes[:].bitcast(I32))
+        for q in range(4):
+            nc.sync.dma_start(out=out_2[0, 4 * q:4 * q + 4, :].bitcast(I32).rearrange("r (c x) -> c r x", c=CH),
+                              in_=y_scales[32 * q:32 * q + 16, :].bitcast(I32))

@@ -60,8 +60,6 @@ def tile_attend_ggate_E_pl_kernel(tc, eT, w1, w2, dy, c1, c2, ts, offs, out_0, o
         nc.sync.dma_start(out=w2_raw[:], in_=w2.rearrange("(p j) f -> p j f", j=L))
         dy_sb = sb.tile([P, L, N], F32, name="dy_sb", tag="dy_then_window", align_bytes=64)
         nc.sync.dma_start(out=dy_sb[:], in_=dy.rearrange("(p t) n -> p t n", t=L))
-        w1_raw = sb.tile([P, L, K], F32, name="w1_raw")
-        nc.sync.dma_start(out=w1_raw[:], in_=w1.rearrange("(p j) f -> p j f", j=L))
         c2_sb = sb.tile([P, L], F32, name="c2_sb")
         nc.scalar.dma_start(out=c2_sb[:], in_=c2.rearrange("(p t) o -> p (t o)", t=L))
         c1_sb = sb.tile([P, L], F32, name="c1_sb")
@@ -72,6 +70,8 @@ def tile_attend_ggate_E_pl_kernel(tc, eT, w1, w2, dy, c1, c2, ts, offs, out_0, o
             plane = sb.tile([P, T], F32, name="e_plane%d" % j, tag="plane_then_y%d" % j, align_bytes=64)
             nc.sync.dma_start(out=plane[:], in_=e_rows[:, j, :])
             e_planes.append(plane)
+        w1_raw = sb.tile([P, L, K], F32, name="w1_raw")
+        nc.sync.dma_start(out=w1_raw[:], in_=w1.rearrange("(p j) f -> p j f", j=L))
 
         def offsets_of(h):
             return offsets[:, h * H // 16:(h + 1) * H // 16]
@@ -82,12 +82,15 @@ def tile_attend_ggate_E_pl_kernel(tc, eT, w1, w2, dy, c1, c2, ts, offs, out_0, o
 
         windows = {}
 
-        def clear(j, tag):
+        def clear(j, tag, engine):
             windows[j] = sb.tile([P, T], F32, name="window%d" % j, tag=tag, align_bytes=64)
-            nc.gpsimd.memset(windows[j][:].bitcast(I32), 0)
+            engine.memset(windows[j][:].bitcast(I32), 0)
 
-        clear(0, "window0")
-        clear(1, "window1")
+        clear(0, "window0", nc.vector)
+        clear(1, "window1", nc.vector)
+
+        warm = sb.tile([P, 1], F32, name="warm")
+        nc.scalar.activation(out=warm[:], in_=ident[:, 0:1], func=ACT.Sigmoid)
 
         ts_all = after_ts.tile([P, T], F32, name="ts_all", offset=0, align_bytes=64)
         ts_view = ts_all[:].rearrange("q (p m) -> q p m", p=P)
@@ -97,17 +100,18 @@ def tile_attend_ggate_E_pl_kernel(tc, eT, w1, w2, dy, c1, c2, ts, offs, out_0, o
                 m = 4 * g + r
                 nc.tensor.transpose(bk[:, r * P:(r + 1) * P], ts_row[:, m:m + 1].to_broadcast([P, P]), ident[:])
             nc.scalar.copy(out=ts_view[:, :, 4 * g:4 * g + 4], in_=bk[:].rearrange("q (r p) -> q p r", r=4))
+
         ts_slot = sb.tile([P, N], F32, name="ts_slot")
         nc.scalar.activation(out=ts_slot[:], in_=ts_all[:].indirect(offsets[:]), func=ACT.Copy)
 
         def flat(x):
             return x[:].rearrange("p a b c -> p (a b c)")
 
-        def along_d(raw, name, wd, copy, step):
-            for t in range(0, L, step):
-                copy(out=wd[:].rearrange("p t m j -> p m j t")[:, :, :, t:t + step],
-                     in_=raw[:].rearrange("p j (m t) -> p m j t", t=L)[:, :, :, t:t + step])
-            return quantise(flat(wd), E4, name + "d", K)
+        def dealt(wd):
+            return wd[:].rearrange("p t m j -> p m j t")
+
+        def rows(raw):
+            return raw[:].rearrange("p j (m t) -> p m j t", t=L)
 
         def along_f(wd, name, wf, first_bank):
             words = flat(wd).bitcast(F32).rearrange("p (t m v) -> p t m v", t=L, v=2)
@@ -120,12 +124,14 @@ def tile_attend_ggate_E_pl_kernel(tc, eT, w1, w2, dy, c1, c2, ts, offs, out_0, o
 
         w2_d = sb.tile([P, L, P, L], BF16, name="w2_d", tag="w2_d", align_bytes=64)
         w2_f = after_ts.tile([P, L, P, L], BF16, name="w2_f", offset=0, align_bytes=64)
-        w1_d = after_ts.tile([P, L, P, L], BF16, name="w1_d", offset=4096, align_bytes=64)
-        w2d_q = along_d(w2_raw, "w2", w2_d, nc.vector.tensor_copy, 4)
+        nc.vector.tensor_copy(out=dealt(w2_d), in_=rows(w2_raw))
+        w2d_q = quantise(flat(w2_d), E4, "w2d", K)
         along_f(w2_d, "w2", w2_f, 4)
-        c2_neg = [sb.tile([P, 2], F32, name="c2_neg%d" % v, tag="c2_then_e%d" % v, align_bytes=64) for v in range(2)]
+        e_slot = sb.tile([P, N, L], BF16, name="e_slot", align_bytes=64)
+        e_high = sb.tile([P, 2, N], BF16, name="e_high", tag="e_then_w1", align_bytes=64)
+        c2_neg = [e_high[:, 0, 0:4].bitcast(F32), e_high[:, 0, 4:8].bitcast(F32)]
         for v in range(2):
-            nc.vector.tensor_scalar(out=c2_neg[v][:], in0=c2_sb[:, 2 * v:2 * v + 2], scalar1=-1.0, scalar2=None, op0=ALU.mult)
+            nc.vector.tensor_scalar(out=c2_neg[v], in0=c2_sb[:, 2 * v:2 * v + 2], scalar1=-1.0, scalar2=None, op0=ALU.mult)
         for_da = sb.tile([P, L, N], F32, name="for_da")
         for_db = sb.tile([P, L, N], F32, name="for_db")
         for t in range(L):
@@ -134,29 +140,19 @@ def tile_attend_ggate_E_pl_kernel(tc, eT, w1, w2, dy, c1, c2, ts, offs, out_0, o
         for t in range(L):
             nc.vector.scalar_tensor_tensor(out=for_db[:, t, :], in0=for_da[:, t, :], scalar=c2_neg[t // 2][:, t % 2:t % 2 + 1],
                                            in1=ts_slot[:], op0=ALU.mult, op1=ALU.mult)
-
-        w1d_q = along_d(w1_raw, "w1", w1_d, nc.scalar.copy, 2)
-
-        w1_f = sb.tile([P, L, P, L], BF16, name="w1_f", align_bytes=64)
-        along_f(w1_d, "w1", w1_f, 6)
-        clear(2, "w2_d")
-        clear(3, "dy_then_window")
-
-        e_slot = after_ts.tile([P, N, L], BF16, name="e_slot", offset=4096, align_bytes=64)
-        e_low = sb.tile([P, 2, N], BF16, name="e_low", tag="c2_then_e1", align_bytes=64)
-        for j in range(2):
-            nc.vector.tensor_copy(out=e_low[:, j, :], in_=e_planes[j][:].indirect(offsets[:]))
-        nc.scalar.copy(out=e_slot[:, :, 0:2], in_=e_low[:].rearrange("p j n -> p n j"))
+        clear(2, "w2_d", nc.gpsimd)
+        clear(3, "dy_then_window", nc.gpsimd)
         w2f_q = quantise(flat(w2_f), E4, "w2f", K)
-        e_high = sb.tile([P, 2, N], BF16, name="e_high", tag="c2_then_e0", align_bytes=64)
+
+        e_low = after_ts.tile([P, 2, N], BF16, name="e_low", offset=4096, align_bytes=64)
+        for j in range(2):
+            nc.scalar.activation(out=e_low[:, j, :], in_=e_planes[j][:].indirect(offsets[:]), func=ACT.Copy)
+        nc.scalar.copy(out=e_slot[:, :, 0:2], in_=e_low[:].rearrange("p j n -> p n j"))
         nc.vector.tensor_copy(out=e_high[:, 0, :], in_=e_planes[2][:].indirect(offsets[:]))
-        w1f_q = quantise(flat(w1_f), E4, "w1f", K)
-        e_q = []
         for h in range(2):
-            nc.vector.tensor_copy(out=e_high[:, 1, half(h)], in_=e_planes[L - 1][:].indirect(offsets_of(h)))
+            nc.vector.tensor_copy(out=e_high[:, 1, half(h)], in_=e_planes[3][:].indirect(offsets_of(h)))
             nc.scalar.copy(out=e_slot[:, half(h), 2:4], in_=e_high[:, :, half(h)].rearrange("p j n -> p n j"))
-        for h in range(2):
-            e_q.append(quantise(e_slot[:, half(h), :].rearrange("p n j -> p (n j)"), E4, "e%d" % h, H))
+        e_q = [quantise(e_slot[:, half(h), :].rearrange("p n j -> p (n j)"), E4, "e%d" % h, H) for h in range(2)]
 
         def woven(x):
             return x.rearrange("p (c i) t -> p c t i", i=2)
@@ -179,6 +175,8 @@ def tile_attend_ggate_E_pl_kernel(tc, eT, w1, w2, dy, c1, c2, ts, offs, out_0, o
                                                    scalar=c2_sb[:, 2 * v + t:2 * v + t + 1], in1=ts_slot[:, half(h)],
                                                    op0=ALU.mult, op1=ALU.mult)
             nc.scalar.activation(out=s[h][:], in_=u[h][:], func=ACT.Sigmoid)
+
+        def square(h):
             nc.scalar.activation(out=woven(sq[h][:]), in_=planar(s[h][:]), func=ACT.Square, bias=-0.5)
 
         def times_a(i, bank_nr):
@@ -200,18 +198,28 @@ def tile_attend_ggate_E_pl_kernel(tc, eT, w1, w2, dy, c1, c2, ts, offs, out_0, o
                                            op0=ALU.subtract, op1=ALU.mult)
             return quantise(db_w[:].rearrange("p n t -> p (n t)"), E5, "db%d" % h, H)
 
+        w1_d = sb.tile([P, L, P, L], BF16, name="w1_d", tag="e_then_w1", align_bytes=64)
+        for t in range(0, L, 2):
+            nc.scalar.copy(out=dealt(w1_d)[:, :, :, t:t + 2], in_=rows(w1_raw)[:, :, :, t:t + 2])
         gate(0)
         gate(1)
+        w1d_q = quantise(flat(w1_d), E4, "w1d", K)
+        da_first = gradient_a(0)
         times_a(0, 4)
         times_a(1, 5)
+        square(0)
+        w1_f = sb.tile([P, L, P, L], BF16, name="w1_f", align_bytes=64)
+        along_f(w1_d, "w1", w1_f, 6)
+        square(1)
 
         out_rows = out_0.rearrange("(p j) c -> p j c", j=L)
 
         def result(out, j, grads):
-            product(out, w1f_q, block(j), grads[0], slice(0, H), E5, True, False)
-            product(out, w2f_q, block(j), grads[1], slice(0, H), E5, False, True)
+            product(out, w2f_q, block(j), grads[1], slice(0, H), E5, True, False)
+            product(out, w1f_q, block(j), grads[0], slice(0, H), E5, False, True)
 
-        grads = (gradient_a(0), gradient_b(0))
+        grads = (da_first, gradient_b(0))
+        w1f_q = quantise(flat(w1_f), E4, "w1f", K)
         times_a(2, 4)
         times_a(3, 5)
         x_first = [bank(2 + v, "x_first%d" % v) for v in range(2)]

@@ -70,7 +70,7 @@ def tile_attend_ggate_E_pl_kernel(tc, eT, w1, w2, dy, c1, c2, ts, offs, out_0, o
             plane = sb.tile([P, T], F32, name="e_plane%d" % j, tag="plane_then_y%d" % j, align_bytes=64)
             nc.sync.dma_start(out=plane[:], in_=e_rows[:, j, :])
             e_planes.append(plane)
-        w1_raw = sb.tile([P, L, K], F32, name="w1_raw")
+        w1_raw = sb.tile([P, L, K], F32, name="w1_raw", tag="da_w0", align_bytes=64)
         nc.sync.dma_start(out=w1_raw[:], in_=w1.rearrange("(p j) f -> p j f", j=L))
 
         def offsets_of(h):
@@ -127,8 +127,8 @@ def tile_attend_ggate_E_pl_kernel(tc, eT, w1, w2, dy, c1, c2, ts, offs, out_0, o
         nc.vector.tensor_copy(out=dealt(w2_d), in_=rows(w2_raw))
         w2d_q = quantise(flat(w2_d), E4, "w2d", K)
         along_f(w2_d, "w2", w2_f, 4)
-        e_slot = sb.tile([P, N, L], BF16, name="e_slot", align_bytes=64)
-        e_high = sb.tile([P, 2, N], BF16, name="e_high", tag="e_then_w1", align_bytes=64)
+        e_slot = sb.tile([P, N, L], BF16, name="e_slot", tag="sq1", align_bytes=64)
+        e_high = sb.tile([P, 2, N], BF16, name="e_high", align_bytes=64)
         c2_neg = [e_high[:, 0, 0:4].bitcast(F32), e_high[:, 0, 4:8].bitcast(F32)]
         for v in range(2):
             nc.vector.tensor_scalar(out=c2_neg[v], in0=c2_sb[:, 2 * v:2 * v + 2], scalar1=-1.0, scalar2=None, op0=ALU.mult)
@@ -161,8 +161,8 @@ def tile_attend_ggate_E_pl_kernel(tc, eT, w1, w2, dy, c1, c2, ts, offs, out_0, o
             return x.rearrange("p t (c i) -> p c t i", i=2)
 
         u = [sb.tile([P, L, H], F32, name="u%d" % h) for h in range(2)]
-        s = [sb.tile([P, L, H], F32, name="s%d" % h) for h in range(2)]
-        sq = [sb.tile([P, H, L], F32, name="sq%d" % h, tag="sq%d" % h) for h in range(2)]
+        s = [sb.tile([P, L, H], F32, name="s0")]
+        sq = [sb.tile([P, H, L], F32, name="sq0")]
         ga = [sb.tile([P, H, L], F32, name="ga%d" % h) for h in range(2)]
 
         def gate(h):
@@ -174,6 +174,8 @@ def tile_attend_ggate_E_pl_kernel(tc, eT, w1, w2, dy, c1, c2, ts, offs, out_0, o
                     nc.vector.scalar_tensor_tensor(out=u[h][:, 2 * v + t, :], in0=bk[:, half(t)],
                                                    scalar=c2_sb[:, 2 * v + t:2 * v + t + 1], in1=ts_slot[:, half(h)],
                                                    op0=ALU.mult, op1=ALU.mult)
+
+        def sigmoid(h):
             nc.scalar.activation(out=s[h][:], in_=u[h][:], func=ACT.Sigmoid)
 
         def square(h):
@@ -188,7 +190,7 @@ def tile_attend_ggate_E_pl_kernel(tc, eT, w1, w2, dy, c1, c2, ts, offs, out_0, o
                                     in1=planar(for_db[:, :, block(i)]), op=ALU.mult)
 
         def gradient_a(h):
-            da_w = sb.tile([P, H, L], BF16, name="da_w%d" % h, align_bytes=64)
+            da_w = sb.tile([P, H, L], BF16, name="da_w%d" % h, tag="da_w%d" % h, align_bytes=64)
             nc.vector.tensor_tensor(out=woven(da_w[:]), in0=planar(for_da[:, :, half(h)]), in1=planar(s[h][:]), op=ALU.mult)
             return quantise(da_w[:].rearrange("p n t -> p (n t)"), E5, "da%d" % h, H)
 
@@ -196,35 +198,36 @@ def tile_attend_ggate_E_pl_kernel(tc, eT, w1, w2, dy, c1, c2, ts, offs, out_0, o
             db_w = sb.tile([P, H, L], BF16, name="db_w%d" % h, align_bytes=64)
             nc.vector.scalar_tensor_tensor(out=db_w[:], in0=sq[h][:], scalar=0.25, in1=ga[h][:],
                                            op0=ALU.subtract, op1=ALU.mult)
-            return quantise(db_w[:].rearrange("p n t -> p (n t)"), E5, "db%d" % h, H)
+            return db_w[:].rearrange("p n t -> p (n t)")
 
-        w1_d = sb.tile([P, L, P, L], BF16, name="w1_d", tag="e_then_w1", align_bytes=64)
-        for t in range(0, L, 2):
-            nc.scalar.copy(out=dealt(w1_d)[:, :, :, t:t + 2], in_=rows(w1_raw)[:, :, :, t:t + 2])
+        w1_d = sb.tile([P, L, P, L], BF16, name="w1_d", tag="sq1", align_bytes=64)
+        nc.gpsimd.tensor_scalar(out=w1_d[:].rearrange("p t m j -> p m t j"), in0=w1_raw[:].rearrange("p j (m t) -> p m t j", t=L),
+                                scalar1=1.0, scalar2=0.0, op0=ALU.mult, op1=ALU.add)
         gate(0)
+        sigmoid(0)
         gate(1)
         w1d_q = quantise(flat(w1_d), E4, "w1d", K)
-        da_first = gradient_a(0)
-        times_a(0, 4)
-        times_a(1, 5)
         square(0)
         w1_f = sb.tile([P, L, P, L], BF16, name="w1_f", align_bytes=64)
         along_f(w1_d, "w1", w1_f, 6)
-        square(1)
-
-        out_rows = out_0.rearrange("(p j) c -> p j c", j=L)
-
-        def result(out, j, grads):
-            product(out, w2f_q, block(j), grads[1], slice(0, H), E5, True, False)
-            product(out, w1f_q, block(j), grads[0], slice(0, H), E5, False, True)
-
-        grads = (da_first, gradient_b(0))
+        da_q = gradient_a(0)
+        times_a(0, 4)
+        times_a(1, 5)
+        db_first = gradient_b(0)
         w1f_q = quantise(flat(w1_f), E4, "w1f", K)
+        db_q = quantise(db_first, E5, "db0", H)
+        s.append(sb.tile([P, L, H], F32, name="s1", tag="sq1", align_bytes=64))
+        sigmoid(1)
+        sq.append(sb.tile([P, H, L], F32, name="sq1", tag="sq1_then_first", align_bytes=64))
+        square(1)
         times_a(2, 4)
         times_a(3, 5)
+
+        out_rows = out_0.rearrange("(p j) c -> p j c", j=L)
         x_first = [bank(2 + v, "x_first%d" % v) for v in range(2)]
         for j in range(L):
-            result(x_first[j // 2][:, half(j % 2)], j, grads)
+            product(x_first[j // 2][:, half(j % 2)], w1f_q, block(j), da_q, slice(0, H), E5, True, False)
+            product(x_first[j // 2][:, half(j % 2)], w2f_q, block(j), db_q, slice(0, H), E5, False, True)
         first_low = sb.tile([P, 2, H], F32, name="first_low")
         nc.scalar.copy(out=first_low[:], in_=x_first[0][:].rearrange("p (t n) -> p t n", t=2))
 
@@ -241,10 +244,10 @@ def tile_attend_ggate_E_pl_kernel(tc, eT, w1, w2, dy, c1, c2, ts, offs, out_0, o
         xs = [bank(4 + j, "x_second%d" % j) for j in range(L)]
         for j in range(L):
             product(xs[j][:, 0:H], w1f_q, block(j), da_q, slice(0, H), E5, True, False)
-        db_q = gradient_b(1)
+        db_q = quantise(gradient_b(1), E5, "db1", H)
         for j in range(L):
             product(xs[j][:, 0:H], w2f_q, block(j), db_q, slice(0, H), E5, False, True)
-        first_high = sb.tile([P, 2, H], F32, name="first_high", tag="sq1")
+        first_high = sb.tile([P, 2, H], F32, name="first_high", tag="sq1_then_first", align_bytes=64)
         nc.vector.tensor_copy(out=first_high[:], in_=x_first[1][:].rearrange("p (t n) -> p t n", t=2))
         scatter_scalar(0, 0, first_low[:, 0, :])
         scatter_scalar(1, 0, first_low[:, 1, :])
@@ -264,7 +267,7 @@ def tile_attend_ggate_E_pl_kernel(tc, eT, w1, w2, dy, c1, c2, ts, offs, out_0, o
         scatter_scalar(3, 1, de_second[3][:])
         store(3)
 
-        split = 21 * T // 32
+        split = 5 * T // 8
         pieces = [(c * CW, (c + 1) * CW) for c in range(CH - 1)] + [(T - CW, T - CW // 2), (T - CW // 2, T)]
         words_out = out_1[0].rearrange("p c l -> p (c l)").bitcast(I32)
         ys = [sb.tile([P, CW * L], BF16, name="y%d" % c, tag="plane_then_y%d" % c, align_bytes=64) for c in range(CH)]

@@ -70,7 +70,7 @@ def tile_attend_ggate_E_pl_kernel(tc, eT, w1, w2, dy, c1, c2, ts, offs, out_0, o
             plane = sb.tile([P, T], F32, name="e_plane%d" % j, tag="plane_then_y%d" % j, align_bytes=64)
             nc.sync.dma_start(out=plane[:], in_=e_rows[:, j, :])
             e_planes.append(plane)
-        w1_raw = sb.tile([P, L, K], F32, name="w1_raw", tag="da_w0", align_bytes=64)
+        w1_raw = sb.tile([P, L, K], F32, name="w1_raw", tag="w1_then_s", align_bytes=64)
         nc.sync.dma_start(out=w1_raw[:], in_=w1.rearrange("(p j) f -> p j f", j=L))
 
         def offsets_of(h):
@@ -127,9 +127,8 @@ def tile_attend_ggate_E_pl_kernel(tc, eT, w1, w2, dy, c1, c2, ts, offs, out_0, o
         nc.vector.tensor_copy(out=dealt(w2_d), in_=rows(w2_raw))
         w2d_q = quantise(flat(w2_d), E4, "w2d", K)
         along_f(w2_d, "w2", w2_f, 4)
-        e_slot = sb.tile([P, N, L], BF16, name="e_slot", tag="sq1", align_bytes=64)
-        e_high = sb.tile([P, 2, N], BF16, name="e_high", align_bytes=64)
-        c2_neg = [e_high[:, 0, 0:4].bitcast(F32), e_high[:, 0, 4:8].bitcast(F32)]
+        e_slot = sb.tile([P, N, L], BF16, name="e_slot", align_bytes=64)
+        c2_neg = [e_slot[:, v * H, :].bitcast(F32) for v in range(2)]
         for v in range(2):
             nc.vector.tensor_scalar(out=c2_neg[v], in0=c2_sb[:, 2 * v:2 * v + 2], scalar1=-1.0, scalar2=None, op0=ALU.mult)
         for_da = sb.tile([P, L, N], F32, name="for_da")
@@ -148,10 +147,9 @@ def tile_attend_ggate_E_pl_kernel(tc, eT, w1, w2, dy, c1, c2, ts, offs, out_0, o
         for j in range(2):
             nc.scalar.activation(out=e_low[:, j, :], in_=e_planes[j][:].indirect(offsets[:]), func=ACT.Copy)
         nc.scalar.copy(out=e_slot[:, :, 0:2], in_=e_low[:].rearrange("p j n -> p n j"))
-        nc.vector.tensor_copy(out=e_high[:, 0, :], in_=e_planes[2][:].indirect(offsets[:]))
+        nc.vector.tensor_copy(out=e_slot[:, :, 2], in_=e_planes[2][:].indirect(offsets[:]))
         for h in range(2):
-            nc.vector.tensor_copy(out=e_high[:, 1, half(h)], in_=e_planes[3][:].indirect(offsets_of(h)))
-            nc.scalar.copy(out=e_slot[:, half(h), 2:4], in_=e_high[:, :, half(h)].rearrange("p j n -> p n j"))
+            nc.vector.tensor_copy(out=e_slot[:, half(h), 3], in_=e_planes[3][:].indirect(offsets_of(h)))
         e_q = [quantise(e_slot[:, half(h), :].rearrange("p n j -> p (n j)"), E4, "e%d" % h, H) for h in range(2)]
 
         def woven(x):
@@ -161,7 +159,7 @@ def tile_attend_ggate_E_pl_kernel(tc, eT, w1, w2, dy, c1, c2, ts, offs, out_0, o
             return x.rearrange("p t (c i) -> p c t i", i=2)
 
         u = [sb.tile([P, L, H], F32, name="u%d" % h) for h in range(2)]
-        s = [sb.tile([P, L, H], F32, name="s0")]
+        s = [sb.tile([P, L, H], F32, name="s0", tag="w1_then_s", align_bytes=64)]
         sq = [sb.tile([P, H, L], F32, name="sq0")]
         ga = [sb.tile([P, H, L], F32, name="ga%d" % h) for h in range(2)]
 
@@ -192,7 +190,7 @@ def tile_attend_ggate_E_pl_kernel(tc, eT, w1, w2, dy, c1, c2, ts, offs, out_0, o
         def gradient_a(h):
             da_w = sb.tile([P, H, L], BF16, name="da_w%d" % h, tag="da_w%d" % h, align_bytes=64)
             nc.vector.tensor_tensor(out=woven(da_w[:]), in0=planar(for_da[:, :, half(h)]), in1=planar(s[h][:]), op=ALU.mult)
-            return quantise(da_w[:].rearrange("p n t -> p (n t)"), E5, "da%d" % h, H)
+            return da_w[:].rearrange("p n t -> p (n t)")
 
         def gradient_b(h):
             db_w = sb.tile([P, H, L], BF16, name="db_w%d" % h, align_bytes=64)
@@ -200,9 +198,8 @@ def tile_attend_ggate_E_pl_kernel(tc, eT, w1, w2, dy, c1, c2, ts, offs, out_0, o
                                            op0=ALU.subtract, op1=ALU.mult)
             return db_w[:].rearrange("p n t -> p (n t)")
 
-        w1_d = sb.tile([P, L, P, L], BF16, name="w1_d", tag="sq1", align_bytes=64)
-        nc.gpsimd.tensor_scalar(out=w1_d[:].rearrange("p t m j -> p m t j"), in0=w1_raw[:].rearrange("p j (m t) -> p m t j", t=L),
-                                scalar1=1.0, scalar2=0.0, op0=ALU.mult, op1=ALU.add)
+        w1_d = after_ts.tile([P, L, P, L], BF16, name="w1_d", offset=4096, align_bytes=64)
+        nc.scalar.copy(out=dealt(w1_d), in_=rows(w1_raw))
         gate(0)
         sigmoid(0)
         gate(1)
@@ -210,18 +207,17 @@ def tile_attend_ggate_E_pl_kernel(tc, eT, w1, w2, dy, c1, c2, ts, offs, out_0, o
         square(0)
         w1_f = sb.tile([P, L, P, L], BF16, name="w1_f", align_bytes=64)
         along_f(w1_d, "w1", w1_f, 6)
-        da_q = gradient_a(0)
+        da_first = gradient_a(0)
         times_a(0, 4)
         times_a(1, 5)
+        da_q = quantise(da_first, E5, "da0", H)
         db_first = gradient_b(0)
         w1f_q = quantise(flat(w1_f), E4, "w1f", K)
         db_q = quantise(db_first, E5, "db0", H)
-        s.append(sb.tile([P, L, H], F32, name="s1", tag="sq1", align_bytes=64))
+        s.append(after_ts.tile([P, L, H], F32, name="s1", offset=4096, align_bytes=64))
         sigmoid(1)
-        sq.append(sb.tile([P, H, L], F32, name="sq1", tag="sq1_then_first", align_bytes=64))
+        sq.append(sb.tile([P, H, L], F32, name="sq1"))
         square(1)
-        times_a(2, 4)
-        times_a(3, 5)
 
         out_rows = out_0.rearrange("(p j) c -> p j c", j=L)
         x_first = [bank(2 + v, "x_first%d" % v) for v in range(2)]
@@ -240,15 +236,20 @@ def tile_attend_ggate_E_pl_kernel(tc, eT, w1, w2, dy, c1, c2, ts, offs, out_0, o
         def store(j):
             nc.sync.dma_start(out=out_rows[:, j, :], in_=windows[j][:])
 
-        da_q = gradient_a(1)
+        times_a(2, 4)
+        da_second = gradient_a(1)
+        times_a(3, 5)
+        da_q = quantise(da_second, E5, "da1", H)
         xs = [bank(4 + j, "x_second%d" % j) for j in range(L)]
         for j in range(L):
             product(xs[j][:, 0:H], w1f_q, block(j), da_q, slice(0, H), E5, True, False)
-        db_q = quantise(gradient_b(1), E5, "db1", H)
+        db_second = gradient_b(1)
+        first_high = sb.tile([P, 2, H], F32, name="first_high")
+        nc.vector.tensor_copy(out=first_high[:, 0, :], in_=x_first[1][:, half(0)])
+        db_q = quantise(db_second, E5, "db1", H)
         for j in range(L):
             product(xs[j][:, 0:H], w2f_q, block(j), db_q, slice(0, H), E5, False, True)
-        first_high = sb.tile([P, 2, H], F32, name="first_high", tag="sq1_then_first", align_bytes=64)
-        nc.vector.tensor_copy(out=first_high[:], in_=x_first[1][:].rearrange("p (t n) -> p t n", t=2))
+        nc.vector.tensor_copy(out=first_high[:, 1, :], in_=x_first[1][:, half(1)])
         scatter_scalar(0, 0, first_low[:, 0, :])
         scatter_scalar(1, 0, first_low[:, 1, :])
         de_second = [sb.tile([P, H], F32, name="de_second%d" % j) for j in range(L)]
@@ -267,7 +268,7 @@ def tile_attend_ggate_E_pl_kernel(tc, eT, w1, w2, dy, c1, c2, ts, offs, out_0, o
         scatter_scalar(3, 1, de_second[3][:])
         store(3)
 
-        split = 5 * T // 8
+        split = 19 * T // 32
         pieces = [(c * CW, (c + 1) * CW) for c in range(CH - 1)] + [(T - CW, T - CW // 2), (T - CW // 2, T)]
         words_out = out_1[0].rearrange("p c l -> p (c l)").bitcast(I32)
         ys = [sb.tile([P, CW * L], BF16, name="y%d" % c, tag="plane_then_y%d" % c, align_bytes=64) for c in range(CH)]

@@ -252,32 +252,35 @@ def tile_attend_ggate_E_pl_kernel(tc, eT, w1, w2, dy, c1, c2, ts, offs, out_0, o
         nc.vector.tensor_copy(out=first_high[:, 1, :], in_=x_first[1][:, half(1)])
         scatter_scalar(0, 0, first_low[:, 0, :])
         scatter_scalar(1, 0, first_low[:, 1, :])
+        scatter_scalar(2, 0, first_high[:, 0, :])
         de_second = [sb.tile([P, H], F32, name="de_second%d" % j) for j in range(L)]
-        nc.vector.tensor_copy(out=de_second[0][:], in_=xs[0][:, 0:H])
-        scatter_vector(0, 1, de_second[0][:])
+        for j in (0, 2):
+            nc.vector.tensor_copy(out=de_second[j][:], in_=xs[j][:, 0:H])
+            scatter_vector(j, 1, de_second[j][:])
         store(0)
         nc.scalar.copy(out=de_second[1][:], in_=xs[1][:, 0:H])
-        scatter_scalar(1, 1, de_second[1][:])
-        store(1)
-        nc.vector.tensor_copy(out=de_second[2][:], in_=xs[2][:, 0:H])
-        scatter_vector(2, 1, de_second[2][:])
-        scatter_vector(2, 0, first_high[:, 0, :])
-        store(2)
         nc.scalar.copy(out=de_second[3][:], in_=xs[3][:, 0:H])
+        scatter_scalar(1, 1, de_second[1][:])
+        store(2)
+        store(1)
         scatter_scalar(3, 0, first_high[:, 1, :])
         scatter_scalar(3, 1, de_second[3][:])
         store(3)
 
-        split = 19 * T // 32
+        split = T // 2
         pieces = [(c * CW, (c + 1) * CW) for c in range(CH - 1)] + [(T - CW, T - CW // 2), (T - CW // 2, T)]
         words_out = out_1[0].rearrange("p c l -> p (c l)").bitcast(I32)
         ys = [sb.tile([P, CW * L], BF16, name="y%d" % c, tag="plane_then_y%d" % c, align_bytes=64) for c in range(CH)]
-        for name, copy, dtype, first, last in (("vector", nc.vector.tensor_copy, I32, 0, split),
-                                               ("scalar", nc.scalar.copy, U32, split, T)):
-            pairs = sb.tile([P, 2, last - first, 2], BF16, name="pairs_" + name, align_bytes=64)
-            for j in range(L):
-                copy(out=pairs[:, j // 2, :, j % 2], in_=windows[j][:, first:last])
-            pair_words = pairs[:].rearrange("p u n e -> p (u n e)").bitcast(dtype).rearrange("p (u n) -> p n u", u=2)
+        shares = ((nc.scalar.copy, U32, split, T), (nc.vector.tensor_copy, I32, 0, split))
+        pairs = [sb.tile([P, L * (last - first)], BF16, name="pairs%d" % first, align_bytes=64) for copy, dtype, first, last in shares]
+        lanes = [x[:].rearrange("p (u n e) -> p u n e", u=2, e=2) for x in pairs]
+        for j in range(2):
+            for share, (copy, dtype, first, last) in zip(lanes, shares):
+                nc.vector.tensor_copy(out=share[:, 0, :, j], in_=windows[j][:, first:last])
+        for pair, share, (copy, dtype, first, last) in zip(pairs, lanes, shares):
+            for j in range(2):
+                copy(out=share[:, 1, :, j], in_=windows[2 + j][:, first:last])
+            pair_words = pair[:].bitcast(dtype).rearrange("p (u n) -> p n u", u=2)
             for lo, hi in pieces:
                 lo, hi, c = max(first, lo), min(last, hi), lo // CW
                 if lo < hi:

@@ -250,22 +250,15 @@ def tile_attend_ggate_E_pl_kernel(tc, eT, w1, w2, dy, c1, c2, ts, offs, out_0, o
         for j in range(L):
             product(xs[j][:, 0:H], w2f_q, block(j), db_q, slice(0, H), E5, False, True)
         nc.vector.tensor_copy(out=first_high[:, 1, :], in_=x_first[1][:, half(1)])
-        scatter_scalar(0, 0, first_low[:, 0, :])
-        scatter_scalar(1, 0, first_low[:, 1, :])
-        scatter_scalar(2, 0, first_high[:, 0, :])
+        for j in range(L):
+            scatter_scalar(j, 0, (first_low if j < 2 else first_high)[:, j % 2, :])
         de_second = [sb.tile([P, H], F32, name="de_second%d" % j) for j in range(L)]
-        for j in (0, 2):
-            nc.vector.tensor_copy(out=de_second[j][:], in_=xs[j][:, 0:H])
-            scatter_vector(j, 1, de_second[j][:])
-        store(0)
-        nc.scalar.copy(out=de_second[1][:], in_=xs[1][:, 0:H])
-        nc.scalar.copy(out=de_second[3][:], in_=xs[3][:, 0:H])
-        scatter_scalar(1, 1, de_second[1][:])
-        store(2)
-        store(1)
-        scatter_scalar(3, 0, first_high[:, 1, :])
-        scatter_scalar(3, 1, de_second[3][:])
-        store(3)
+        for copy, scatter, planes in ((nc.vector.tensor_copy, scatter_vector, (0, 1)), (nc.scalar.copy, scatter_scalar, (2, 3))):
+            for j in planes:
+                copy(out=de_second[j][:], in_=xs[j][:, 0:H])
+            for j in planes:
+                scatter(j, 1, de_second[j][:])
+                store(j)
 
         split = T // 2
         pieces = [(c * CW, (c + 1) * CW) for c in range(CH - 1)] + [(T - CW, T - CW // 2), (T - CW // 2, T)]

@@ -70,7 +70,7 @@ def tile_attend_ggate_E_pl_kernel(tc, eT, w1, w2, dy, c1, c2, ts, offs, out_0, o
             plane = sb.tile([P, T], F32, name="e_plane%d" % j, tag="plane_then_y%d" % j, align_bytes=64)
             nc.sync.dma_start(out=plane[:], in_=e_rows[:, j, :])
             e_planes.append(plane)
-        w1_raw = sb.tile([P, L, K], F32, name="w1_raw", tag="w1_then_s", align_bytes=64)
+        w1_raw = sb.tile([P, L, K], F32, name="w1_raw", align_bytes=64)
         nc.sync.dma_start(out=w1_raw[:], in_=w1.rearrange("(p j) f -> p j f", j=L))
 
         def offsets_of(h):
@@ -127,7 +127,7 @@ def tile_attend_ggate_E_pl_kernel(tc, eT, w1, w2, dy, c1, c2, ts, offs, out_0, o
         nc.vector.tensor_copy(out=dealt(w2_d), in_=rows(w2_raw))
         w2d_q = quantise(flat(w2_d), E4, "w2d", K)
         along_f(w2_d, "w2", w2_f, 4)
-        e_slot = sb.tile([P, N, L], BF16, name="e_slot", align_bytes=64)
+        e_slot = sb.tile([P, N, L], BF16, name="e_slot", tag="e_slot", align_bytes=64)
         c2_neg = [e_slot[:, v * H, :].bitcast(F32) for v in range(2)]
         for v in range(2):
             nc.vector.tensor_scalar(out=c2_neg[v], in0=c2_sb[:, 2 * v:2 * v + 2], scalar1=-1.0, scalar2=None, op0=ALU.mult)
@@ -159,7 +159,7 @@ def tile_attend_ggate_E_pl_kernel(tc, eT, w1, w2, dy, c1, c2, ts, offs, out_0, o
             return x.rearrange("p t (c i) -> p c t i", i=2)
 
         u = [sb.tile([P, L, H], F32, name="u%d" % h) for h in range(2)]
-        s = [sb.tile([P, L, H], F32, name="s0", tag="w1_then_s", align_bytes=64)]
+        s = [w1_raw[:, :, 0:H]]
         sq = [sb.tile([P, H, L], F32, name="sq0")]
         ga = [sb.tile([P, H, L], F32, name="ga%d" % h) for h in range(2)]
 
@@ -174,10 +174,10 @@ def tile_attend_ggate_E_pl_kernel(tc, eT, w1, w2, dy, c1, c2, ts, offs, out_0, o
                                                    op0=ALU.mult, op1=ALU.mult)
 
         def sigmoid(h):
-            nc.scalar.activation(out=s[h][:], in_=u[h][:], func=ACT.Sigmoid)
+            nc.scalar.activation(out=s[h], in_=u[h][:], func=ACT.Sigmoid)
 
         def square(h):
-            nc.scalar.activation(out=woven(sq[h][:]), in_=planar(s[h][:]), func=ACT.Square, bias=-0.5)
+            nc.scalar.activation(out=woven(sq[h][:]), in_=planar(s[h]), func=ACT.Square, bias=-0.5)
 
         def times_a(i, bank_nr):
             bk = bank(bank_nr, "a%d" % i)
@@ -189,7 +189,7 @@ def tile_attend_ggate_E_pl_kernel(tc, eT, w1, w2, dy, c1, c2, ts, offs, out_0, o
 
         def gradient_a(h):
             da_w = sb.tile([P, H, L], BF16, name="da_w%d" % h, tag="da_w%d" % h, align_bytes=64)
-            nc.vector.tensor_tensor(out=woven(da_w[:]), in0=planar(for_da[:, :, half(h)]), in1=planar(s[h][:]), op=ALU.mult)
+            nc.vector.tensor_tensor(out=woven(da_w[:]), in0=planar(for_da[:, :, half(h)]), in1=planar(s[h]), op=ALU.mult)
             return da_w[:].rearrange("p n t -> p (n t)")
 
         def gradient_b(h):
@@ -198,8 +198,11 @@ def tile_attend_ggate_E_pl_kernel(tc, eT, w1, w2, dy, c1, c2, ts, offs, out_0, o
                                            op0=ALU.subtract, op1=ALU.mult)
             return db_w[:].rearrange("p n t -> p (n t)")
 
-        w1_d = after_ts.tile([P, L, P, L], BF16, name="w1_d", offset=4096, align_bytes=64)
-        nc.scalar.copy(out=dealt(w1_d), in_=rows(w1_raw))
+        w1_d = sb.tile([P, L, P, L], BF16, name="w1_d", tag="e_slot", align_bytes=64)
+        nc.scalar.copy(out=dealt(w1_d)[:, 0:P // 2], in_=rows(w1_raw)[:, 0:P // 2])
+        nc.gpsimd.tensor_scalar(out=w1_d[:].rearrange("p t m j -> p m t j")[:, P // 2:P],
+                                in0=w1_raw[:].rearrange("p j (m t) -> p m t j", t=L)[:, P // 2:P],
+                                scalar1=1.0, scalar2=0.0, op0=ALU.mult, op1=ALU.add)
         gate(0)
         sigmoid(0)
         gate(1)
@@ -214,16 +217,22 @@ def tile_attend_ggate_E_pl_kernel(tc, eT, w1, w2, dy, c1, c2, ts, offs, out_0, o
         db_first = gradient_b(0)
         w1f_q = quantise(flat(w1_f), E4, "w1f", K)
         db_q = quantise(db_first, E5, "db0", H)
-        s.append(after_ts.tile([P, L, H], F32, name="s1", offset=4096, align_bytes=64))
+        s_second = sb.tile([P, L, H], F32, name="s_second", tag="e_slot", align_bytes=64)
+        s.append(s_second[:])
         sigmoid(1)
         sq.append(sb.tile([P, H, L], F32, name="sq1"))
         square(1)
 
         out_rows = out_0.rearrange("(p j) c -> p j c", j=L)
-        x_first = [bank(2 + v, "x_first%d" % v) for v in range(2)]
-        for j in range(L):
-            product(x_first[j // 2][:, half(j % 2)], w1f_q, block(j), da_q, slice(0, H), E5, True, False)
-            product(x_first[j // 2][:, half(j % 2)], w2f_q, block(j), db_q, slice(0, H), E5, False, True)
+
+        def first_results(v, bank_nr):
+            bk = bank(bank_nr, "x_first%d" % v)
+            for i in range(2):
+                product(bk[:, half(i)], w1f_q, block(2 * v + i), da_q, slice(0, H), E5, True, False)
+                product(bk[:, half(i)], w2f_q, block(2 * v + i), db_q, slice(0, H), E5, False, True)
+            return bk
+
+        x_first = [first_results(0, 2)]
         first_low = sb.tile([P, 2, H], F32, name="first_low")
         nc.scalar.copy(out=first_low[:], in_=x_first[0][:].rearrange("p (t n) -> p t n", t=2))
 
@@ -237,10 +246,11 @@ def tile_attend_ggate_E_pl_kernel(tc, eT, w1, w2, dy, c1, c2, ts, offs, out_0, o
             nc.sync.dma_start(out=out_rows[:, j, :], in_=windows[j][:])
 
         times_a(2, 4)
+        x_first.append(first_results(1, 4))
         da_second = gradient_a(1)
         times_a(3, 5)
         da_q = quantise(da_second, E5, "da1", H)
-        xs = [bank(4 + j, "x_second%d" % j) for j in range(L)]
+        xs = [bank(nr, "x_second%d" % j) for j, nr in enumerate((0, 1, 6, 7))]
         for j in range(L):
             product(xs[j][:, 0:H], w1f_q, block(j), da_q, slice(0, H), E5, True, False)
         db_second = gradient_b(1)

@@ -247,30 +247,30 @@ def tile_attend_ggate_E_pl_kernel(tc, eT, w1, w2, dy, c1, c2, ts, offs, out_0, o
 
         times_a(2, 4)
         x_first.append(first_results(1, 4))
-        da_second = gradient_a(1)
         times_a(3, 5)
-        da_q = quantise(da_second, E5, "da1", H)
-        xs = [bank(nr, "x_second%d" % j) for j, nr in enumerate((0, 1, 6, 7))]
-        for j in range(L):
-            product(xs[j][:, 0:H], w1f_q, block(j), da_q, slice(0, H), E5, True, False)
+        da_second = gradient_a(1)
         db_second = gradient_b(1)
-        first_high = sb.tile([P, 2, H], F32, name="first_high")
-        nc.vector.tensor_copy(out=first_high[:, 0, :], in_=x_first[1][:, half(0)])
+        da_q = quantise(da_second, E5, "da1", H)
         db_q = quantise(db_second, E5, "db1", H)
+        first_high = sb.tile([P, 2, H], F32, name="first_high")
+        nc.vector.tensor_copy(out=first_high[:], in_=x_first[1][:].rearrange("p (t n) -> p t n", t=2))
+        low = [bank(j, "x_second%d" % j) for j in range(2)]
+        high = bank(4, "x_second_high")
+        xs = [low[0][:, 0:H], low[1][:, 0:H], high[:, half(0)], high[:, half(1)]]
         for j in range(L):
-            product(xs[j][:, 0:H], w2f_q, block(j), db_q, slice(0, H), E5, False, True)
-        nc.vector.tensor_copy(out=first_high[:, 1, :], in_=x_first[1][:, half(1)])
+            product(xs[j], w1f_q, block(j), da_q, slice(0, H), E5, True, False)
+            product(xs[j], w2f_q, block(j), db_q, slice(0, H), E5, False, True)
         for j in range(L):
             scatter_scalar(j, 0, (first_low if j < 2 else first_high)[:, j % 2, :])
         de_second = [sb.tile([P, H], F32, name="de_second%d" % j) for j in range(L)]
         for copy, scatter, planes in ((nc.vector.tensor_copy, scatter_vector, (0, 1)), (nc.scalar.copy, scatter_scalar, (2, 3))):
             for j in planes:
-                copy(out=de_second[j][:], in_=xs[j][:, 0:H])
+                copy(out=de_second[j][:], in_=xs[j])
             for j in planes:
                 scatter(j, 1, de_second[j][:])
                 store(j)
 
-        split = T // 2
+        split = 17 * T // 32
         pieces = [(c * CW, (c + 1) * CW) for c in range(CH - 1)] + [(T - CW, T - CW // 2), (T - CW // 2, T)]
         words_out = out_1[0].rearrange("p c l -> p (c l)").bitcast(I32)
         ys = [sb.tile([P, CW * L], BF16, name="y%d" % c, tag="plane_then_y%d" % c, align_bytes=64) for c in range(CH)]

@@ -54,10 +54,10 @@ def tile_attend_ggate_E_pl_kernel(tc, eT, w1, w2, dy, c1, c2, ts, offs, out_0, o
 
         ts_row = sb.tile([P, T // P], F32, name="ts_row")
         nc.sync.dma_start(out=ts_row[:], in_=ts[0:1, :].rearrange("o (p m) -> (o p) m", p=P))
-        offsets = sb.tile([P, N // 16], U16, name="offsets")
-        nc.sync.dma_start(offsets[:], offs)
         w2_raw = sb.tile([P, L, K], F32, name="w2_raw")
         nc.sync.dma_start(out=w2_raw[:], in_=w2.rearrange("(p j) f -> p j f", j=L))
+        offsets = sb.tile([P, N // 16], U16, name="offsets")
+        nc.sync.dma_start(offsets[:], offs)
         dy_sb = sb.tile([P, L, N], F32, name="dy_sb", tag="dy_then_window", align_bytes=64)
         nc.sync.dma_start(out=dy_sb[:], in_=dy.rearrange("(p t) n -> p t n", t=L))
         c2_sb = sb.tile([P, L], F32, name="c2_sb")
@@ -163,15 +163,14 @@ def tile_attend_ggate_E_pl_kernel(tc, eT, w1, w2, dy, c1, c2, ts, offs, out_0, o
         sq = [sb.tile([P, H, L], F32, name="sq0")]
         ga = [sb.tile([P, H, L], F32, name="ga%d" % h) for h in range(2)]
 
-        def gate(h):
-            for v in range(2):
-                bk = bank(2 * h + v, "b%d_%d" % (h, v))
-                for t in range(2):
-                    product(bk[:, half(t)], w2d_q, block(2 * v + t), e_q[h], slice(0, H), E4, True, True)
-                for t in range(2):
-                    nc.vector.scalar_tensor_tensor(out=u[h][:, 2 * v + t, :], in0=bk[:, half(t)],
-                                                   scalar=c2_sb[:, 2 * v + t:2 * v + t + 1], in1=ts_slot[:, half(h)],
-                                                   op0=ALU.mult, op1=ALU.mult)
+        def gate(h, lanes_by_bank):
+            for bank_nr, lanes in lanes_by_bank:
+                bk = bank(bank_nr, "b%d_%d" % (h, lanes[0]))
+                for i, t in enumerate(lanes):
+                    product(bk[:, half(i)], w2d_q, block(t), e_q[h], slice(0, H), E4, True, True)
+                for i, t in enumerate(lanes):
+                    nc.vector.scalar_tensor_tensor(out=u[h][:, t, :], in0=bk[:, half(i)], scalar=c2_sb[:, t:t + 1],
+                                                   in1=ts_slot[:, half(h)], op0=ALU.mult, op1=ALU.mult)
 
         def sigmoid(h):
             nc.scalar.activation(out=s[h], in_=u[h][:], func=ACT.Sigmoid)
@@ -203,9 +202,9 @@ def tile_attend_ggate_E_pl_kernel(tc, eT, w1, w2, dy, c1, c2, ts, offs, out_0, o
         nc.gpsimd.tensor_scalar(out=w1_d[:].rearrange("p t m j -> p m t j")[:, P // 2:P],
                                 in0=w1_raw[:].rearrange("p j (m t) -> p m t j", t=L)[:, P // 2:P],
                                 scalar1=1.0, scalar2=0.0, op0=ALU.mult, op1=ALU.add)
-        gate(0)
+        gate(0, ((0, (0, 1)), (1, (2,)), (2, (3,))))
         sigmoid(0)
-        gate(1)
+        gate(1, ((3, (0, 1)), (5, (2, 3))))
         w1d_q = quantise(flat(w1_d), E4, "w1d", K)
         square(0)
         w1_f = sb.tile([P, L, P, L], BF16, name="w1_f", align_bytes=64)
@@ -225,16 +224,15 @@ def tile_attend_ggate_E_pl_kernel(tc, eT, w1, w2, dy, c1, c2, ts, offs, out_0, o
 
         out_rows = out_0.rearrange("(p j) c -> p j c", j=L)
 
-        def first_results(v, bank_nr):
-            bk = bank(bank_nr, "x_first%d" % v)
-            for i in range(2):
-                product(bk[:, half(i)], w1f_q, block(2 * v + i), da_q, slice(0, H), E5, True, False)
-                product(bk[:, half(i)], w2f_q, block(2 * v + i), db_q, slice(0, H), E5, False, True)
-            return bk
+        def results(j, out, da_codes, db_codes):
+            product(out, w1f_q, block(j), da_codes, slice(0, H), E5, True, False)
+            product(out, w2f_q, block(j), db_codes, slice(0, H), E5, False, True)
 
-        x_first = [first_results(0, 2)]
         first_low = sb.tile([P, 2, H], F32, name="first_low")
-        nc.scalar.copy(out=first_low[:], in_=x_first[0][:].rearrange("p (t n) -> p t n", t=2))
+        for j in range(2):
+            bk = bank(j, "x_first%d" % j)
+            results(j, bk[:, 0:H], da_q, db_q)
+            nc.scalar.copy(out=first_low[:, j, :], in_=bk[:, 0:H])
 
         def scatter_scalar(j, h, src):
             nc.scalar.activation(out=windows[j][:].indirect(offsets_of(h)), in_=src, func=ACT.Copy)
@@ -246,20 +244,21 @@ def tile_attend_ggate_E_pl_kernel(tc, eT, w1, w2, dy, c1, c2, ts, offs, out_0, o
             nc.sync.dma_start(out=out_rows[:, j, :], in_=windows[j][:])
 
         times_a(2, 4)
-        x_first.append(first_results(1, 4))
+        x_first_high = bank(4, "x_first_high")
+        for i in range(2):
+            results(2 + i, x_first_high[:, half(i)], da_q, db_q)
         times_a(3, 5)
         da_second = gradient_a(1)
         db_second = gradient_b(1)
         da_q = quantise(da_second, E5, "da1", H)
         db_q = quantise(db_second, E5, "db1", H)
         first_high = sb.tile([P, 2, H], F32, name="first_high")
-        nc.vector.tensor_copy(out=first_high[:], in_=x_first[1][:].rearrange("p (t n) -> p t n", t=2))
-        low = [bank(j, "x_second%d" % j) for j in range(2)]
+        nc.vector.tensor_copy(out=first_high[:], in_=x_first_high[:].rearrange("p (t n) -> p t n", t=2))
+        low = [bank(2 + j, "x_second%d" % j) for j in range(2)]
         high = bank(4, "x_second_high")
         xs = [low[0][:, 0:H], low[1][:, 0:H], high[:, half(0)], high[:, half(1)]]
         for j in range(L):
-            product(xs[j], w1f_q, block(j), da_q, slice(0, H), E5, True, False)
-            product(xs[j], w2f_q, block(j), db_q, slice(0, H), E5, False, True)
+            results(j, xs[j], da_q, db_q)
         for j in range(L):
             scatter_scalar(j, 0, (first_low if j < 2 else first_high)[:, j % 2, :])
         de_second = [sb.tile([P, H], F32, name="de_second%d" % j) for j in range(L)]
@@ -270,7 +269,7 @@ def tile_attend_ggate_E_pl_kernel(tc, eT, w1, w2, dy, c1, c2, ts, offs, out_0, o
                 scatter(j, 1, de_second[j][:])
                 store(j)
 
-        split = 17 * T // 32
+        split = T // 2
         pieces = [(c * CW, (c + 1) * CW) for c in range(CH - 1)] + [(T - CW, T - CW // 2), (T - CW // 2, T)]
         words_out = out_1[0].rearrange("p c l -> p (c l)").bitcast(I32)
         ys = [sb.tile([P, CW * L], BF16, name="y%d" % c, tag="plane_then_y%d" % c, align_bytes=64) for c in range(CH)]

from contextlib import ExitStack

import concourse.mybir as mybir
from concourse.masks import make_identity

F32 = mybir.dt.float32
BF16 = mybir.dt.bfloat16
I32 = mybir.dt.int32
U32 = mybir.dt.uint32
U16 = mybir.dt.uint16
U8 = mybir.dt.uint8
E4 = mybir.dt.float8_e4m3fn_x4
E5 = mybir.dt.float8_e5m2_x4
ALU = mybir.AluOpType
ACT = mybir.ActivationFunctionType

P = 128
L = 4
N = 512
H = N // 2
T = 2048
K = 512
CH = 4
CW = T // CH

FLOPS = 4 * 2 * 512 * 512 * 512


def tile_attend_ggate_E_pl_kernel(tc, eT, w1, w2, dy, c1, c2, ts, offs, out_0, out_1, out_2):
    nc = tc.nc
    with ExitStack() as ctx:
        sb = ctx.enter_context(tc.tile_pool(name="sb", bufs=1))
        after_ts = ctx.enter_context(tc.tile_pool(name="after_ts", bufs=1))
        ps = ctx.enter_context(tc.psum_pool(name="ps", bufs=1))

        def bank(i, name):
            return ps.tile([P, 512], F32, name=name, tag="bank%d" % i)

        def quantise(src, fmt, name, width):
            codes = sb.tile([P, width], U32, name=name + "_codes", align_bytes=64)
            scales = sb.tile([P, width], U8, name=name + "_scales", align_bytes=64)
            nc.vector.quantize_mx(out=codes[:].bitcast(fmt), scales=scales[:], in_=src)
            return codes, scales

        def product(out, stat, stat_cols, mov, mov_cols, mov_fmt, start, stop):
            nc.tensor.matmul_mx(out=out, lhsT=stat[0][:, stat_cols].bitcast(E4), lhsT_scale=stat[1][:, stat_cols],
                                rhs=mov[0][:, mov_cols].bitcast(mov_fmt), rhs_scale=mov[1][:, mov_cols], start=start, stop=stop)

        def block(i):
            return slice(i * P, (i + 1) * P)

        def half(h):
            return slice(h * H, (h + 1) * H)

        ts_row = sb.tile([P, T // P], F32, name="ts_row")
        nc.sync.dma_start(out=ts_row[:], in_=ts[0:1, :].rearrange("o (p m) -> (o p) m", p=P))
        w2_raw = sb.tile([P, L, K], F32, name="w2_raw")
        nc.sync.dma_start(out=w2_raw[:], in_=w2.rearrange("(p j) f -> p j f", j=L))
        offsets = sb.tile([P, N // 16], U16, name="offsets")
        nc.sync.dma_start(offsets[:], offs)
        dy_sb = sb.tile([P, L, N], F32, name="dy_sb", tag="dy_then_window", align_bytes=64)
        nc.sync.dma_start(out=dy_sb[:], in_=dy.rearrange("(p t) n -> p t n", t=L))
        c2_sb = sb.tile([P, L], F32, name="c2_sb")
        nc.scalar.dma_start(out=c2_sb[:], in_=c2.rearrange("(p t) o -> p (t o)", t=L))
        c1_sb = sb.tile([P, L], F32, name="c1_sb")
        nc.scalar.dma_start(out=c1_sb[:], in_=c1.rearrange("(p t) o -> p (t o)", t=L))
        e_rows = eT.rearrange("(p j) c -> p j c", j=L)
        e_planes = []
        for j in range(L):
            plane = sb.tile([P, T], F32, name="e_plane%d" % j, tag="plane_then_y%d" % j, align_bytes=64)
            nc.sync.dma_start(out=plane[:], in_=e_rows[:, j, :])
            e_planes.append(plane)
        w1_raw = sb.tile([P, L, K], F32, name="w1_raw", align_bytes=64)
        nc.sync.dma_start(out=w1_raw[:], in_=w1.rearrange("(p j) f -> p j f", j=L))

        def offsets_of(h):
            return offsets[:, h * H // 16:(h + 1) * H // 16]

        ident = sb.tile([P, P], F32, name="ident")
        make_identity(nc, ident[:])


        windows = {}

        def clear(j, tag, engine):
            windows[j] = sb.tile([P, T], F32, name="window%d" % j, tag=tag, align_bytes=64)
            engine.memset(windows[j][:].bitcast(I32), 0)

        clear(0, "window0", nc.vector)
        clear(1, "window1", nc.vector)

        warm = sb.tile([P, 1], F32, name="warm")
        nc.scalar.activation(out=warm[:], in_=ident[:, 0:1], func=ACT.Sigmoid)

        ts_all = after_ts.tile([P, T], F32, name="ts_all", offset=0, align_bytes=64)
        ts_view = ts_all[:].rearrange("q (p m) -> q p m", p=P)
        for g in range(4):
            bk = bank(g, "ts_bank%d" % g)
            for r in range(4):
                m = 4 * g + r
                nc.tensor.transpose(bk[:, r * P:(r + 1) * P], ts_row[:, m:m + 1].to_broadcast([P, P]), ident[:])
            nc.scalar.copy(out=ts_view[:, :, 4 * g:4 * g + 4], in_=bk[:].rearrange("q (r p) -> q p r", r=4))

        ts_slot = sb.tile([P, N], F32, name="ts_slot")
        nc.scalar.activation(out=ts_slot[:], in_=ts_all[:].indirect(offsets[:]), func=ACT.Copy)

        def flat(x):
            return x[:].rearrange("p a b c -> p (a b c)")

        def dealt(wd):
            return wd[:].rearrange("p t m j -> p m j t")

        def rows(raw):
            return raw[:].rearrange("p j (m t) -> p m j t", t=L)

        def along_f(wd, name, wf, first_bank):
            words = flat(wd).bitcast(F32).rearrange("p (t m v) -> p t m v", t=L, v=2)
            for v in range(2):
                bk = bank(first_bank + v, "%s_turn%d" % (name, v))
                for t in range(L):
                    nc.tensor.transpose(bk[:, block(t)], words[:, t, :, v], ident[:])
                nc.scalar.copy(out=wf[:, 2 * v:2 * v + 2, :, :],
                               in_=bk[:].bitcast(BF16).rearrange("m (t p e) -> m e p t", t=L, e=2))

        w2_d = sb.tile([P, L, P, L], BF16, name="w2_d", tag="w2_d", align_bytes=64)
        w2_f = after_ts.tile([P, L, P, L], BF16, name="w2_f", offset=0, align_bytes=64)
        nc.vector.tensor_copy(out=dealt(w2_d), in_=rows(w2_raw))
        w2d_q = quantise(flat(w2_d), E4, "w2d", K)
        along_f(w2_d, "w2", w2_f, 4)
        e_slot = sb.tile([P, N, L], BF16, name="e_slot", tag="e_slot", align_bytes=64)
        c2_neg = [e_slot[:, v * H, :].bitcast(F32) for v in range(2)]
        for v in range(2):
            nc.vector.tensor_scalar(out=c2_neg[v], in0=c2_sb[:, 2 * v:2 * v + 2], scalar1=-1.0, scalar2=None, op0=ALU.mult)
        for_da = sb.tile([P, L, N], F32, name="for_da")
        for_db = sb.tile([P, L, N], F32, name="for_db")
        for t in range(L):
            nc.vector.scalar_tensor_tensor(out=for_da[:, t, :], in0=dy_sb[:, t, :], scalar=c1_sb[:, t:t + 1],
                                           in1=ts_slot[:], op0=ALU.mult, op1=ALU.mult)
        for t in range(L):
            nc.vector.scalar_tensor_tensor(out=for_db[:, t, :], in0=for_da[:, t, :], scalar=c2_neg[t // 2][:, t % 2:t % 2 + 1],
                                           in1=ts_slot[:], op0=ALU.mult, op1=ALU.mult)
        clear(2, "w2_d", nc.gpsimd)
        clear(3, "dy_then_window", nc.gpsimd)
        w2f_q = quantise(flat(w2_f), E4, "w2f", K)

        e_low = after_ts.tile([P, 2, N], BF16, name="e_low", offset=4096, align_bytes=64)
        for j in range(2):
            nc.scalar.activation(out=e_low[:, j, :], in_=e_planes[j][:].indirect(offsets[:]), func=ACT.Copy)
        nc.scalar.copy(out=e_slot[:, :, 0:2], in_=e_low[:].rearrange("p j n -> p n j"))
        nc.vector.tensor_copy(out=e_slot[:, :, 2], in_=e_planes[2][:].indirect(offsets[:]))
        for h in range(2):
            nc.vector.tensor_copy(out=e_slot[:, half(h), 3], in_=e_planes[3][:].indirect(offsets_of(h)))
        e_q = [quantise(e_slot[:, half(h), :].rearrange("p n j -> p (n j)"), E4, "e%d" % h, H) for h in range(2)]

        def woven(x):
            return x.rearrange("p (c i) t -> p c t i", i=2)

        def planar(x):
            return x.rearrange("p t (c i) -> p c t i", i=2)

        u = [sb.tile([P, L, H], F32, name="u%d" % h) for h in range(2)]
        s = [w1_raw[:, :, 0:H]]
        sq = [sb.tile([P, H, L], F32, name="sq0")]
        ga = [sb.tile([P, H, L], F32, name="ga%d" % h) for h in range(2)]

        def gate(h, lanes_by_bank):
            for bank_nr, lanes in lanes_by_bank:
                bk = bank(bank_nr, "b%d_%d" % (h, lanes[0]))
                for i, t in enumerate(lanes):
                    product(bk[:, half(i)], w2d_q, block(t), e_q[h], slice(0, H), E4, True, True)
                for i, t in enumerate(lanes):
                    nc.vector.scalar_tensor_tensor(out=u[h][:, t, :], in0=bk[:, half(i)], scalar=c2_sb[:, t:t + 1],
                                                   in1=ts_slot[:, half(h)], op0=ALU.mult, op1=ALU.mult)

        def sigmoid(h):
            nc.scalar.activation(out=s[h], in_=u[h][:], func=ACT.Sigmoid)

        def square(h):
            nc.scalar.activation(out=woven(sq[h][:]), in_=planar(s[h]), func=ACT.Square, bias=-0.5)

        def times_a(i, bank_nr):
            bk = bank(bank_nr, "a%d" % i)
            for t in range(L):
                product(bk[:, block(t)], w1d_q, block(t), e_q[i // 2], block(i % 2), E4, True, True)
            nc.vector.tensor_tensor(out=woven(ga[i // 2][:, block(i % 2), :]),
                                    in0=planar(bk[:].rearrange("p (t n) -> p t n", t=L)),
                                    in1=planar(for_db[:, :, block(i)]), op=ALU.mult)

        def gradient_a(h):
            da_w = sb.tile([P, H, L], BF16, name="da_w%d" % h, tag="da_w%d" % h, align_bytes=64)
            nc.vector.tensor_tensor(out=woven(da_w[:]), in0=planar(for_da[:, :, half(h)]), in1=planar(s[h]), op=ALU.mult)
            return da_w[:].rearrange("p n t -> p (n t)")

        def gradient_b(h):
            db_w = sb.tile([P, H, L], BF16, name="db_w%d" % h, align_bytes=64)
            nc.vector.scalar_tensor_tensor(out=db_w[:], in0=sq[h][:], scalar=0.25, in1=ga[h][:],
                                           op0=ALU.subtract, op1=ALU.mult)
            return db_w[:].rearrange("p n t -> p (n t)")

        w1_d = sb.tile([P, L, P, L], BF16, name="w1_d", tag="e_slot", align_bytes=64)
        nc.scalar.copy(out=dealt(w1_d)[:, 0:P // 2], in_=rows(w1_raw)[:, 0:P // 2])
        nc.gpsimd.tensor_scalar(out=w1_d[:].rearrange("p t m j -> p m t j")[:, P // 2:P],
                                in0=w1_raw[:].rearrange("p j (m t) -> p m t j", t=L)[:, P // 2:P],
                                scalar1=1.0, scalar2=0.0, op0=ALU.mult, op1=ALU.add)
        gate(0, ((0, (0, 1)), (1, (2,)), (2, (3,))))
        sigmoid(0)
        gate(1, ((3, (0, 1)), (5, (2, 3))))
        w1d_q = quantise(flat(w1_d), E4, "w1d", K)
        square(0)
        w1_f = sb.tile([P, L, P, L], BF16, name="w1_f", align_bytes=64)
        along_f(w1_d, "w1", w1_f, 6)
        da_first = gradient_a(0)
        times_a(0, 4)
        times_a(1, 5)
        da_q = quantise(da_first, E5, "da0", H)
        db_first = gradient_b(0)
        w1f_q = quantise(flat(w1_f), E4, "w1f", K)
        db_q = quantise(db_first, E5, "db0", H)
        s_second = sb.tile([P, L, H], F32, name="s_second", tag="e_slot", align_bytes=64)
        s.append(s_second[:])
        sigmoid(1)
        sq.append(sb.tile([P, H, L], F32, name="sq1"))
        square(1)

        out_rows = out_0.rearrange("(p j) c -> p j c", j=L)

        def results(j, out, da_codes, db_codes):
            product(out, w1f_q, block(j), da_codes, slice(0, H), E5, True, False)
            product(out, w2f_q, block(j), db_codes, slice(0, H), E5, False, True)

        first_low = sb.tile([P, 2, H], F32, name="first_low")
        for j in range(2):
            bk = bank(j, "x_first%d" % j)
            results(j, bk[:, 0:H], da_q, db_q)
            nc.scalar.copy(out=first_low[:, j, :], in_=bk[:, 0:H])

        def scatter_scalar(j, h, src):
            nc.scalar.activation(out=windows[j][:].indirect(offsets_of(h)), in_=src, func=ACT.Copy)

        def scatter_vector(j, h, src):
            nc.vector.tensor_copy(out=windows[j][:].indirect(offsets_of(h)), in_=src)

        def store(j):
            nc.sync.dma_start(out=out_rows[:, j, :], in_=windows[j][:])

        times_a(2, 4)
        x_first_high = bank(4, "x_first_high")
        for i in range(2):
            results(2 + i, x_first_high[:, half(i)], da_q, db_q)
        times_a(3, 5)
        da_second = gradient_a(1)
        db_second = gradient_b(1)
        da_q = quantise(da_second, E5, "da1", H)
        db_q = quantise(db_second, E5, "db1", H)
        first_high = sb.tile([P, 2, H], F32, name="first_high")
        nc.vector.tensor_copy(out=first_high[:], in_=x_first_high[:].rearrange("p (t n) -> p t n", t=2))
        low = [bank(2 + j, "x_second%d" % j) for j in range(2)]
        high = bank(4, "x_second_high")
        xs = [low[0][:, 0:H], low[1][:, 0:H], high[:, half(0)], high[:, half(1)]]
        for j in range(L):
            results(j, xs[j], da_q, db_q)
        for j in range(L):
            scatter_scalar(j, 0, (first_low if j < 2 else first_high)[:, j % 2, :])
        de_second = [sb.tile([P, H], F32, name="de_second%d" % j) for j in range(L)]
        for copy, scatter, planes in ((nc.vector.tensor_copy, scatter_vector, (0, 1)), (nc.scalar.copy, scatter_scalar, (2, 3))):
            for j in planes:
                copy(out=de_second[j][:], in_=xs[j])
            for j in planes:
                scatter(j, 1, de_second[j][:])
                store(j)

        split = T // 2
        pieces = [(c * CW, (c + 1) * CW) for c in range(CH - 1)] + [(T - CW, T - CW // 2), (T - CW // 2, T)]
        words_out = out_1[0].rearrange("p c l -> p (c l)").bitcast(I32)
        ys = [sb.tile([P, CW * L], BF16, name="y%d" % c, tag="plane_then_y%d" % c, align_bytes=64) for c in range(CH)]
        shares = ((nc.scalar.copy, U32, split, T), (nc.vector.tensor_copy, I32, 0, split))
        pairs = [sb.tile([P, L * (last - first)], BF16, name="pairs%d" % first, align_bytes=64) for copy, dtype, first, last in shares]
        lanes = [x[:].rearrange("p (u n e) -> p u n e", u=2, e=2) for x in pairs]
        for j in range(2):
            for share, (copy, dtype, first, last) in zip(lanes, shares):
                nc.vector.tensor_copy(out=share[:, 0, :, j], in_=windows[j][:, first:last])
        for pair, share, (copy, dtype, first, last) in zip(pairs, lanes, shares):
            for j in range(2):
                copy(out=share[:, 1, :, j], in_=windows[2 + j][:, first:last])
            pair_words = pair[:].bitcast(dtype).rearrange("p (u n) -> p n u", u=2)
            for lo, hi in pieces:
                lo, hi, c = max(first, lo), min(last, hi), lo // CW
                if lo < hi:
                    y_words = ys[c][:].bitcast(dtype).rearrange("p (n u) -> p n u", u=2)
                    copy(out=y_words[:, lo - c * CW:hi - c * CW, :], in_=pair_words[:, lo - first:hi - first, :])

        y_scales = sb.tile([P, CW], U8, name="y_scales", align_bytes=64)
        for lo, hi in pieces:
            c = lo // CW
            codes = sb.tile([P, hi - lo], U32, name="y_codes%d" % lo, align_bytes=64)
            nc.vector.quantize_mx(out=codes[:].bitcast(E4), scales=y_scales[4 * c:P, lo - c * CW:hi - c * CW],
                                  in_=ys[c][:, L * (lo - c * CW):L * (hi - c * CW)])
            nc.sync.dma_start(out=words_out[:, lo:hi], in_=codes[:].bitcast(I32))
        for q in range(4):
            nc.sync.dma_start(out=out_2[0, 4 * q:4 * q + 4, :].bitcast(I32).rearrange("r (c x) -> c r x", c=CH),
                              in_=y_scales[32 * q:32 * q + 16, :].bitcast(I32))
